import numpy as np
import ml_dtypes


def mxq(x, axis, fmt="e4m3"):
    dtype, down = {"e4m3": (ml_dtypes.float8_e4m3fn, 7), "e5m2": (ml_dtypes.float8_e5m2, 14)}[fmt]
    v = np.moveaxis(np.asarray(x, np.float32).astype(ml_dtypes.bfloat16).astype(np.float64), axis, -1)
    blocks = v.reshape(v.shape[:-1] + (-1, 32))
    amax = np.abs(blocks).max(-1, keepdims=True)
    byte = np.maximum(np.where(amax > 0, np.frexp(amax)[1] - 1 + 127, 0) - down, 1)
    scale = np.exp2(byte - 127.0)
    codes = (blocks / scale).astype(np.float32).astype(dtype).astype(np.float64)
    return np.moveaxis((codes * scale).reshape(v.shape), -1, axis)


WIDE = False


def mx_kscale(k):
    if not WIDE:
        return np.ones(k)
    levels = np.array([10, -10, 5, -5, 0])
    if k % 512:
        return np.exp2(np.random.permutation(np.resize(levels, k // 32))).repeat(32)
    a = np.empty((k // 512, 16))
    for p in range(k // 512):
        a[p, :8] = np.random.permutation(np.resize(levels, 8))
        for g in range(8):
            far = levels[np.abs(levels - a[p, g]) >= 10]
            a[p, g + 8] = far[np.random.randint(len(far))]
    return np.exp2(a.ravel()).repeat(32)


def f64(x):
    return np.asarray(x).astype(np.float64)


def striped(idx):
    return np.tile(idx.reshape(-1, 16).T, (8, 1)).astype(np.uint16)


def unstriped(offs):
    return offs[:16].T.reshape(-1).astype(np.int64)


def striped8(idx):
    return np.concatenate([x.reshape(-1, 16).T for x in idx]).astype(np.uint16)


def runs(offs, k):
    lists = np.stack([offs[16 * r : 16 * r + 16].T.reshape(-1) for r in range(8)]).astype(np.int64)
    return lists[np.arange(k) % 512 // 64]


def pack_weight(w):
    k, n = w.shape
    w = f64(np.asarray(w, np.float32).astype(ml_dtypes.bfloat16)).reshape(k // 32, 32, n)
    amax = np.abs(w).max(1)
    byte = np.clip(np.where(amax > 0, np.frexp(amax)[1] - 1 + 127 - 7, 1), 1, 254)
    scaled = (w * np.exp2(127.0 - byte)[:, None, :]).reshape(k, n).astype(np.float32)
    words = np.ascontiguousarray(scaled.reshape(k // 512, 128, 4, n).transpose(0, 1, 3, 2)).astype(ml_dtypes.float8_e4m3fn).view(np.uint8)
    return words, np.ascontiguousarray(byte.astype(np.uint8).reshape(k // 512, 16, n))


def unpack_weight(words, scales):
    g, p, n, _ = words.shape
    vals = np.ascontiguousarray(words).view(ml_dtypes.float8_e4m3fn).astype(np.float64) * np.repeat(np.exp2(scales.astype(np.float64) - 127.0), 8, axis=1)[..., None]
    return vals.transpose(0, 1, 3, 2).reshape(g * 512, n)


E2M1 = np.array([0.0, 0.5, 1.0, 1.5, 2.0, 3.0, 4.0, 6.0, -0.0, -0.5, -1.0, -1.5, -2.0, -3.0, -4.0, -6.0])


def pack_fp4(w):
    k, n = w.shape
    w = f64(np.asarray(w, np.float32).astype(ml_dtypes.bfloat16)).reshape(k // 32, 32, n)
    amax = np.abs(w).max(1)
    mant, ex = np.frexp(amax / 6.0)
    byte = np.clip(np.where(amax > 0, np.where(mant > 0.5, ex, ex - 1) + 127, 1), 1, 254)
    scaled = (w * np.exp2(127.0 - byte)[:, None, :]).reshape(k, n).astype(np.float32)
    c = np.ascontiguousarray(scaled.reshape(k // 512, 128, 4, n).transpose(0, 1, 3, 2)).astype(ml_dtypes.float4_e2m1fn).view(np.uint8) & 0xF
    words = (c[..., 0::2] | (c[..., 1::2] << 4)).reshape(k // 512, 128, 2 * n)
    return np.ascontiguousarray(words), np.ascontiguousarray(byte.astype(np.uint8).reshape(k // 512, 16, n))


def unpack_fp4(words, scales):
    g, _, n = scales.shape
    words = np.ascontiguousarray(words).reshape(g, 128, n, 2)
    nib = np.empty((g, 128, n, 4), np.uint8)
    nib[..., 0::2] = words & 0xF
    nib[..., 1::2] = words >> 4
    vals = E2M1[nib] * np.repeat(np.exp2(scales.astype(np.float64) - 127.0), 8, axis=1)[..., None]
    return vals.transpose(0, 1, 3, 2).reshape(g * 512, n)


def silu(v):
    return v / (1.0 + np.exp(-np.maximum(v, -700.0)))

def planes(y):
    n, m = y.shape
    v = y.astype(np.float32).astype(ml_dtypes.bfloat16).astype(np.float64).reshape(n // 32, 32, m)
    top = np.abs(v).max(1)
    byte = np.clip(np.where(top > 0, np.frexp(top)[1] - 1 + 127 - 7, 1), 1, 254)
    codes = (v * np.exp2(127.0 - byte)[:, None, :]).reshape(n, m).astype(np.float32).astype(ml_dtypes.float8_e4m3fn).view(np.uint8)
    words = codes.reshape(n // 512, 128, 4, m).transpose(0, 1, 3, 2)
    return np.ascontiguousarray(words), np.ascontiguousarray(byte.astype(np.uint8).reshape(n // 512, 16, m))


K, T, S, V, N, H = 512, 2048, 1024, 512, 512, 512


def setup_inputs():
    n = np.random.standard_normal
    s = mx_kscale(K)[:, None]
    u = mx_kscale(H)
    packed_xT = pack_weight(n((K, T)) * s)
    packed_w2 = pack_fp4(n((H, N)) / np.sqrt(H) / u[:, None])
    return {
        "x_words": packed_xT[0],
        "x_scales": packed_xT[1],
        "w1": (n((K, H)) / np.sqrt(K) / s * u).astype(np.float32),
        "w2_words": packed_w2[0],
        "w2_scales": packed_w2[1],
        "offs": striped(np.random.permutation(T)[:S]),
        "order": striped8(np.stack([np.random.permutation(S) for _ in range(8)])),
        "bucket": striped8(np.random.randint(0, V, (8, S))),
    }


def reference(x_words, x_scales, w1, w2_words, w2_scales, offs, order, bucket):
    xq = unpack_weight(x_words, x_scales)[:, unstriped(offs)]
    y = mxq(f64(w1), 0, "e4m3").T @ xq
    s = y[np.arange(H)[:, None], runs(order, H)]
    p = s.reshape(H, V, 2).mean(axis=2)
    z = silu(y - (p[np.arange(H)[:, None], runs(bucket, H)]))
    out_0 = unpack_fp4(w2_words, w2_scales).T @ mxq(z, 0, "e4m3")
    return (out_0,) + planes(out_0)

@@ -1,0 +1,184 @@
+from contextlib import ExitStack
+
+import concourse.mybir as mybir
+
+F32 = mybir.dt.float32
+BF16 = mybir.dt.bfloat16
+I32 = mybir.dt.int32
+U32 = mybir.dt.uint32
+U16 = mybir.dt.uint16
+U8 = mybir.dt.uint8
+FP8X4 = mybir.dt.float8_e4m3fn_x4
+FP4X4 = mybir.dt.float4_e2m1fn_x4
+ALU = mybir.AluOpType
+ACT = mybir.ActivationFunctionType
+
+K, T, S, V, N, H = 512, 2048, 1024, 512, 512, 512
+FLOPS = 2 * K * H * S + 2 * H * N * S
+P = 128
+PACK = 4
+BANK = 512
+BLOCK = 128
+PIECES = (512, 256, 256)
+CHUNKS = (128,256,256,256,128)
+VECTOR_CASTS = (2, 5, 7)
+
+
+def tile_picked_lshmean_silu_po_kernel(
+    tc, x_words, x_scales, w1, w2_words, w2_scales, offs, order, bucket, out_0, out_1, out_2
+):
+    nc = tc.nc
+    with ExitStack() as ctx:
+        lists = ctx.enter_context(tc.tile_pool(name="lists", bufs=1))
+        keep = ctx.enter_context(tc.tile_pool(name="keep", bufs=1))
+        psum_y = ctx.enter_context(tc.psum_pool(name="psum_y", bufs=4))
+        psum_o = ctx.enter_context(tc.psum_pool(name="psum_o", bufs=4))
+
+        offs_t = lists.tile([P, S // 16], U16, name="offs_t")
+        order_t = lists.tile([P, S // 16], U16, name="order_t")
+        bucket_t = lists.tile([P, S // 16], U16, name="bucket_t")
+
+        xs_all = keep.tile([P, T], U8, name="xs_all", align_bytes=64)
+        xw_all = keep.tile([P, T], I32, name="xw_all", align_bytes=64)
+        w2s_raw = keep.tile([P, N], U8, name="w2s_raw", align_bytes=64)
+        w2w_raw = keep.tile([P, 2 * N], U8, name="w2w_raw", align_bytes=64)
+        w1_raw = [keep.tile([P, PACK, H // 2], F32, name=f"w1_raw{h}", align_bytes=64) for h in range(2)]
+        warm = keep.tile([P, 1], F32, name="warm")
+        warm_out = keep.tile([P, 1], F32, name="warm_out")
+
+        nc.vector.memset(xs_all[:].bitcast(I32), 0)
+        nc.vector.memset(w2s_raw[:].bitcast(I32), 0)
+        nc.vector.memset(warm[:], 0.0)
+        nc.scalar.activation(warm_out[:], warm[:], ACT.Silu)
+
+        nc.sync.dma_start(offs_t[:], offs)
+        nc.sync.dma_start(order_t[:], order)
+        nc.sync.dma_start(bucket_t[:], bucket)
+        for q in range(4):
+            nc.sync.dma_start(xs_all[32 * q : 32 * q + 4, :].bitcast(I32), x_scales[0, 4 * q : 4 * q + 4, :].bitcast(I32))
+        w1_rows = w1.rearrange("(p j) c -> p j c", j=PACK)
+        for h in range(2):
+            nc.sync.dma_start(w1_raw[h][:], w1_rows[:, :, h * (H // 2) : (h + 1) * (H // 2)])
+        nc.sync.dma_start(xw_all[:], x_words[0].rearrange("p c r -> p (c r)").bitcast(I32))
+        nc.sync.dma_start(w2w_raw[:].bitcast(I32), w2_words[0].bitcast(I32))
+        for q in range(4):
+            nc.sync.dma_start(w2s_raw[32 * q : 32 * q + 4, :].bitcast(I32), w2_scales[0, 4 * q : 4 * q + 4, :].bitcast(I32))
+
+        xs = keep.tile([P, S], U8, name="xs", align_bytes=64)
+        pieces = [(sum(PIECES[:i]), n) for i, n in enumerate(PIECES)]
+        xw = [keep.tile([P, n], U32, name=f"xw{i}", align_bytes=64) for i, n in enumerate(PIECES)]
+        nc.vector.tensor_copy(xs[:], xs_all[:].indirect(offs_t[:]))
+
+        w1_bf = keep.tile([P, PACK * H], BF16, name="w1_bf", align_bytes=64)
+        w1_dealt = w1_bf[:].rearrange("p (t m j) -> p m j t", t=PACK, j=PACK)
+        half = P // 2
+        for h in range(2):
+            nc.scalar.copy(w1_dealt[:, h * half : (h + 1) * half], w1_raw[h][:].rearrange("p j (m t) -> p m j t", t=PACK))
+        w1_codes = [keep.tile([P, P], U32, name=f"w1_codes{t}", align_bytes=64) for t in range(PACK)]
+        w1_scales = [keep.tile([P, P], U8, name=f"w1_scales{t}", align_bytes=64) for t in range(PACK)]
+        for t in range(PACK):
+            nc.vector.quantize_mx(w1_codes[t][:].bitcast(FP8X4), w1_scales[t][:], w1_bf[:, t * H : (t + 1) * H])
+        for i, (j0, n) in enumerate(pieces):
+            nc.vector.tensor_copy(xw[i][:], xw_all[:].bitcast(U32).indirect(offs_t[:, j0 // 16 : (j0 + n) // 16]))
+
+        w2w = keep.tile([P, 2 * N], U8, name="w2w", align_bytes=64)
+        w2s = keep.tile([P, N], U8, name="w2s", align_bytes=64)
+        nc.vector.tensor_copy(
+            w2w[:].rearrange("p (t m b) -> p m t b", t=PACK, b=2), w2w_raw[:].rearrange("p (m t b) -> p m t b", t=PACK, b=2)
+        )
+        nc.vector.tensor_copy(w2s[:].rearrange("p (t m) -> p m t", t=PACK), w2s_raw[:].rearrange("p (m t) -> p m t", t=PACK))
+
+        y = [keep.tile([P, S], F32, name=f"y{t}", align_bytes=64) for t in range(PACK)]
+        for t in range(PACK):
+            for i, (j0, n) in enumerate(pieces):
+                cols = slice(j0, j0 + n)
+                acc = psum_y.tile([P, BANK], F32, name="acc")
+                nc.tensor.matmul_mx(
+                    acc[:, 0:n], lhsT=w1_codes[t][:].bitcast(FP8X4), lhsT_scale=w1_scales[t][:],
+                    rhs=xw[i][:].bitcast(FP8X4), rhs_scale=xs[:, cols], start=True, stop=True,
+                )
+                nc.scalar.copy(y[t][:, cols], acc[:, 0:n])
+
+        s = [keep.tile([P, S], F32, name=f"s{t}", align_bytes=64) for t in range(PACK)]
+        p = [keep.tile([P, V], F32, name=f"p{t}", align_bytes=64) for t in range(PACK)]
+
+        def line_up(t, h):
+            nc.vector.tensor_scalar(
+                s[t][:, h * V : (h + 1) * V], y[t][:].indirect(order_t[:, h * 32 : (h + 1) * 32]), 0.5, 0.0, ALU.mult, ALU.add
+            )
+
+        def pair_sums(t):
+            pairs = s[t][:].rearrange("p (v e) -> p v e", e=2)
+            nc.vector.tensor_tensor(p[t][:], pairs[:, :, 0], pairs[:, :, 1], ALU.add)
+
+        for t in range(PACK):
+            line_up(t, 0)
+            if t > 0:
+                pair_sums(t - 1)
+            line_up(t, 1)
+
+        out_rows = out_0.rearrange("(p t) j -> p t j", t=PACK)
+        out_words = out_1[0].rearrange("p c r -> p (c r)").bitcast(I32)
+        o_scales = keep.tile([P, S], U8, name="o_scales", align_bytes=64)
+        starts = [sum(CHUNKS[:c]) for c in range(len(CHUNKS))]
+        u = [keep.tile([P, PACK, n], F32, name=f"u{c}", align_bytes=64) for c, n in enumerate(CHUNKS)]
+        z_bf = [keep.tile([P, PACK * n], BF16, name=f"z_bf{c}", align_bytes=64) for c, n in enumerate(CHUNKS)]
+        z_codes = [keep.tile([P, n], U32, name=f"z_codes{c}", align_bytes=64) for c, n in enumerate(CHUNKS)]
+        z_scales = [keep.tile([P, n], U8, name=f"z_scales{c}", align_bytes=64) for c, n in enumerate(CHUNKS)]
+        o_f32 = [keep.tile([P, PACK, n], F32, name=f"o_f32{c}", align_bytes=64) for c, n in enumerate(CHUNKS)]
+        o_bf = [keep.tile([P, PACK * n], BF16, name=f"o_bf{c}", align_bytes=64) for c, n in enumerate(CHUNKS)]
+        o_codes = [keep.tile([P, n], I32, name=f"o_codes{c}", align_bytes=64) for c, n in enumerate(CHUNKS)]
+
+        def differences(c):
+            j0, n = starts[c], CHUNKS[c]
+            for t in range(PACK):
+                nc.vector.tensor_tensor(
+                    u[c][:, t, :], p[t][:].indirect(bucket_t[:, j0 // 16 : (j0 + n) // 16]), y[t][:, j0 : j0 + n], ALU.subtract
+                )
+                if c == 0 and t == 0:
+                    pair_sums(PACK - 1)
+            nc.scalar.activation(
+                z_bf[c][:].rearrange("p (g i t) -> p g t i", i=4, t=PACK),
+                u[c][:].rearrange("p t (g i) -> p g t i", i=4),
+                ACT.Silu,
+                scale=-1.0,
+            )
+
+        def second_product(c):
+            j0, n = starts[c], CHUNKS[c]
+            nc.vector.quantize_mx(z_codes[c][:].bitcast(FP8X4), z_scales[c][:], z_bf[c][:])
+            for b in range(n // BLOCK):
+                cols = slice(b * BLOCK, (b + 1) * BLOCK)
+                res = psum_o.tile([P, PACK, BLOCK], F32, name="res")
+                for t in range(PACK):
+                    nc.tensor.matmul_mx(
+                        res[:, t, :], lhsT=w2w[:, 2 * P * t : 2 * P * (t + 1)].bitcast(FP4X4), lhsT_scale=w2s[:, P * t : P * (t + 1)],
+                        rhs=z_codes[c][:, cols].bitcast(FP8X4), rhs_scale=z_scales[c][:, cols], start=True, stop=True,
+                    )
+                nc.scalar.copy(o_f32[c][:, :, cols], res[:])
+                bf_cols = o_bf[c][:, PACK * BLOCK * b : PACK * BLOCK * (b + 1)]
+                if j0 // BLOCK + b in VECTOR_CASTS:
+                    nc.vector.tensor_copy(
+                        bf_cols.rearrange("p (g i t) -> p g t i", i=4, t=PACK),
+                        o_f32[c][:, :, cols].rearrange("p t (g i) -> p g t i", i=4),
+                    )
+                else:
+                    nc.scalar.copy(bf_cols.rearrange("p (j t) -> p j t", t=PACK), res[:].rearrange("p t j -> p j t"))
+            nc.sync.dma_start(out_rows[:, :, j0 : j0 + n], o_f32[c][:])
+
+        def hand_on(c):
+            j0, n = starts[c], CHUNKS[c]
+            nc.vector.quantize_mx(o_codes[c][:].bitcast(FP8X4), o_scales[:, j0 : j0 + n], o_bf[c][:])
+            nc.sync.dma_start(out_words[:, j0 : j0 + n], o_codes[c][:])
+
+        last = len(CHUNKS) - 1
+        for step in range(last + 3):
+            if step <= last:
+                differences(step)
+            if 1 <= step <= last + 1:
+                second_product(step - 1)
+            if step >= 2:
+                hand_on(step - 2)
+        for q in range(4):
+            queue = nc.sync if q % 2 == 0 else nc.scalar
+            queue.dma_start(out_2[0, 4 * q : 4 * q + 4, :].bitcast(I32), o_scales[32 * q : 32 * q + 4, :].bitcast(I32))

@@ -1,6 +1,7 @@
 from contextlib import ExitStack
 
 import concourse.mybir as mybir
+from concourse.masks import make_identity
 
 F32 = mybir.dt.float32
 BF16 = mybir.dt.bfloat16
@@ -19,9 +20,11 @@ P = 128
 PACK = 4
 BANK = 512
 BLOCK = 128
-PIECES = (512, 256, 256)
+PIECES = (512, 512)
+W1_SCALAR = 64
+TENSOR_SUMS = 5
 CHUNKS = (128,256,256,256,128)
-VECTOR_CASTS = (2, 5, 7)
+VECTOR_CASTS = (2, 4, 5, 6)
 
 
 def tile_picked_lshmean_silu_po_kernel(
@@ -31,8 +34,9 @@ def tile_picked_lshmean_silu_po_kernel(
     with ExitStack() as ctx:
         lists = ctx.enter_context(tc.tile_pool(name="lists", bufs=1))
         keep = ctx.enter_context(tc.tile_pool(name="keep", bufs=1))
-        psum_y = ctx.enter_context(tc.psum_pool(name="psum_y", bufs=4))
-        psum_o = ctx.enter_context(tc.psum_pool(name="psum_o", bufs=4))
+        ring = ctx.enter_context(tc.tile_pool(name="ring", bufs=2))
+        psum = ctx.enter_context(tc.psum_pool(name="psum", bufs=6))
+        psum_turn = ctx.enter_context(tc.psum_pool(name="psum_turn", bufs=2))
 
         offs_t = lists.tile([P, S // 16], U16, name="offs_t")
         order_t = lists.tile([P, S // 16], U16, name="order_t")
@@ -42,7 +46,7 @@ def tile_picked_lshmean_silu_po_kernel(
         xw_all = keep.tile([P, T], I32, name="xw_all", align_bytes=64)
         w2s_raw = keep.tile([P, N], U8, name="w2s_raw", align_bytes=64)
         w2w_raw = keep.tile([P, 2 * N], U8, name="w2w_raw", align_bytes=64)
-        w1_raw = [keep.tile([P, PACK, H // 2], F32, name=f"w1_raw{h}", align_bytes=64) for h in range(2)]
+        w1_raw = [keep.tile([P, PACK, H // 2], F32, name=f"w1_raw{h}", tag=f"w1_raw{h}", align_bytes=64) for h in range(2)]
         warm = keep.tile([P, 1], F32, name="warm")
         warm_out = keep.tile([P, 1], F32, name="warm_out")
 
@@ -51,15 +55,15 @@ def tile_picked_lshmean_silu_po_kernel(
         nc.vector.memset(warm[:], 0.0)
         nc.scalar.activation(warm_out[:], warm[:], ACT.Silu)
 
+        w1_rows = w1.rearrange("(p j) c -> p j c", j=PACK)
         nc.sync.dma_start(offs_t[:], offs)
+        nc.sync.dma_start(w1_raw[0][:], w1_rows[:, :, 0 : H // 2])
         nc.sync.dma_start(order_t[:], order)
-        nc.sync.dma_start(bucket_t[:], bucket)
         for q in range(4):
             nc.sync.dma_start(xs_all[32 * q : 32 * q + 4, :].bitcast(I32), x_scales[0, 4 * q : 4 * q + 4, :].bitcast(I32))
-        w1_rows = w1.rearrange("(p j) c -> p j c", j=PACK)
-        for h in range(2):
-            nc.sync.dma_start(w1_raw[h][:], w1_rows[:, :, h * (H // 2) : (h + 1) * (H // 2)])
         nc.sync.dma_start(xw_all[:], x_words[0].rearrange("p c r -> p (c r)").bitcast(I32))
+        nc.sync.dma_start(w1_raw[1][:], w1_rows[:, :, H // 2 : H])
+        nc.sync.dma_start(bucket_t[:], bucket)
         nc.sync.dma_start(w2w_raw[:].bitcast(I32), w2_words[0].bitcast(I32))
         for q in range(4):
             nc.sync.dma_start(w2s_raw[32 * q : 32 * q + 4, :].bitcast(I32), w2_scales[0, 4 * q : 4 * q + 4, :].bitcast(I32))
@@ -69,20 +73,21 @@ def tile_picked_lshmean_silu_po_kernel(
         xw = [keep.tile([P, n], U32, name=f"xw{i}", align_bytes=64) for i, n in enumerate(PIECES)]
         nc.vector.tensor_copy(xs[:], xs_all[:].indirect(offs_t[:]))
 
-        w1_bf = keep.tile([P, PACK * H], BF16, name="w1_bf", align_bytes=64)
+        w1_bf = keep.tile([P, PACK * H], BF16, name="w1_bf", tag="w1_bf", align_bytes=64)
         w1_dealt = w1_bf[:].rearrange("p (t m j) -> p m j t", t=PACK, j=PACK)
         half = P // 2
-        for h in range(2):
-            nc.scalar.copy(w1_dealt[:, h * half : (h + 1) * half], w1_raw[h][:].rearrange("p j (m t) -> p m j t", t=PACK))
+        for i, (j0, n) in enumerate(pieces):
+            nc.vector.tensor_copy(xw[i][:], xw_all[:].bitcast(U32).indirect(offs_t[:, j0 // 16 : (j0 + n) // 16]))
+        w1_src = [w1_raw[h][:].rearrange("p j (m t) -> p m j t", t=PACK) for h in range(2)]
+        nc.scalar.copy(w1_dealt[:, 0:half], w1_src[0])
+        nc.scalar.copy(w1_dealt[:, half : half + W1_SCALAR], w1_src[1][:, 0:W1_SCALAR])
         w1_codes = [keep.tile([P, P], U32, name=f"w1_codes{t}", align_bytes=64) for t in range(PACK)]
         w1_scales = [keep.tile([P, P], U8, name=f"w1_scales{t}", align_bytes=64) for t in range(PACK)]
         for t in range(PACK):
             nc.vector.quantize_mx(w1_codes[t][:].bitcast(FP8X4), w1_scales[t][:], w1_bf[:, t * H : (t + 1) * H])
-        for i, (j0, n) in enumerate(pieces):
-            nc.vector.tensor_copy(xw[i][:], xw_all[:].bitcast(U32).indirect(offs_t[:, j0 // 16 : (j0 + n) // 16]))
 
-        w2w = keep.tile([P, 2 * N], U8, name="w2w", align_bytes=64)
-        w2s = keep.tile([P, N], U8, name="w2s", align_bytes=64)
+        w2w = keep.tile([P, 2 * N], U8, name="w2w", tag="w1_bf", align_bytes=64)
+        w2s = keep.tile([P, N], U8, name="w2s", tag="w1_raw1", align_bytes=64)
         nc.vector.tensor_copy(
             w2w[:].rearrange("p (t m b) -> p m t b", t=PACK, b=2), w2w_raw[:].rearrange("p (m t b) -> p m t b", t=PACK, b=2)
         )
@@ -92,36 +97,56 @@ def tile_picked_lshmean_silu_po_kernel(
         for t in range(PACK):
             for i, (j0, n) in enumerate(pieces):
                 cols = slice(j0, j0 + n)
-                acc = psum_y.tile([P, BANK], F32, name="acc")
+                acc = psum.tile([P, BANK], F32, name="acc", tag="bank")
                 nc.tensor.matmul_mx(
                     acc[:, 0:n], lhsT=w1_codes[t][:].bitcast(FP8X4), lhsT_scale=w1_scales[t][:],
                     rhs=xw[i][:].bitcast(FP8X4), rhs_scale=xs[:, cols], start=True, stop=True,
                 )
                 nc.scalar.copy(y[t][:, cols], acc[:, 0:n])
 
-        s = [keep.tile([P, S], F32, name=f"s{t}", align_bytes=64) for t in range(PACK)]
-        p = [keep.tile([P, V], F32, name=f"p{t}", align_bytes=64) for t in range(PACK)]
+        ident = keep.tile([P, P], F32, name="ident", align_bytes=64)
+        make_identity(nc, ident[:])
+        s = [[keep.tile([P, V], F32, name=f"s{t}_{h}", align_bytes=64) for h in range(2)] for t in range(PACK - 1)]
+        s.append([ring.tile([P, V], F32, name=f"s_last{h}", tag="ring", align_bytes=64) for h in range(2)])
+        turned_sb = [keep.tile([P, 2, P], F32, name=f"turned_sb{i}", tag="turned", align_bytes=64) for i in range(TENSOR_SUMS)]
+        p = [keep.tile([P, V], F32, name=f"p{t}", align_bytes=64) for t in range(PACK - 1)]
+        p.append(keep.tile([P, V], F32, name="p_last", tag="turned", align_bytes=64))
 
         def line_up(t, h):
             nc.vector.tensor_scalar(
-                s[t][:, h * V : (h + 1) * V], y[t][:].indirect(order_t[:, h * 32 : (h + 1) * 32]), 0.5, 0.0, ALU.mult, ALU.add
+                s[t][h][:], y[t][:].indirect(order_t[:, h * 32 : (h + 1) * 32]), 0.5, 0.0, ALU.mult, ALU.add
             )
 
-        def pair_sums(t):
-            pairs = s[t][:].rearrange("p (v e) -> p v e", e=2)
-            nc.vector.tensor_tensor(p[t][:], pairs[:, :, 0], pairs[:, :, 1], ALU.add)
+        def pair_sums(t, h):
+            pairs = s[t][h][:].rearrange("p (v e) -> p v e", e=2)
+            means = p[t][:, h * (V // 2) : (h + 1) * (V // 2)]
+            if 2 * t + h >= TENSOR_SUMS:
+                nc.vector.tensor_tensor(means, pairs[:, :, 0], pairs[:, :, 1], ALU.add)
+                return
+            turned = psum_turn.tile([P, 2, P], F32, name="turned")
+            for b in range(2):
+                for e in range(2):
+                    nc.tensor.matmul(
+                        turned[:, b, :], lhsT=pairs[:, b * P : (b + 1) * P, e], rhs=ident[:], is_transpose=True, start=(e == 0), stop=(e == 1)
+                    )
+            nc.scalar.copy(turned_sb[2 * t + h][:], turned[:])
+            back = psum.tile([P, 2, P], F32, name="back", tag="bank")
+            for b in range(2):
+                nc.tensor.transpose(back[:, b, :], turned_sb[2 * t + h][:, b, :], ident[:])
+            nc.scalar.copy(means, back[:].rearrange("p b v -> p (b v)"))
 
         for t in range(PACK):
             line_up(t, 0)
             if t > 0:
-                pair_sums(t - 1)
+                pair_sums(t - 1, 1)
             line_up(t, 1)
+            pair_sums(t, 0)
 
         out_rows = out_0.rearrange("(p t) j -> p t j", t=PACK)
         out_words = out_1[0].rearrange("p c r -> p (c r)").bitcast(I32)
         o_scales = keep.tile([P, S], U8, name="o_scales", align_bytes=64)
         starts = [sum(CHUNKS[:c]) for c in range(len(CHUNKS))]
-        u = [keep.tile([P, PACK, n], F32, name=f"u{c}", align_bytes=64) for c, n in enumerate(CHUNKS)]
+        u = [ring.tile([P, PACK, n], F32, name=f"u{c}", tag="ring", align_bytes=64) for c, n in enumerate(CHUNKS)]
         z_bf = [keep.tile([P, PACK * n], BF16, name=f"z_bf{c}", align_bytes=64) for c, n in enumerate(CHUNKS)]
         z_codes = [keep.tile([P, n], U32, name=f"z_codes{c}", align_bytes=64) for c, n in enumerate(CHUNKS)]
         z_scales = [keep.tile([P, n], U8, name=f"z_scales{c}", align_bytes=64) for c, n in enumerate(CHUNKS)]
@@ -136,7 +161,7 @@ def tile_picked_lshmean_silu_po_kernel(
                     u[c][:, t, :], p[t][:].indirect(bucket_t[:, j0 // 16 : (j0 + n) // 16]), y[t][:, j0 : j0 + n], ALU.subtract
                 )
                 if c == 0 and t == 0:
-                    pair_sums(PACK - 1)
+                    pair_sums(PACK - 1, 1)
             nc.scalar.activation(
                 z_bf[c][:].rearrange("p (g i t) -> p g t i", i=4, t=PACK),
                 u[c][:].rearrange("p t (g i) -> p g t i", i=4),
@@ -149,13 +174,15 @@ def tile_picked_lshmean_silu_po_kernel(
             nc.vector.quantize_mx(z_codes[c][:].bitcast(FP8X4), z_scales[c][:], z_bf[c][:])
             for b in range(n // BLOCK):
                 cols = slice(b * BLOCK, (b + 1) * BLOCK)
-                res = psum_o.tile([P, PACK, BLOCK], F32, name="res")
+                res = psum.tile([P, PACK, BLOCK], F32, name="res", tag="bank")
                 for t in range(PACK):
                     nc.tensor.matmul_mx(
                         res[:, t, :], lhsT=w2w[:, 2 * P * t : 2 * P * (t + 1)].bitcast(FP4X4), lhsT_scale=w2s[:, P * t : P * (t + 1)],
                         rhs=z_codes[c][:, cols].bitcast(FP8X4), rhs_scale=z_scales[c][:, cols], start=True, stop=True,
                     )
-                nc.scalar.copy(o_f32[c][:, :, cols], res[:])
+                final = j0 // BLOCK + b == S // BLOCK - 1
+                if not final:
+                    nc.scalar.copy(o_f32[c][:, :, cols], res[:])
                 bf_cols = o_bf[c][:, PACK * BLOCK * b : PACK * BLOCK * (b + 1)]
                 if j0 // BLOCK + b in VECTOR_CASTS:
                     nc.vector.tensor_copy(
@@ -164,6 +191,8 @@ def tile_picked_lshmean_silu_po_kernel(
                     )
                 else:
                     nc.scalar.copy(bf_cols.rearrange("p (j t) -> p j t", t=PACK), res[:].rearrange("p t j -> p j t"))
+                if final:
+                    nc.scalar.copy(o_f32[c][:, :, cols], res[:])
             nc.sync.dma_start(out_rows[:, :, j0 : j0 + n], o_f32[c][:])
 
         def hand_on(c):

@@ -1,7 +1,6 @@
 from contextlib import ExitStack
 
 import concourse.mybir as mybir
-from concourse.masks import make_identity
 
 F32 = mybir.dt.float32
 BF16 = mybir.dt.bfloat16
@@ -22,7 +21,7 @@ BANK = 512
 BLOCK = 128
 PIECES = (512, 512)
 W1_SCALAR = 64
-TENSOR_SUMS = 5
+GPSIMD_SUMS = 7
 CHUNKS = (128,256,256,256,128)
 VECTOR_CASTS = (2, 4, 5, 6)
 
@@ -35,8 +34,7 @@ def tile_picked_lshmean_silu_po_kernel(
         lists = ctx.enter_context(tc.tile_pool(name="lists", bufs=1))
         keep = ctx.enter_context(tc.tile_pool(name="keep", bufs=1))
         ring = ctx.enter_context(tc.tile_pool(name="ring", bufs=2))
-        psum = ctx.enter_context(tc.psum_pool(name="psum", bufs=6))
-        psum_turn = ctx.enter_context(tc.psum_pool(name="psum_turn", bufs=2))
+        psum = ctx.enter_context(tc.psum_pool(name="psum", bufs=8))
 
         offs_t = lists.tile([P, S // 16], U16, name="offs_t")
         order_t = lists.tile([P, S // 16], U16, name="order_t")
@@ -47,13 +45,9 @@ def tile_picked_lshmean_silu_po_kernel(
         w2s_raw = keep.tile([P, N], U8, name="w2s_raw", align_bytes=64)
         w2w_raw = keep.tile([P, 2 * N], U8, name="w2w_raw", align_bytes=64)
         w1_raw = [keep.tile([P, PACK, H // 2], F32, name=f"w1_raw{h}", tag=f"w1_raw{h}", align_bytes=64) for h in range(2)]
-        warm = keep.tile([P, 1], F32, name="warm")
-        warm_out = keep.tile([P, 1], F32, name="warm_out")
 
         nc.vector.memset(xs_all[:].bitcast(I32), 0)
         nc.vector.memset(w2s_raw[:].bitcast(I32), 0)
-        nc.vector.memset(warm[:], 0.0)
-        nc.scalar.activation(warm_out[:], warm[:], ACT.Silu)
 
         w1_rows = w1.rearrange("(p j) c -> p j c", j=PACK)
         nc.sync.dma_start(offs_t[:], offs)
@@ -104,13 +98,9 @@ def tile_picked_lshmean_silu_po_kernel(
                 )
                 nc.scalar.copy(y[t][:, cols], acc[:, 0:n])
 
-        ident = keep.tile([P, P], F32, name="ident", align_bytes=64)
-        make_identity(nc, ident[:])
         s = [[keep.tile([P, V], F32, name=f"s{t}_{h}", align_bytes=64) for h in range(2)] for t in range(PACK - 1)]
         s.append([ring.tile([P, V], F32, name=f"s_last{h}", tag="ring", align_bytes=64) for h in range(2)])
-        turned_sb = [keep.tile([P, 2, P], F32, name=f"turned_sb{i}", tag="turned", align_bytes=64) for i in range(TENSOR_SUMS)]
-        p = [keep.tile([P, V], F32, name=f"p{t}", align_bytes=64) for t in range(PACK - 1)]
-        p.append(keep.tile([P, V], F32, name="p_last", tag="turned", align_bytes=64))
+        p = [keep.tile([P, V], F32, name=f"p{t}", align_bytes=64) for t in range(PACK)]
 
         def line_up(t, h):
             nc.vector.tensor_scalar(
@@ -120,20 +110,8 @@ def tile_picked_lshmean_silu_po_kernel(
         def pair_sums(t, h):
             pairs = s[t][h][:].rearrange("p (v e) -> p v e", e=2)
             means = p[t][:, h * (V // 2) : (h + 1) * (V // 2)]
-            if 2 * t + h >= TENSOR_SUMS:
-                nc.vector.tensor_tensor(means, pairs[:, :, 0], pairs[:, :, 1], ALU.add)
-                return
-            turned = psum_turn.tile([P, 2, P], F32, name="turned")
-            for b in range(2):
-                for e in range(2):
-                    nc.tensor.matmul(
-                        turned[:, b, :], lhsT=pairs[:, b * P : (b + 1) * P, e], rhs=ident[:], is_transpose=True, start=(e == 0), stop=(e == 1)
-                    )
-            nc.scalar.copy(turned_sb[2 * t + h][:], turned[:])
-            back = psum.tile([P, 2, P], F32, name="back", tag="bank")
-            for b in range(2):
-                nc.tensor.transpose(back[:, b, :], turned_sb[2 * t + h][:, b, :], ident[:])
-            nc.scalar.copy(means, back[:].rearrange("p b v -> p (b v)"))
+            engine = nc.gpsimd if 2 * t + h < GPSIMD_SUMS else nc.vector
+            engine.tensor_tensor(means, pairs[:, :, 0], pairs[:, :, 1], ALU.add)
 
         for t in range(PACK):
             line_up(t, 0)

@@ -18,12 +18,9 @@ FLOPS = 2 * K * H * S + 2 * H * N * S
 P = 128
 PACK = 4
 BANK = 512
-BLOCK = 128
-PIECES = (512, 512)
-W1_SCALAR = 64
-GPSIMD_SUMS = 7
-CHUNKS = (128,256,256,256,128)
-VECTOR_CASTS = (2, 4, 5, 6)
+STRIP = 128
+W1_VECTOR = 0
+CHUNKS = (128, 256, 256, 128, 128, 128)
 
 
 def tile_picked_lshmean_silu_po_kernel(
@@ -47,7 +44,7 @@ def tile_picked_lshmean_silu_po_kernel(
         w1_raw = [keep.tile([P, PACK, H // 2], F32, name=f"w1_raw{h}", tag=f"w1_raw{h}", align_bytes=64) for h in range(2)]
 
         nc.vector.memset(xs_all[:].bitcast(I32), 0)
-        nc.vector.memset(w2s_raw[:].bitcast(I32), 0)
+        nc.gpsimd.memset(w2s_raw[:].bitcast(I32), 0)
 
         w1_rows = w1.rearrange("(p j) c -> p j c", j=PACK)
         nc.sync.dma_start(offs_t[:], offs)
@@ -63,73 +60,80 @@ def tile_picked_lshmean_silu_po_kernel(
             nc.sync.dma_start(w2s_raw[32 * q : 32 * q + 4, :].bitcast(I32), w2_scales[0, 4 * q : 4 * q + 4, :].bitcast(I32))
 
         xs = keep.tile([P, S], U8, name="xs", align_bytes=64)
-        pieces = [(sum(PIECES[:i]), n) for i, n in enumerate(PIECES)]
-        xw = [keep.tile([P, n], U32, name=f"xw{i}", align_bytes=64) for i, n in enumerate(PIECES)]
+        xw = [keep.tile([P, BANK], U32, name=f"xw{h}", align_bytes=64) for h in range(2)]
         nc.vector.tensor_copy(xs[:], xs_all[:].indirect(offs_t[:]))
+        for h in range(2):
+            nc.vector.tensor_copy(xw[h][:], xw_all[:].bitcast(U32).indirect(offs_t[:, 32 * h : 32 * (h + 1)]))
 
         w1_bf = keep.tile([P, PACK * H], BF16, name="w1_bf", tag="w1_bf", align_bytes=64)
         w1_dealt = w1_bf[:].rearrange("p (t m j) -> p m j t", t=PACK, j=PACK)
         half = P // 2
-        for i, (j0, n) in enumerate(pieces):
-            nc.vector.tensor_copy(xw[i][:], xw_all[:].bitcast(U32).indirect(offs_t[:, j0 // 16 : (j0 + n) // 16]))
         w1_src = [w1_raw[h][:].rearrange("p j (m t) -> p m j t", t=PACK) for h in range(2)]
         nc.scalar.copy(w1_dealt[:, 0:half], w1_src[0])
-        nc.scalar.copy(w1_dealt[:, half : half + W1_SCALAR], w1_src[1][:, 0:W1_SCALAR])
-        w1_codes = [keep.tile([P, P], U32, name=f"w1_codes{t}", align_bytes=64) for t in range(PACK)]
+        nc.scalar.copy(w1_dealt[:, half : P - W1_VECTOR], w1_src[1][:, 0 : half - W1_VECTOR])
+        w1_codes = [keep.tile([P, P], U32, name=f"w1_codes{t}", tag=f"w1_codes{t}", align_bytes=64) for t in range(PACK)]
         w1_scales = [keep.tile([P, P], U8, name=f"w1_scales{t}", align_bytes=64) for t in range(PACK)]
         for t in range(PACK):
             nc.vector.quantize_mx(w1_codes[t][:].bitcast(FP8X4), w1_scales[t][:], w1_bf[:, t * H : (t + 1) * H])
 
-        w2w = keep.tile([P, 2 * N], U8, name="w2w", tag="w1_bf", align_bytes=64)
-        w2s = keep.tile([P, N], U8, name="w2s", tag="w1_raw1", align_bytes=64)
-        nc.vector.tensor_copy(
-            w2w[:].rearrange("p (t m b) -> p m t b", t=PACK, b=2), w2w_raw[:].rearrange("p (m t b) -> p m t b", t=PACK, b=2)
-        )
-        nc.vector.tensor_copy(w2s[:].rearrange("p (t m) -> p m t", t=PACK), w2s_raw[:].rearrange("p (m t) -> p m t", t=PACK))
-
         y = [keep.tile([P, S], F32, name=f"y{t}", align_bytes=64) for t in range(PACK)]
         for t in range(PACK):
-            for i, (j0, n) in enumerate(pieces):
+            n = BANK // 2 if t == 0 else BANK
+            for j0 in range(0, S, n):
                 cols = slice(j0, j0 + n)
-                acc = psum.tile([P, BANK], F32, name="acc", tag="bank")
+                acc = psum.tile([P, n], F32, name="acc", tag="bank")
                 nc.tensor.matmul_mx(
-                    acc[:, 0:n], lhsT=w1_codes[t][:].bitcast(FP8X4), lhsT_scale=w1_scales[t][:],
-                    rhs=xw[i][:].bitcast(FP8X4), rhs_scale=xs[:, cols], start=True, stop=True,
+                    acc[:], lhsT=w1_codes[t][:].bitcast(FP8X4), lhsT_scale=w1_scales[t][:],
+                    rhs=xw[j0 // BANK][:, j0 % BANK : j0 % BANK + n].bitcast(FP8X4), rhs_scale=xs[:, cols], start=True, stop=True,
                 )
-                nc.scalar.copy(y[t][:, cols], acc[:, 0:n])
+                if t == 0 and j0 // n % 2 == 1:
+                    nc.vector.tensor_copy(y[t][:, cols], acc[:])
+                else:
+                    nc.scalar.copy(y[t][:, cols], acc[:])
+
+        w2w = keep.tile([P, 2 * N], U8, name="w2w", tag="w1_bf", align_bytes=64)
+        w2s = keep.tile([P, N], U8, name="w2s", tag="w1_codes0", align_bytes=64)
+        nc.gpsimd.tensor_copy(
+            w2w[:].rearrange("p (t m b) -> p t m b", t=PACK, b=2), w2w_raw[:].rearrange("p (m t b) -> p t m b", t=PACK, b=2)
+        )
+        nc.gpsimd.tensor_copy(w2s[:].rearrange("p (t m) -> p t m", t=PACK), w2s_raw[:].rearrange("p (m t) -> p t m", t=PACK))
 
         s = [[keep.tile([P, V], F32, name=f"s{t}_{h}", align_bytes=64) for h in range(2)] for t in range(PACK - 1)]
         s.append([ring.tile([P, V], F32, name=f"s_last{h}", tag="ring", align_bytes=64) for h in range(2)])
         p = [keep.tile([P, V], F32, name=f"p{t}", align_bytes=64) for t in range(PACK)]
 
-        def line_up(t, h):
+        def line_up(t, j0, n):
             nc.vector.tensor_scalar(
-                s[t][h][:], y[t][:].indirect(order_t[:, h * 32 : (h + 1) * 32]), 0.5, 0.0, ALU.mult, ALU.add
+                s[t][j0 // V][:, j0 % V : j0 % V + n], y[t][:].indirect(order_t[:, j0 // 16 : (j0 + n) // 16]), 0.5, 0.0, ALU.mult, ALU.add
             )
 
-        def pair_sums(t, h):
-            pairs = s[t][h][:].rearrange("p (v e) -> p v e", e=2)
-            means = p[t][:, h * (V // 2) : (h + 1) * (V // 2)]
-            engine = nc.gpsimd if 2 * t + h < GPSIMD_SUMS else nc.vector
-            engine.tensor_tensor(means, pairs[:, :, 0], pairs[:, :, 1], ALU.add)
+        def pair_sums(engine, t, j0, n):
+            pairs = s[t][j0 // V][:, j0 % V : j0 % V + n].rearrange("p (v e) -> p v e", e=2)
+            engine.tensor_tensor(p[t][:, j0 // 2 : (j0 + n) // 2], pairs[:, :, 0], pairs[:, :, 1], ALU.add)
 
+        last_piece = (S - V // 2, V // 2)
         for t in range(PACK):
-            line_up(t, 0)
-            if t > 0:
-                pair_sums(t - 1, 1)
-            line_up(t, 1)
-            pair_sums(t, 0)
+            pieces = [(0, V), (V, V)] if t < PACK - 1 else [(0, V), (V, V // 2), last_piece]
+            for j0, n in pieces:
+                line_up(t, j0, n)
+                if (t, j0) != (PACK - 1, last_piece[0]):
+                    pair_sums(nc.gpsimd, t, j0, n)
 
         out_rows = out_0.rearrange("(p t) j -> p t j", t=PACK)
         out_words = out_1[0].rearrange("p c r -> p (c r)").bitcast(I32)
         o_scales = keep.tile([P, S], U8, name="o_scales", align_bytes=64)
+        last = len(CHUNKS) - 1
         starts = [sum(CHUNKS[:c]) for c in range(len(CHUNKS))]
         u = [ring.tile([P, PACK, n], F32, name=f"u{c}", tag="ring", align_bytes=64) for c, n in enumerate(CHUNKS)]
         z_bf = [keep.tile([P, PACK * n], BF16, name=f"z_bf{c}", align_bytes=64) for c, n in enumerate(CHUNKS)]
         z_codes = [keep.tile([P, n], U32, name=f"z_codes{c}", align_bytes=64) for c, n in enumerate(CHUNKS)]
         z_scales = [keep.tile([P, n], U8, name=f"z_scales{c}", align_bytes=64) for c, n in enumerate(CHUNKS)]
         o_f32 = [keep.tile([P, PACK, n], F32, name=f"o_f32{c}", align_bytes=64) for c, n in enumerate(CHUNKS)]
-        o_bf = [keep.tile([P, PACK * n], BF16, name=f"o_bf{c}", align_bytes=64) for c, n in enumerate(CHUNKS)]
+        o_bf = [
+            keep.tile([P, PACK * n], BF16, name=f"o_bf{c}", align_bytes=64) if c in (0, last)
+            else ring.tile([P, PACK * n], BF16, name=f"o_bf{c}", tag="ring", align_bytes=64)
+            for c, n in enumerate(CHUNKS)
+        ]
         o_codes = [keep.tile([P, n], I32, name=f"o_codes{c}", align_bytes=64) for c, n in enumerate(CHUNKS)]
 
         def differences(c):
@@ -139,7 +143,7 @@ def tile_picked_lshmean_silu_po_kernel(
                     u[c][:, t, :], p[t][:].indirect(bucket_t[:, j0 // 16 : (j0 + n) // 16]), y[t][:, j0 : j0 + n], ALU.subtract
                 )
                 if c == 0 and t == 0:
-                    pair_sums(PACK - 1, 1)
+                    pair_sums(nc.vector, PACK - 1, *last_piece)
             nc.scalar.activation(
                 z_bf[c][:].rearrange("p (g i t) -> p g t i", i=4, t=PACK),
                 u[c][:].rearrange("p t (g i) -> p g t i", i=4),
@@ -150,42 +154,44 @@ def tile_picked_lshmean_silu_po_kernel(
         def second_product(c):
             j0, n = starts[c], CHUNKS[c]
             nc.vector.quantize_mx(z_codes[c][:].bitcast(FP8X4), z_scales[c][:], z_bf[c][:])
-            for b in range(n // BLOCK):
-                cols = slice(b * BLOCK, (b + 1) * BLOCK)
-                res = psum.tile([P, PACK, BLOCK], F32, name="res", tag="bank")
+            for b in range(n // STRIP):
+                cols = slice(b * STRIP, (b + 1) * STRIP)
+                res = psum.tile([P, PACK, STRIP], F32, name="res", tag="bank")
                 for t in range(PACK):
                     nc.tensor.matmul_mx(
                         res[:, t, :], lhsT=w2w[:, 2 * P * t : 2 * P * (t + 1)].bitcast(FP4X4), lhsT_scale=w2s[:, P * t : P * (t + 1)],
                         rhs=z_codes[c][:, cols].bitcast(FP8X4), rhs_scale=z_scales[c][:, cols], start=True, stop=True,
                     )
-                final = j0 // BLOCK + b == S // BLOCK - 1
-                if not final:
+                if c != last:
                     nc.scalar.copy(o_f32[c][:, :, cols], res[:])
-                bf_cols = o_bf[c][:, PACK * BLOCK * b : PACK * BLOCK * (b + 1)]
-                if j0 // BLOCK + b in VECTOR_CASTS:
-                    nc.vector.tensor_copy(
-                        bf_cols.rearrange("p (g i t) -> p g t i", i=4, t=PACK),
-                        o_f32[c][:, :, cols].rearrange("p t (g i) -> p g t i", i=4),
-                    )
-                else:
+                if c in (0, last):
+                    bf_cols = o_bf[c][:, PACK * STRIP * b : PACK * STRIP * (b + 1)]
                     nc.scalar.copy(bf_cols.rearrange("p (j t) -> p j t", t=PACK), res[:].rearrange("p t j -> p j t"))
-                if final:
+                if c == last:
                     nc.scalar.copy(o_f32[c][:, :, cols], res[:])
             nc.sync.dma_start(out_rows[:, :, j0 : j0 + n], o_f32[c][:])
 
         def hand_on(c):
             j0, n = starts[c], CHUNKS[c]
+            if c not in (0, last):
+                for b in range(n // STRIP):
+                    nc.vector.tensor_copy(
+                        o_bf[c][:, PACK * STRIP * b : PACK * STRIP * (b + 1)].rearrange("p (g i t) -> p g t i", i=4, t=PACK),
+                        o_f32[c][:, :, b * STRIP : (b + 1) * STRIP].rearrange("p t (g i) -> p g t i", i=4),
+                    )
             nc.vector.quantize_mx(o_codes[c][:].bitcast(FP8X4), o_scales[:, j0 : j0 + n], o_bf[c][:])
-            nc.sync.dma_start(out_words[:, j0 : j0 + n], o_codes[c][:])
+            queue = nc.scalar if c == last else nc.sync
+            queue.dma_start(out_words[:, j0 : j0 + n], o_codes[c][:])
 
-        last = len(CHUNKS) - 1
-        for step in range(last + 3):
-            if step <= last:
-                differences(step)
-            if 1 <= step <= last + 1:
-                second_product(step - 1)
-            if step >= 2:
-                hand_on(step - 2)
+        for c in range(last + 1):
+            differences(c)
+            if c >= 1:
+                second_product(c - 1)
+            if c == 2:
+                hand_on(0)
+        second_product(last)
+        for c in range(1, last + 1):
+            hand_on(c)
         for q in range(4):
             queue = nc.sync if q % 2 == 0 else nc.scalar
             queue.dma_start(out_2[0, 4 * q : 4 * q + 4, :].bitcast(I32), o_scales[32 * q : 32 * q + 4, :].bitcast(I32))

@@ -19,7 +19,7 @@ P = 128
 PACK = 4
 BANK = 512
 STRIP = 128
-W1_VECTOR = 0
+FIRST_ON_SCALAR = 64
 CHUNKS = (128, 256, 256, 128, 128, 128)
 
 
@@ -31,50 +31,59 @@ def tile_picked_lshmean_silu_po_kernel(
         lists = ctx.enter_context(tc.tile_pool(name="lists", bufs=1))
         keep = ctx.enter_context(tc.tile_pool(name="keep", bufs=1))
         ring = ctx.enter_context(tc.tile_pool(name="ring", bufs=2))
+        reuse = ctx.enter_context(tc.tile_pool(name="reuse", bufs=1))
         psum = ctx.enter_context(tc.psum_pool(name="psum", bufs=8))
 
         offs_t = lists.tile([P, S // 16], U16, name="offs_t")
         order_t = lists.tile([P, S // 16], U16, name="order_t")
         bucket_t = lists.tile([P, S // 16], U16, name="bucket_t")
 
-        xs_all = keep.tile([P, T], U8, name="xs_all", align_bytes=64)
+        xs_all = reuse.tile([P, T], U8, name="xs_all", align_bytes=64, offset=0)
         xw_all = keep.tile([P, T], I32, name="xw_all", align_bytes=64)
-        w2s_raw = keep.tile([P, N], U8, name="w2s_raw", align_bytes=64)
-        w2w_raw = keep.tile([P, 2 * N], U8, name="w2w_raw", align_bytes=64)
-        w1_raw = [keep.tile([P, PACK, H // 2], F32, name=f"w1_raw{h}", tag=f"w1_raw{h}", align_bytes=64) for h in range(2)]
+        w2s_raw = reuse.tile([P, N], U8, name="w2s_raw", align_bytes=64, offset=2 * N)
+        w2w_raw = reuse.tile([P, 2 * N], U8, name="w2w_raw", align_bytes=64, offset=0)
+        w1_raw = keep.tile([P, PACK, H], F32, name="w1_raw", align_bytes=64)
 
-        nc.vector.memset(xs_all[:].bitcast(I32), 0)
-        nc.gpsimd.memset(w2s_raw[:].bitcast(I32), 0)
+        xs = keep.tile([P, S], U8, name="xs", align_bytes=64)
+        nc.vector.memset(xs_all[0:16, :].bitcast(I32), 0)
+        nc.gpsimd.memset(xs_all[32:64, :].bitcast(I32), 0)
+        nc.gpsimd.memset(xs_all[64:P, :].bitcast(I32), 0)
+        nc.vector.memset(xs[:].bitcast(I32), 0)
 
         w1_rows = w1.rearrange("(p j) c -> p j c", j=PACK)
         nc.sync.dma_start(offs_t[:], offs)
-        nc.sync.dma_start(w1_raw[0][:], w1_rows[:, :, 0 : H // 2])
-        nc.sync.dma_start(order_t[:], order)
-        for q in range(4):
-            nc.sync.dma_start(xs_all[32 * q : 32 * q + 4, :].bitcast(I32), x_scales[0, 4 * q : 4 * q + 4, :].bitcast(I32))
+        nc.sync.dma_start(xs_all[16:32, :].bitcast(I32), x_scales[0].bitcast(I32))
         nc.sync.dma_start(xw_all[:], x_words[0].rearrange("p c r -> p (c r)").bitcast(I32))
-        nc.sync.dma_start(w1_raw[1][:], w1_rows[:, :, H // 2 : H])
+        nc.sync.dma_start(w1_raw[:], w1_rows)
+        nc.sync.dma_start(order_t[:], order)
         nc.sync.dma_start(bucket_t[:], bucket)
+
+        xs_picked = keep.tile([P, S], U8, name="xs_picked", align_bytes=64)
+        xw = keep.tile([P, S], U32, name="xw", align_bytes=64)
+        nc.vector.tensor_copy(xs_picked[:], xs_all[:].indirect(offs_t[:]))
+        for r in range(4):
+            nc.sync.dma_start(xs[r:P:32, :].bitcast(I32), xs_picked[16 + r : 32 : 4, :].bitcast(I32))
         nc.sync.dma_start(w2w_raw[:].bitcast(I32), w2_words[0].bitcast(I32))
-        for q in range(4):
-            nc.sync.dma_start(w2s_raw[32 * q : 32 * q + 4, :].bitcast(I32), w2_scales[0, 4 * q : 4 * q + 4, :].bitcast(I32))
+        nc.gpsimd.memset(w2s_raw[:].bitcast(I32), 0)
+        for r in range(4):
+            nc.sync.dma_start(w2s_raw[r:P:32, :].bitcast(I32), w2_scales[0, r:16:4, :].bitcast(I32))
+        nc.vector.tensor_copy(xw[:], xw_all[:].bitcast(U32).indirect(offs_t[:]))
 
-        xs = keep.tile([P, S], U8, name="xs", align_bytes=64)
-        xw = [keep.tile([P, BANK], U32, name=f"xw{h}", align_bytes=64) for h in range(2)]
-        nc.vector.tensor_copy(xs[:], xs_all[:].indirect(offs_t[:]))
-        for h in range(2):
-            nc.vector.tensor_copy(xw[h][:], xw_all[:].bitcast(U32).indirect(offs_t[:, 32 * h : 32 * (h + 1)]))
-
-        w1_bf = keep.tile([P, PACK * H], BF16, name="w1_bf", tag="w1_bf", align_bytes=64)
-        w1_dealt = w1_bf[:].rearrange("p (t m j) -> p m j t", t=PACK, j=PACK)
-        half = P // 2
-        w1_src = [w1_raw[h][:].rearrange("p j (m t) -> p m j t", t=PACK) for h in range(2)]
-        nc.scalar.copy(w1_dealt[:, 0:half], w1_src[0])
-        nc.scalar.copy(w1_dealt[:, half : P - W1_VECTOR], w1_src[1][:, 0 : half - W1_VECTOR])
+        w1_src = w1_raw[:].rearrange("p j (m t) -> p m j t", t=PACK)
+        w1_first = keep.tile([P, H], BF16, name="w1_first", tag="w1_first", align_bytes=64)
+        w1_mid = keep.tile([P, 2 * H], BF16, name="w1_mid", tag="w1_mid", align_bytes=64)
+        w1_last = keep.tile([P, H], BF16, name="w1_last", tag="w1_first", align_bytes=64)
+        w1_bf = [w1_first[:], w1_mid[:, 0:H], w1_mid[:, H : 2 * H], w1_last[:]]
         w1_codes = [keep.tile([P, P], U32, name=f"w1_codes{t}", tag=f"w1_codes{t}", align_bytes=64) for t in range(PACK)]
         w1_scales = [keep.tile([P, P], U8, name=f"w1_scales{t}", align_bytes=64) for t in range(PACK)]
-        for t in range(PACK):
-            nc.vector.quantize_mx(w1_codes[t][:].bitcast(FP8X4), w1_scales[t][:], w1_bf[:, t * H : (t + 1) * H])
+        first_dealt = w1_first[:].rearrange("p (m j) -> p m j", j=PACK)
+        nc.scalar.copy(first_dealt[:, 0:FIRST_ON_SCALAR], w1_src[:, 0:FIRST_ON_SCALAR, :, 0])
+        nc.vector.tensor_copy(first_dealt[:, FIRST_ON_SCALAR:P], w1_src[:, FIRST_ON_SCALAR:P, :, 0])
+        nc.vector.quantize_mx(w1_codes[0][:].bitcast(FP8X4), w1_scales[0][:], w1_bf[0])
+        nc.scalar.copy(w1_mid[:].rearrange("p (t m j) -> p m j t", t=2, j=PACK), w1_src[:, :, :, 1:3])
+        nc.vector.tensor_copy(w1_last[:].rearrange("p (m j) -> p m j", j=PACK), w1_src[:, :, :, PACK - 1])
+        for t in range(1, PACK):
+            nc.vector.quantize_mx(w1_codes[t][:].bitcast(FP8X4), w1_scales[t][:], w1_bf[t])
 
         y = [keep.tile([P, S], F32, name=f"y{t}", align_bytes=64) for t in range(PACK)]
         for t in range(PACK):
@@ -84,15 +93,15 @@ def tile_picked_lshmean_silu_po_kernel(
                 acc = psum.tile([P, n], F32, name="acc", tag="bank")
                 nc.tensor.matmul_mx(
                     acc[:], lhsT=w1_codes[t][:].bitcast(FP8X4), lhsT_scale=w1_scales[t][:],
-                    rhs=xw[j0 // BANK][:, j0 % BANK : j0 % BANK + n].bitcast(FP8X4), rhs_scale=xs[:, cols], start=True, stop=True,
+                    rhs=xw[:, cols].bitcast(FP8X4), rhs_scale=xs[:, cols], start=True, stop=True,
                 )
                 if t == 0 and j0 // n % 2 == 1:
                     nc.vector.tensor_copy(y[t][:, cols], acc[:])
                 else:
                     nc.scalar.copy(y[t][:, cols], acc[:])
 
-        w2w = keep.tile([P, 2 * N], U8, name="w2w", tag="w1_bf", align_bytes=64)
-        w2s = keep.tile([P, N], U8, name="w2s", tag="w1_codes0", align_bytes=64)
+        w2w = keep.tile([P, 2 * N], U8, name="w2w", tag="w1_first", align_bytes=64)
+        w2s = keep.tile([P, N], U8, name="w2s", tag="w1_codes1", align_bytes=64)
         nc.gpsimd.tensor_copy(
             w2w[:].rearrange("p (t m b) -> p t m b", t=PACK, b=2), w2w_raw[:].rearrange("p (m t b) -> p t m b", t=PACK, b=2)
         )

@@ -21,6 +21,10 @@ BANK = 512
 STRIP = 128
 FIRST_ON_SCALAR = 64
 CHUNKS = (128, 256, 256, 128, 128, 128)
+WORD_GROUPS = ((0,), (1, 2), (3, 4), (5, 6), (7,))
+STORE_GROUPS = ((0,), (1, 2), (3, 4), (5,), (6,), (7,))
+SCALAR_ROUNDS = (0, 6)
+RUN = 2
 
 
 def tile_picked_lshmean_silu_po_kernel(
@@ -73,15 +77,15 @@ def tile_picked_lshmean_silu_po_kernel(
         w1_first = keep.tile([P, H], BF16, name="w1_first", tag="w1_first", align_bytes=64)
         w1_mid = keep.tile([P, 2 * H], BF16, name="w1_mid", tag="w1_mid", align_bytes=64)
         w1_last = keep.tile([P, H], BF16, name="w1_last", tag="w1_first", align_bytes=64)
-        w1_bf = [w1_first[:], w1_mid[:, 0:H], w1_mid[:, H : 2 * H], w1_last[:]]
+        w1_bf = [w1_first[:], w1_last[:], w1_mid[:, 0:H], w1_mid[:, H : 2 * H]]
         w1_codes = [keep.tile([P, P], U32, name=f"w1_codes{t}", tag=f"w1_codes{t}", align_bytes=64) for t in range(PACK)]
         w1_scales = [keep.tile([P, P], U8, name=f"w1_scales{t}", align_bytes=64) for t in range(PACK)]
         first_dealt = w1_first[:].rearrange("p (m j) -> p m j", j=PACK)
         nc.scalar.copy(first_dealt[:, 0:FIRST_ON_SCALAR], w1_src[:, 0:FIRST_ON_SCALAR, :, 0])
         nc.vector.tensor_copy(first_dealt[:, FIRST_ON_SCALAR:P], w1_src[:, FIRST_ON_SCALAR:P, :, 0])
         nc.vector.quantize_mx(w1_codes[0][:].bitcast(FP8X4), w1_scales[0][:], w1_bf[0])
-        nc.scalar.copy(w1_mid[:].rearrange("p (t m j) -> p m j t", t=2, j=PACK), w1_src[:, :, :, 1:3])
-        nc.vector.tensor_copy(w1_last[:].rearrange("p (m j) -> p m j", j=PACK), w1_src[:, :, :, PACK - 1])
+        nc.scalar.copy(w1_mid[:].rearrange("p (t m j) -> p m j t", t=2, j=PACK), w1_src[:, :, :, 2:4])
+        nc.vector.tensor_copy(w1_last[:].rearrange("p (m j) -> p m j", j=PACK), w1_src[:, :, :, 1])
         for t in range(1, PACK):
             nc.vector.quantize_mx(w1_codes[t][:].bitcast(FP8X4), w1_scales[t][:], w1_bf[t])
 
@@ -100,7 +104,7 @@ def tile_picked_lshmean_silu_po_kernel(
                 else:
                     nc.scalar.copy(y[t][:, cols], acc[:])
 
-        w2w = keep.tile([P, 2 * N], U8, name="w2w", tag="w1_first", align_bytes=64)
+        w2w = keep.tile([P, 2 * N], U8, name="w2w", tag="w1_mid", align_bytes=64)
         w2s = keep.tile([P, N], U8, name="w2s", tag="w1_codes1", align_bytes=64)
         nc.gpsimd.tensor_copy(
             w2w[:].rearrange("p (t m b) -> p t m b", t=PACK, b=2), w2w_raw[:].rearrange("p (m t b) -> p t m b", t=PACK, b=2)
@@ -132,18 +136,29 @@ def tile_picked_lshmean_silu_po_kernel(
         out_words = out_1[0].rearrange("p c r -> p (c r)").bitcast(I32)
         o_scales = keep.tile([P, S], U8, name="o_scales", align_bytes=64)
         last = len(CHUNKS) - 1
+        last_strip = S // STRIP - 1
         starts = [sum(CHUNKS[:c]) for c in range(len(CHUNKS))]
         u = [ring.tile([P, PACK, n], F32, name=f"u{c}", tag="ring", align_bytes=64) for c, n in enumerate(CHUNKS)]
         z_bf = [keep.tile([P, PACK * n], BF16, name=f"z_bf{c}", align_bytes=64) for c, n in enumerate(CHUNKS)]
         z_codes = [keep.tile([P, n], U32, name=f"z_codes{c}", align_bytes=64) for c, n in enumerate(CHUNKS)]
         z_scales = [keep.tile([P, n], U8, name=f"z_scales{c}", align_bytes=64) for c, n in enumerate(CHUNKS)]
-        o_f32 = [keep.tile([P, PACK, n], F32, name=f"o_f32{c}", align_bytes=64) for c, n in enumerate(CHUNKS)]
+        o_f32 = [keep.tile([P, PACK, STRIP * len(g)], F32, name=f"o_f32{g[0]}", align_bytes=64) for g in STORE_GROUPS]
         o_bf = [
-            keep.tile([P, PACK * n], BF16, name=f"o_bf{c}", align_bytes=64) if c in (0, last)
-            else ring.tile([P, PACK * n], BF16, name=f"o_bf{c}", tag="ring", align_bytes=64)
-            for c, n in enumerate(CHUNKS)
+            ring.tile([P, PACK * STRIP * len(g)], BF16, name=f"o_bf{g[0]}", tag="ring", align_bytes=64) if i in (1, 2)
+            else keep.tile([P, PACK * STRIP * len(g)], BF16, name=f"o_bf{g[0]}", align_bytes=64)
+            for i, g in enumerate(WORD_GROUPS)
         ]
-        o_codes = [keep.tile([P, n], I32, name=f"o_codes{c}", align_bytes=64) for c, n in enumerate(CHUNKS)]
+        o_codes = [keep.tile([P, STRIP * len(g)], I32, name=f"o_codes{g[0]}", align_bytes=64) for g in WORD_GROUPS]
+        f32_strip = {b: o_f32[i][:, :, k * STRIP : (k + 1) * STRIP] for i, g in enumerate(STORE_GROUPS) for k, b in enumerate(g)}
+        bf_strip = {
+            b: o_bf[i][:, k * PACK * STRIP : (k + 1) * PACK * STRIP] for i, g in enumerate(WORD_GROUPS) for k, b in enumerate(g)
+        }
+
+        def woven(ap):
+            return ap.rearrange("p (g i t) -> p g t i", i=RUN, t=PACK)
+
+        def planes(ap):
+            return ap.rearrange("p t (g i) -> p g t i", i=RUN)
 
         def differences(c):
             j0, n = starts[c], CHUNKS[c]
@@ -153,44 +168,41 @@ def tile_picked_lshmean_silu_po_kernel(
                 )
                 if c == 0 and t == 0:
                     pair_sums(nc.vector, PACK - 1, *last_piece)
-            nc.scalar.activation(
-                z_bf[c][:].rearrange("p (g i t) -> p g t i", i=4, t=PACK),
-                u[c][:].rearrange("p t (g i) -> p g t i", i=4),
-                ACT.Silu,
-                scale=-1.0,
-            )
+            nc.scalar.activation(woven(z_bf[c][:]), planes(u[c][:]), ACT.Silu, scale=-1.0)
 
         def second_product(c):
             j0, n = starts[c], CHUNKS[c]
             nc.vector.quantize_mx(z_codes[c][:].bitcast(FP8X4), z_scales[c][:], z_bf[c][:])
-            for b in range(n // STRIP):
-                cols = slice(b * STRIP, (b + 1) * STRIP)
+            for k in range(n // STRIP):
+                b = j0 // STRIP + k
+                cols = slice(k * STRIP, (k + 1) * STRIP)
                 res = psum.tile([P, PACK, STRIP], F32, name="res", tag="bank")
                 for t in range(PACK):
                     nc.tensor.matmul_mx(
                         res[:, t, :], lhsT=w2w[:, 2 * P * t : 2 * P * (t + 1)].bitcast(FP4X4), lhsT_scale=w2s[:, P * t : P * (t + 1)],
                         rhs=z_codes[c][:, cols].bitcast(FP8X4), rhs_scale=z_scales[c][:, cols], start=True, stop=True,
                     )
-                if c != last:
-                    nc.scalar.copy(o_f32[c][:, :, cols], res[:])
-                if c in (0, last):
-                    bf_cols = o_bf[c][:, PACK * STRIP * b : PACK * STRIP * (b + 1)]
-                    nc.scalar.copy(bf_cols.rearrange("p (j t) -> p j t", t=PACK), res[:].rearrange("p t j -> p j t"))
-                if c == last:
-                    nc.scalar.copy(o_f32[c][:, :, cols], res[:])
-            nc.sync.dma_start(out_rows[:, :, j0 : j0 + n], o_f32[c][:])
+                nc.scalar.copy(f32_strip[b], res[:])
+                if b in SCALAR_ROUNDS:
+                    nc.scalar.copy(woven(bf_strip[b]), planes(res[:]))
+                for i, g in enumerate(STORE_GROUPS):
+                    if g[-1] == b:
+                        nc.sync.dma_start(out_rows[:, :, g[0] * STRIP : (b + 1) * STRIP], o_f32[i][:])
 
-        def hand_on(c):
-            j0, n = starts[c], CHUNKS[c]
-            if c not in (0, last):
-                for b in range(n // STRIP):
-                    nc.vector.tensor_copy(
-                        o_bf[c][:, PACK * STRIP * b : PACK * STRIP * (b + 1)].rearrange("p (g i t) -> p g t i", i=4, t=PACK),
-                        o_f32[c][:, :, b * STRIP : (b + 1) * STRIP].rearrange("p t (g i) -> p g t i", i=4),
-                    )
-            nc.vector.quantize_mx(o_codes[c][:].bitcast(FP8X4), o_scales[:, j0 : j0 + n], o_bf[c][:])
-            queue = nc.scalar if c == last else nc.sync
-            queue.dma_start(out_words[:, j0 : j0 + n], o_codes[c][:])
+        def hand_on(i):
+            g = WORD_GROUPS[i]
+            cols = slice(g[0] * STRIP, (g[-1] + 1) * STRIP)
+            for b in g:
+                if b not in SCALAR_ROUNDS:
+                    nc.vector.tensor_copy(woven(bf_strip[b]), planes(f32_strip[b]))
+            nc.vector.quantize_mx(o_codes[i][:].bitcast(FP8X4), o_scales[:, cols], o_bf[i][:])
+            queue = nc.scalar if i == len(WORD_GROUPS) - 1 else nc.sync
+            queue.dma_start(out_words[:, cols], o_codes[i][:])
+
+        def store_scales(cols):
+            for r in range(4):
+                queue = nc.sync if r % 2 == 0 else nc.scalar
+                queue.dma_start(out_2[0, r:16:4, cols].bitcast(I32), o_scales[r:P:32, cols].bitcast(I32))
 
         for c in range(last + 1):
             differences(c)
@@ -199,8 +211,6 @@ def tile_picked_lshmean_silu_po_kernel(
             if c == 2:
                 hand_on(0)
         second_product(last)
-        for c in range(1, last + 1):
-            hand_on(c)
-        for q in range(4):
-            queue = nc.sync if q % 2 == 0 else nc.scalar
-            queue.dma_start(out_2[0, 4 * q : 4 * q + 4, :].bitcast(I32), o_scales[32 * q : 32 * q + 4, :].bitcast(I32))
+        for i in range(1, len(WORD_GROUPS)):
+            hand_on(i)
+        store_scales(slice(0, S))

@@ -19,11 +19,12 @@ P = 128
 PACK = 4
 BANK = 512
 STRIP = 128
-FIRST_ON_SCALAR = 64
-CHUNKS = (128, 256, 256, 128, 128, 128)
-WORD_GROUPS = ((0,), (1, 2), (3, 4), (5, 6), (7,))
-STORE_GROUPS = ((0,), (1, 2), (3, 4), (5,), (6,), (7,))
-SCALAR_ROUNDS = (0, 6)
+FIRST_ON_SCALAR = 48
+CHUNKS = (256, 256, 256, 128, 128)
+WORD_GROUPS = ((0, 1), (2, 3), (4, 5), (6,), (7,))
+SCALAR_ROUNDS = ()
+WORD_STORE_ENDS = (256, 896, 1024)
+WHOLE_STORES = ()
 RUN = 2
 
 
@@ -74,20 +75,15 @@ def tile_picked_lshmean_silu_po_kernel(
         nc.vector.tensor_copy(xw[:], xw_all[:].bitcast(U32).indirect(offs_t[:]))
 
         w1_src = w1_raw[:].rearrange("p j (m t) -> p m j t", t=PACK)
-        w1_first = keep.tile([P, H], BF16, name="w1_first", tag="w1_first", align_bytes=64)
-        w1_mid = keep.tile([P, 2 * H], BF16, name="w1_mid", tag="w1_mid", align_bytes=64)
-        w1_last = keep.tile([P, H], BF16, name="w1_last", tag="w1_first", align_bytes=64)
-        w1_bf = [w1_first[:], w1_last[:], w1_mid[:, 0:H], w1_mid[:, H : 2 * H]]
+        w1_bf = [keep.tile([P, 2 * H], BF16, name=f"w1_bf{i}", tag=f"w1_bf{i}", align_bytes=64) for i in range(2)]
+        w1_dealt = [w1_bf[i][:].rearrange("p (t m j) -> p m j t", t=2, j=PACK) for i in range(2)]
         w1_codes = [keep.tile([P, P], U32, name=f"w1_codes{t}", tag=f"w1_codes{t}", align_bytes=64) for t in range(PACK)]
         w1_scales = [keep.tile([P, P], U8, name=f"w1_scales{t}", align_bytes=64) for t in range(PACK)]
-        first_dealt = w1_first[:].rearrange("p (m j) -> p m j", j=PACK)
-        nc.scalar.copy(first_dealt[:, 0:FIRST_ON_SCALAR], w1_src[:, 0:FIRST_ON_SCALAR, :, 0])
-        nc.vector.tensor_copy(first_dealt[:, FIRST_ON_SCALAR:P], w1_src[:, FIRST_ON_SCALAR:P, :, 0])
-        nc.vector.quantize_mx(w1_codes[0][:].bitcast(FP8X4), w1_scales[0][:], w1_bf[0])
-        nc.scalar.copy(w1_mid[:].rearrange("p (t m j) -> p m j t", t=2, j=PACK), w1_src[:, :, :, 2:4])
-        nc.vector.tensor_copy(w1_last[:].rearrange("p (m j) -> p m j", j=PACK), w1_src[:, :, :, 1])
-        for t in range(1, PACK):
-            nc.vector.quantize_mx(w1_codes[t][:].bitcast(FP8X4), w1_scales[t][:], w1_bf[t])
+        nc.scalar.copy(w1_dealt[0][:, 0:FIRST_ON_SCALAR], w1_src[:, 0:FIRST_ON_SCALAR, :, 0:2])
+        nc.vector.tensor_copy(w1_dealt[0][:, FIRST_ON_SCALAR:P], w1_src[:, FIRST_ON_SCALAR:P, :, 0:2])
+        nc.scalar.copy(w1_dealt[1], w1_src[:, :, :, 2:4])
+        for t in range(PACK):
+            nc.vector.quantize_mx(w1_codes[t][:].bitcast(FP8X4), w1_scales[t][:], w1_bf[t // 2][:, t % 2 * H : (t % 2 + 1) * H])
 
         y = [keep.tile([P, S], F32, name=f"y{t}", align_bytes=64) for t in range(PACK)]
         for t in range(PACK):
@@ -104,8 +100,8 @@ def tile_picked_lshmean_silu_po_kernel(
                 else:
                     nc.scalar.copy(y[t][:, cols], acc[:])
 
-        w2w = keep.tile([P, 2 * N], U8, name="w2w", tag="w1_mid", align_bytes=64)
-        w2s = keep.tile([P, N], U8, name="w2s", tag="w1_codes1", align_bytes=64)
+        w2w = keep.tile([P, 2 * N], U8, name="w2w", tag="w1_bf1", align_bytes=64)
+        w2s = keep.tile([P, N], U8, name="w2s", tag="w1_codes3", align_bytes=64)
         nc.gpsimd.tensor_copy(
             w2w[:].rearrange("p (t m b) -> p t m b", t=PACK, b=2), w2w_raw[:].rearrange("p (m t b) -> p t m b", t=PACK, b=2)
         )
@@ -136,20 +132,21 @@ def tile_picked_lshmean_silu_po_kernel(
         out_words = out_1[0].rearrange("p c r -> p (c r)").bitcast(I32)
         o_scales = keep.tile([P, S], U8, name="o_scales", align_bytes=64)
         last = len(CHUNKS) - 1
-        last_strip = S // STRIP - 1
         starts = [sum(CHUNKS[:c]) for c in range(len(CHUNKS))]
         u = [ring.tile([P, PACK, n], F32, name=f"u{c}", tag="ring", align_bytes=64) for c, n in enumerate(CHUNKS)]
         z_bf = [keep.tile([P, PACK * n], BF16, name=f"z_bf{c}", align_bytes=64) for c, n in enumerate(CHUNKS)]
         z_codes = [keep.tile([P, n], U32, name=f"z_codes{c}", align_bytes=64) for c, n in enumerate(CHUNKS)]
         z_scales = [keep.tile([P, n], U8, name=f"z_scales{c}", align_bytes=64) for c, n in enumerate(CHUNKS)]
-        o_f32 = [keep.tile([P, PACK, STRIP * len(g)], F32, name=f"o_f32{g[0]}", align_bytes=64) for g in STORE_GROUPS]
+        o_f32 = [keep.tile([P, PACK, n], F32, name=f"o_f32{c}", align_bytes=64) for c, n in enumerate(CHUNKS)]
         o_bf = [
-            ring.tile([P, PACK * STRIP * len(g)], BF16, name=f"o_bf{g[0]}", tag="ring", align_bytes=64) if i in (1, 2)
+            ring.tile([P, PACK * STRIP * len(g)], BF16, name=f"o_bf{g[0]}", tag="ring", align_bytes=64) if i in (0, 1)
             else keep.tile([P, PACK * STRIP * len(g)], BF16, name=f"o_bf{g[0]}", align_bytes=64)
             for i, g in enumerate(WORD_GROUPS)
         ]
-        o_codes = [keep.tile([P, STRIP * len(g)], I32, name=f"o_codes{g[0]}", align_bytes=64) for g in WORD_GROUPS]
-        f32_strip = {b: o_f32[i][:, :, k * STRIP : (k + 1) * STRIP] for i, g in enumerate(STORE_GROUPS) for k, b in enumerate(g)}
+        o_codes = keep.tile([P, S], I32, name="o_codes", align_bytes=64)
+        f32_strip = {
+            starts[c] // STRIP + k: o_f32[c][:, :, k * STRIP : (k + 1) * STRIP] for c, n in enumerate(CHUNKS) for k in range(n // STRIP)
+        }
         bf_strip = {
             b: o_bf[i][:, k * PACK * STRIP : (k + 1) * PACK * STRIP] for i, g in enumerate(WORD_GROUPS) for k, b in enumerate(g)
         }
@@ -173,21 +170,21 @@ def tile_picked_lshmean_silu_po_kernel(
         def second_product(c):
             j0, n = starts[c], CHUNKS[c]
             nc.vector.quantize_mx(z_codes[c][:].bitcast(FP8X4), z_scales[c][:], z_bf[c][:])
-            for k in range(n // STRIP):
-                b = j0 // STRIP + k
-                cols = slice(k * STRIP, (k + 1) * STRIP)
-                res = psum.tile([P, PACK, STRIP], F32, name="res", tag="bank")
-                for t in range(PACK):
+            for t0 in range(0, PACK, 2):
+                res = psum.tile([P, 2, n], F32, name="res", tag="bank")
+                for t in (t0, t0 + 1):
                     nc.tensor.matmul_mx(
-                        res[:, t, :], lhsT=w2w[:, 2 * P * t : 2 * P * (t + 1)].bitcast(FP4X4), lhsT_scale=w2s[:, P * t : P * (t + 1)],
-                        rhs=z_codes[c][:, cols].bitcast(FP8X4), rhs_scale=z_scales[c][:, cols], start=True, stop=True,
+                        res[:, t - t0, :], lhsT=w2w[:, 2 * P * t : 2 * P * (t + 1)].bitcast(FP4X4), lhsT_scale=w2s[:, P * t : P * (t + 1)],
+                        rhs=z_codes[c][:].bitcast(FP8X4), rhs_scale=z_scales[c][:], start=True, stop=True,
                     )
-                nc.scalar.copy(f32_strip[b], res[:])
+                nc.scalar.copy(o_f32[c][:, t0 : t0 + 2, :], res[:])
+                if c not in WHOLE_STORES:
+                    nc.sync.dma_start(out_rows[:, t0 : t0 + 2, j0 : j0 + n], o_f32[c][:, t0 : t0 + 2, :])
+            if c in WHOLE_STORES:
+                nc.sync.dma_start(out_rows[:, :, j0 : j0 + n], o_f32[c][:])
+            for b in range(j0 // STRIP, (j0 + n) // STRIP):
                 if b in SCALAR_ROUNDS:
-                    nc.scalar.copy(woven(bf_strip[b]), planes(res[:]))
-                for i, g in enumerate(STORE_GROUPS):
-                    if g[-1] == b:
-                        nc.sync.dma_start(out_rows[:, :, g[0] * STRIP : (b + 1) * STRIP], o_f32[i][:])
+                    nc.scalar.copy(woven(bf_strip[b]), planes(f32_strip[b]))
 
         def hand_on(i):
             g = WORD_GROUPS[i]
@@ -195,9 +192,12 @@ def tile_picked_lshmean_silu_po_kernel(
             for b in g:
                 if b not in SCALAR_ROUNDS:
                     nc.vector.tensor_copy(woven(bf_strip[b]), planes(f32_strip[b]))
-            nc.vector.quantize_mx(o_codes[i][:].bitcast(FP8X4), o_scales[:, cols], o_bf[i][:])
-            queue = nc.scalar if i == len(WORD_GROUPS) - 1 else nc.sync
-            queue.dma_start(out_words[:, cols], o_codes[i][:])
+            nc.vector.quantize_mx(o_codes[:, cols].bitcast(FP8X4), o_scales[:, cols], o_bf[i][:])
+            if cols.stop in WORD_STORE_ENDS:
+                k = WORD_STORE_ENDS.index(cols.stop)
+                stored = slice(WORD_STORE_ENDS[k - 1] if k else 0, cols.stop)
+                queue = nc.scalar if cols.stop == S else nc.sync
+                queue.dma_start(out_words[:, stored], o_codes[:, stored])
 
         def store_scales(cols):
             for r in range(4):
@@ -208,9 +208,7 @@ def tile_picked_lshmean_silu_po_kernel(
             differences(c)
             if c >= 1:
                 second_product(c - 1)
-            if c == 2:
-                hand_on(0)
         second_product(last)
-        for i in range(1, len(WORD_GROUPS)):
+        for i in range(len(WORD_GROUPS)):
             hand_on(i)
         store_scales(slice(0, S))

@@ -19,12 +19,13 @@ P = 128
 PACK = 4
 BANK = 512
 STRIP = 128
-FIRST_ON_SCALAR = 48
+FIRST_ON_SCALAR = 64
 CHUNKS = (256, 256, 256, 128, 128)
 WORD_GROUPS = ((0, 1), (2, 3), (4, 5), (6,), (7,))
 SCALAR_ROUNDS = ()
 WORD_STORE_ENDS = (256, 896, 1024)
 WHOLE_STORES = ()
+FIRST_PIECES = (256, 256, 256, 128, 128)
 RUN = 2
 
 
@@ -87,15 +88,16 @@ def tile_picked_lshmean_silu_po_kernel(
 
         y = [keep.tile([P, S], F32, name=f"y{t}", align_bytes=64) for t in range(PACK)]
         for t in range(PACK):
-            n = BANK // 2 if t == 0 else BANK
-            for j0 in range(0, S, n):
+            widths = FIRST_PIECES if t == 0 else (BANK, BANK)
+            for k, n in enumerate(widths):
+                j0 = sum(widths[:k])
                 cols = slice(j0, j0 + n)
                 acc = psum.tile([P, n], F32, name="acc", tag="bank")
                 nc.tensor.matmul_mx(
                     acc[:], lhsT=w1_codes[t][:].bitcast(FP8X4), lhsT_scale=w1_scales[t][:],
                     rhs=xw[:, cols].bitcast(FP8X4), rhs_scale=xs[:, cols], start=True, stop=True,
                 )
-                if t == 0 and j0 // n % 2 == 1:
+                if t == 0 and k % 2 == 1:
                     nc.vector.tensor_copy(y[t][:, cols], acc[:])
                 else:
                     nc.scalar.copy(y[t][:, cols], acc[:])
@@ -134,13 +136,13 @@ def tile_picked_lshmean_silu_po_kernel(
         last = len(CHUNKS) - 1
         starts = [sum(CHUNKS[:c]) for c in range(len(CHUNKS))]
         u = [ring.tile([P, PACK, n], F32, name=f"u{c}", tag="ring", align_bytes=64) for c, n in enumerate(CHUNKS)]
-        z_bf = [keep.tile([P, PACK * n], BF16, name=f"z_bf{c}", align_bytes=64) for c, n in enumerate(CHUNKS)]
+        z_bf = [keep.tile([P, PACK * n], BF16, name=f"z_bf{c}", tag=f"z_bf{c}", align_bytes=64) for c, n in enumerate(CHUNKS)]
         z_codes = [keep.tile([P, n], U32, name=f"z_codes{c}", align_bytes=64) for c, n in enumerate(CHUNKS)]
         z_scales = [keep.tile([P, n], U8, name=f"z_scales{c}", align_bytes=64) for c, n in enumerate(CHUNKS)]
         o_f32 = [keep.tile([P, PACK, n], F32, name=f"o_f32{c}", align_bytes=64) for c, n in enumerate(CHUNKS)]
         o_bf = [
-            ring.tile([P, PACK * STRIP * len(g)], BF16, name=f"o_bf{g[0]}", tag="ring", align_bytes=64) if i in (0, 1)
-            else keep.tile([P, PACK * STRIP * len(g)], BF16, name=f"o_bf{g[0]}", align_bytes=64)
+            ring.tile([P, PACK * STRIP * len(g)], BF16, name=f"o_bf{g[0]}", tag="ring", align_bytes=64) if i in (0,)
+            else keep.tile([P, PACK * STRIP * len(g)], BF16, name=f"o_bf{g[0]}", tag=f"z_bf{last - 1}" if i == 1 else f"o_bf{i}", align_bytes=64)
             for i, g in enumerate(WORD_GROUPS)
         ]
         o_codes = keep.tile([P, S], I32, name="o_codes", align_bytes=64)

@@ -1,6 +1,7 @@
 from contextlib import ExitStack
 
 import concourse.mybir as mybir
+from concourse.masks import make_identity
 
 F32 = mybir.dt.float32
 BF16 = mybir.dt.bfloat16
@@ -26,6 +27,7 @@ SCALAR_ROUNDS = ()
 WORD_STORE_ENDS = (256, 896, 1024)
 WHOLE_STORES = ()
 FIRST_PIECES = (256, 256, 256, 128, 128)
+TURNED_PLANES = 1
 RUN = 2
 
 
@@ -55,6 +57,9 @@ def tile_picked_lshmean_silu_po_kernel(
         nc.gpsimd.memset(xs_all[32:64, :].bitcast(I32), 0)
         nc.gpsimd.memset(xs_all[64:P, :].bitcast(I32), 0)
         nc.vector.memset(xs[:].bitcast(I32), 0)
+
+        ident = keep.tile([P, P], F32, name="ident", align_bytes=64)
+        make_identity(nc, ident[:])
 
         w1_rows = w1.rearrange("(p j) c -> p j c", j=PACK)
         nc.sync.dma_start(offs_t[:], offs)
@@ -122,12 +127,29 @@ def tile_picked_lshmean_silu_po_kernel(
             pairs = s[t][j0 // V][:, j0 % V : j0 % V + n].rearrange("p (v e) -> p v e", e=2)
             engine.tensor_tensor(p[t][:, j0 // 2 : (j0 + n) // 2], pairs[:, :, 0], pairs[:, :, 1], ALU.add)
 
+        def pair_sums_turned(t, j0):
+            pairs = s[t][j0 // V][:].rearrange("p (v e) -> p v e", e=2)
+            turned = psum.tile([P, 2, P], F32, name="turned", tag="bank")
+            for b in range(2):
+                for e in range(2):
+                    nc.tensor.matmul(
+                        turned[:, b, :], lhsT=pairs[:, b * P : (b + 1) * P, e], rhs=ident[:], is_transpose=True, start=(e == 0), stop=(e == 1)
+                    )
+            turned_sb = keep.tile([P, 2, P], F32, name=f"turned_sb{t}_{j0}", align_bytes=64)
+            nc.scalar.copy(turned_sb[:], turned[:])
+            back = psum.tile([P, 2, P], F32, name="back", tag="bank")
+            for b in range(2):
+                nc.tensor.transpose(back[:, b, :], turned_sb[:, b, :], ident[:])
+            nc.scalar.copy(p[t][:, j0 // 2 : (j0 + V) // 2], back[:].rearrange("p b v -> p (b v)"))
+
         last_piece = (S - V // 2, V // 2)
         for t in range(PACK):
             pieces = [(0, V), (V, V)] if t < PACK - 1 else [(0, V), (V, V // 2), last_piece]
             for j0, n in pieces:
                 line_up(t, j0, n)
-                if (t, j0) != (PACK - 1, last_piece[0]):
+                if t < TURNED_PLANES:
+                    pair_sums_turned(t, j0)
+                elif (t, j0) != (PACK - 1, last_piece[0]):
                     pair_sums(nc.gpsimd, t, j0, n)
 
         out_rows = out_0.rearrange("(p t) j -> p t j", t=PACK)

@@ -27,7 +27,7 @@ SCALAR_ROUNDS = ()
 WORD_STORE_ENDS = (256, 896, 1024)
 WHOLE_STORES = ()
 FIRST_PIECES = (256, 256, 256, 128, 128)
-TURNED_PLANES = 1
+TURNED = ((PACK - 2, V),)
 RUN = 2
 
 
@@ -142,12 +142,11 @@ def tile_picked_lshmean_silu_po_kernel(
                 nc.tensor.transpose(back[:, b, :], turned_sb[:, b, :], ident[:])
             nc.scalar.copy(p[t][:, j0 // 2 : (j0 + V) // 2], back[:].rearrange("p b v -> p (b v)"))
 
-        last_piece = (S - V // 2, V // 2)
+        last_piece = (V, V)
         for t in range(PACK):
-            pieces = [(0, V), (V, V)] if t < PACK - 1 else [(0, V), (V, V // 2), last_piece]
-            for j0, n in pieces:
+            for j0, n in ((0, V), last_piece):
                 line_up(t, j0, n)
-                if t < TURNED_PLANES:
+                if (t, j0) in TURNED:
                     pair_sums_turned(t, j0)
                 elif (t, j0) != (PACK - 1, last_piece[0]):
                     pair_sums(nc.gpsimd, t, j0, n)

@@ -24,8 +24,8 @@ FIRST_ON_SCALAR = 64
 CHUNKS = (256, 256, 256, 128, 128)
 WORD_GROUPS = ((0, 1), (2, 3), (4, 5), (6,), (7,))
 SCALAR_ROUNDS = ()
-WORD_STORE_ENDS = (256, 896, 1024)
-WHOLE_STORES = ()
+WORD_STORE_ENDS = (256, 768, 1024)
+WHOLE_STORES = (3, 4)
 FIRST_PIECES = (256, 256, 256, 128, 128)
 TURNED = ((PACK - 2, V),)
 RUN = 2
@@ -163,7 +163,7 @@ def tile_picked_lshmean_silu_po_kernel(
         o_f32 = [keep.tile([P, PACK, n], F32, name=f"o_f32{c}", align_bytes=64) for c, n in enumerate(CHUNKS)]
         o_bf = [
             ring.tile([P, PACK * STRIP * len(g)], BF16, name=f"o_bf{g[0]}", tag="ring", align_bytes=64) if i in (0,)
-            else keep.tile([P, PACK * STRIP * len(g)], BF16, name=f"o_bf{g[0]}", tag=f"z_bf{last - 1}" if i == 1 else f"o_bf{i}", align_bytes=64)
+            else keep.tile([P, PACK * STRIP * len(g)], BF16, name=f"o_bf{g[0]}", tag=f"z_bf{last}" if i == 1 else f"o_bf{i}", align_bytes=64)
             for i, g in enumerate(WORD_GROUPS)
         ]
         o_codes = keep.tile([P, S], I32, name="o_codes", align_bytes=64)
@@ -190,10 +190,11 @@ def tile_picked_lshmean_silu_po_kernel(
                     pair_sums(nc.vector, PACK - 1, *last_piece)
             nc.scalar.activation(woven(z_bf[c][:]), planes(u[c][:]), ACT.Silu, scale=-1.0)
 
-        def second_product(c):
+        def second_product(c, halves=(0, 2)):
             j0, n = starts[c], CHUNKS[c]
-            nc.vector.quantize_mx(z_codes[c][:].bitcast(FP8X4), z_scales[c][:], z_bf[c][:])
-            for t0 in range(0, PACK, 2):
+            if 0 in halves:
+                nc.vector.quantize_mx(z_codes[c][:].bitcast(FP8X4), z_scales[c][:], z_bf[c][:])
+            for t0 in halves:
                 res = psum.tile([P, 2, n], F32, name="res", tag="bank")
                 for t in (t0, t0 + 1):
                     nc.tensor.matmul_mx(
@@ -205,16 +206,18 @@ def tile_picked_lshmean_silu_po_kernel(
                     nc.sync.dma_start(out_rows[:, t0 : t0 + 2, j0 : j0 + n], o_f32[c][:, t0 : t0 + 2, :])
             if c in WHOLE_STORES:
                 nc.sync.dma_start(out_rows[:, :, j0 : j0 + n], o_f32[c][:])
-            for b in range(j0 // STRIP, (j0 + n) // STRIP):
-                if b in SCALAR_ROUNDS:
-                    nc.scalar.copy(woven(bf_strip[b]), planes(f32_strip[b]))
+
+        def round_out(i):
+            g = WORD_GROUPS[i]
+            c = max(k for k in range(last + 1) if starts[k] <= g[0] * STRIP)
+            if c == last:
+                nc.scalar.copy(woven(o_bf[i][:]), planes(o_f32[c][:]))
+            else:
+                nc.vector.tensor_copy(woven(o_bf[i][:]), planes(o_f32[c][:]))
 
         def hand_on(i):
             g = WORD_GROUPS[i]
             cols = slice(g[0] * STRIP, (g[-1] + 1) * STRIP)
-            for b in g:
-                if b not in SCALAR_ROUNDS:
-                    nc.vector.tensor_copy(woven(bf_strip[b]), planes(f32_strip[b]))
             nc.vector.quantize_mx(o_codes[:, cols].bitcast(FP8X4), o_scales[:, cols], o_bf[i][:])
             if cols.stop in WORD_STORE_ENDS:
                 k = WORD_STORE_ENDS.index(cols.stop)
@@ -227,11 +230,19 @@ def tile_picked_lshmean_silu_po_kernel(
                 queue = nc.sync if r % 2 == 0 else nc.scalar
                 queue.dma_start(out_2[0, r:16:4, cols].bitcast(I32), o_scales[r:P:32, cols].bitcast(I32))
 
-        for c in range(last + 1):
+        for c in range(last):
             differences(c)
             if c >= 1:
-                second_product(c - 1)
+                second_product(c - 1, (0,) if c == last - 1 else (0, 2))
+        differences(last)
+        second_product(last - 2, (2,))
+        second_product(last - 1)
         second_product(last)
-        for i in range(len(WORD_GROUPS)):
+        round_out(0)
+        hand_on(0)
+        round_out(1)
+        for i in range(1, len(WORD_GROUPS)):
+            if i + 1 < len(WORD_GROUPS):
+                round_out(i + 1)
             hand_on(i)
         store_scales(slice(0, S))

@@ -23,9 +23,7 @@ STRIP = 128
 FIRST_ON_SCALAR = 64
 CHUNKS = (256, 256, 256, 128, 128)
 WORD_GROUPS = ((0, 1), (2, 3), (4, 5), (6,), (7,))
-SCALAR_ROUNDS = ()
 WORD_STORE_ENDS = (256, 768, 1024)
-WHOLE_STORES = (3, 4)
 FIRST_PIECES = (256, 256, 256, 128, 128)
 TURNED = ((PACK - 2, V),)
 RUN = 2
@@ -160,19 +158,15 @@ def tile_picked_lshmean_silu_po_kernel(
         z_bf = [keep.tile([P, PACK * n], BF16, name=f"z_bf{c}", tag=f"z_bf{c}", align_bytes=64) for c, n in enumerate(CHUNKS)]
         z_codes = [keep.tile([P, n], U32, name=f"z_codes{c}", align_bytes=64) for c, n in enumerate(CHUNKS)]
         z_scales = [keep.tile([P, n], U8, name=f"z_scales{c}", align_bytes=64) for c, n in enumerate(CHUNKS)]
-        o_f32 = [keep.tile([P, PACK, n], F32, name=f"o_f32{c}", align_bytes=64) for c, n in enumerate(CHUNKS)]
+        o_f32 = [keep.tile([P, PACK, n], F32, name=f"o_f32{c}", align_bytes=64)[:] for c, n in enumerate(CHUNKS[: last - 1])]
+        o_short = keep.tile([P, PACK, 2 * STRIP], F32, name="o_short", align_bytes=64)
+        o_f32 = o_f32 + [o_short[:, :, 0:STRIP], o_short[:, :, STRIP : 2 * STRIP]]
         o_bf = [
             ring.tile([P, PACK * STRIP * len(g)], BF16, name=f"o_bf{g[0]}", tag="ring", align_bytes=64) if i in (0,)
             else keep.tile([P, PACK * STRIP * len(g)], BF16, name=f"o_bf{g[0]}", tag=f"z_bf{last}" if i == 1 else f"o_bf{i}", align_bytes=64)
             for i, g in enumerate(WORD_GROUPS)
         ]
         o_codes = keep.tile([P, S], I32, name="o_codes", align_bytes=64)
-        f32_strip = {
-            starts[c] // STRIP + k: o_f32[c][:, :, k * STRIP : (k + 1) * STRIP] for c, n in enumerate(CHUNKS) for k in range(n // STRIP)
-        }
-        bf_strip = {
-            b: o_bf[i][:, k * PACK * STRIP : (k + 1) * PACK * STRIP] for i, g in enumerate(WORD_GROUPS) for k, b in enumerate(g)
-        }
 
         def woven(ap):
             return ap.rearrange("p (g i t) -> p g t i", i=RUN, t=PACK)
@@ -202,18 +196,18 @@ def tile_picked_lshmean_silu_po_kernel(
                         rhs=z_codes[c][:].bitcast(FP8X4), rhs_scale=z_scales[c][:], start=True, stop=True,
                     )
                 nc.scalar.copy(o_f32[c][:, t0 : t0 + 2, :], res[:])
-                if c not in WHOLE_STORES:
+                if c < last - 1:
                     nc.sync.dma_start(out_rows[:, t0 : t0 + 2, j0 : j0 + n], o_f32[c][:, t0 : t0 + 2, :])
-            if c in WHOLE_STORES:
-                nc.sync.dma_start(out_rows[:, :, j0 : j0 + n], o_f32[c][:])
+                elif c == last:
+                    nc.sync.dma_start(out_rows[:, t0 : t0 + 2, starts[last - 1] : S], o_short[:, t0 : t0 + 2, :])
 
         def round_out(i):
             g = WORD_GROUPS[i]
             c = max(k for k in range(last + 1) if starts[k] <= g[0] * STRIP)
             if c == last:
-                nc.scalar.copy(woven(o_bf[i][:]), planes(o_f32[c][:]))
+                nc.scalar.copy(woven(o_bf[i][:]), planes(o_f32[c]))
             else:
-                nc.vector.tensor_copy(woven(o_bf[i][:]), planes(o_f32[c][:]))
+                nc.vector.tensor_copy(woven(o_bf[i][:]), planes(o_f32[c]))
 
         def hand_on(i):
             g = WORD_GROUPS[i]

@@ -26,6 +26,7 @@ WORD_GROUPS = ((0, 1), (2, 3), (4, 5), (6,), (7,))
 WORD_STORE_ENDS = (256, 768, 1024)
 FIRST_PIECES = (256, 256, 256, 128, 128)
 TURNED = ((PACK - 2, V),)
+WHOLE_PLANES = (1, 2)
 RUN = 2
 
 
@@ -61,9 +62,10 @@ def tile_picked_lshmean_silu_po_kernel(
 
         w1_rows = w1.rearrange("(p j) c -> p j c", j=PACK)
         nc.sync.dma_start(offs_t[:], offs)
-        nc.sync.dma_start(xs_all[16:32, :].bitcast(I32), x_scales[0].bitcast(I32))
+        nc.scalar.dma_start(xs_all[16:32, :].bitcast(I32), x_scales[0].bitcast(I32))
         nc.sync.dma_start(xw_all[:], x_words[0].rearrange("p c r -> p (c r)").bitcast(I32))
-        nc.sync.dma_start(w1_raw[:], w1_rows)
+        for h in range(2):
+            nc.sync.dma_start(w1_raw[:, 2 * h : 2 * h + 2, :], w1_rows[:, 2 * h : 2 * h + 2, :])
         nc.sync.dma_start(order_t[:], order)
         nc.sync.dma_start(bucket_t[:], bucket)
 
@@ -83,13 +85,15 @@ def tile_picked_lshmean_silu_po_kernel(
         w1_dealt = [w1_bf[i][:].rearrange("p (t m j) -> p m j t", t=2, j=PACK) for i in range(2)]
         w1_codes = [keep.tile([P, P], U32, name=f"w1_codes{t}", tag=f"w1_codes{t}", align_bytes=64) for t in range(PACK)]
         w1_scales = [keep.tile([P, P], U8, name=f"w1_scales{t}", align_bytes=64) for t in range(PACK)]
-        nc.scalar.copy(w1_dealt[0][:, 0:FIRST_ON_SCALAR], w1_src[:, 0:FIRST_ON_SCALAR, :, 0:2])
-        nc.vector.tensor_copy(w1_dealt[0][:, FIRST_ON_SCALAR:P], w1_src[:, FIRST_ON_SCALAR:P, :, 0:2])
+        nc.scalar.copy(w1_dealt[0][:, :, 0:2, :], w1_src[:, :, 0:2, 0:2])
+        nc.scalar.copy(w1_dealt[0][:, 0:FIRST_ON_SCALAR, 2:4, :], w1_src[:, 0:FIRST_ON_SCALAR, 2:4, 0:2])
+        nc.vector.tensor_copy(w1_dealt[0][:, FIRST_ON_SCALAR:P, 2:4, :], w1_src[:, FIRST_ON_SCALAR:P, 2:4, 0:2])
         nc.scalar.copy(w1_dealt[1], w1_src[:, :, :, 2:4])
         for t in range(PACK):
             nc.vector.quantize_mx(w1_codes[t][:].bitcast(FP8X4), w1_scales[t][:], w1_bf[t // 2][:, t % 2 * H : (t % 2 + 1) * H])
 
-        y = [keep.tile([P, S], F32, name=f"y{t}", align_bytes=64) for t in range(PACK)]
+        y = [keep.tile([P, 2 * S if t in WHOLE_PLANES else S], F32, name=f"y{t}", align_bytes=64) for t in range(PACK)]
+        nc.gpsimd.memset(y[1][:, S : 2 * S], 0.0)
         for t in range(PACK):
             widths = FIRST_PIECES if t == 0 else (BANK, BANK)
             for k, n in enumerate(widths):
@@ -112,8 +116,12 @@ def tile_picked_lshmean_silu_po_kernel(
         )
         nc.gpsimd.tensor_copy(w2s[:].rearrange("p (t m) -> p t m", t=PACK), w2s_raw[:].rearrange("p (m t) -> p t m", t=PACK))
 
-        s = [[keep.tile([P, V], F32, name=f"s{t}_{h}", align_bytes=64) for h in range(2)] for t in range(PACK - 1)]
-        s.append([ring.tile([P, V], F32, name=f"s_last{h}", tag="ring", align_bytes=64) for h in range(2)])
+        s_wide = keep.tile([P, S], F32, name="s_wide", align_bytes=64)
+        s_mid = keep.tile([P, S], F32, name="s_mid", align_bytes=64)
+        s_whole = [y[2][:, S : 2 * S], s_mid[:], s_wide[:]]
+        s = [[s_whole[t][:, h * V : (h + 1) * V] for h in range(2)] for t in range(PACK - 1)]
+        s_last = [ring.tile([P, V], F32, name=f"s_last{h}", tag="ring", align_bytes=64) for h in range(2)]
+        s.append([s_last[h][:] for h in range(2)])
         p = [keep.tile([P, V], F32, name=f"p{t}", align_bytes=64) for t in range(PACK)]
 
         def line_up(t, j0, n):
@@ -126,7 +134,7 @@ def tile_picked_lshmean_silu_po_kernel(
             engine.tensor_tensor(p[t][:, j0 // 2 : (j0 + n) // 2], pairs[:, :, 0], pairs[:, :, 1], ALU.add)
 
         def pair_sums_turned(t, j0):
-            pairs = s[t][j0 // V][:].rearrange("p (v e) -> p v e", e=2)
+            pairs = s[t][j0 // V].rearrange("p (v e) -> p v e", e=2)
             turned = psum.tile([P, 2, P], F32, name="turned", tag="bank")
             for b in range(2):
                 for e in range(2):
@@ -142,8 +150,11 @@ def tile_picked_lshmean_silu_po_kernel(
 
         last_piece = (V, V)
         for t in range(PACK):
+            if t in WHOLE_PLANES:
+                nc.vector.tensor_scalar(s_whole[t], y[t][:].indirect(order_t[:]), 0.5, 0.0, ALU.mult, ALU.add)
             for j0, n in ((0, V), last_piece):
-                line_up(t, j0, n)
+                if t not in WHOLE_PLANES:
+                    line_up(t, j0, n)
                 if (t, j0) in TURNED:
                     pair_sums_turned(t, j0)
                 elif (t, j0) != (PACK - 1, last_piece[0]):

@@ -26,7 +26,7 @@ WORD_GROUPS = ((0, 1), (2, 3), (4, 5), (6,), (7,))
 WORD_STORE_ENDS = (256, 768, 1024)
 FIRST_PIECES = (256, 256, 256, 128, 128)
 TURNED = ((PACK - 2, V),)
-WHOLE_PLANES = (1, 2)
+WHOLE_PLANES = (1,)
 RUN = 2
 
 
@@ -118,7 +118,8 @@ def tile_picked_lshmean_silu_po_kernel(
 
         s_wide = keep.tile([P, S], F32, name="s_wide", align_bytes=64)
         s_mid = keep.tile([P, S], F32, name="s_mid", align_bytes=64)
-        s_whole = [y[2][:, S : 2 * S], s_mid[:], s_wide[:]]
+        s_first = keep.tile([P, S], F32, name="s_first", align_bytes=64)
+        s_whole = [s_first[:], s_mid[:], s_wide[:]]
         s = [[s_whole[t][:, h * V : (h + 1) * V] for h in range(2)] for t in range(PACK - 1)]
         s_last = [ring.tile([P, V], F32, name=f"s_last{h}", tag="ring", align_bytes=64) for h in range(2)]
         s.append([s_last[h][:] for h in range(2)])
@@ -152,7 +153,7 @@ def tile_picked_lshmean_silu_po_kernel(
         for t in range(PACK):
             if t in WHOLE_PLANES:
                 nc.vector.tensor_scalar(s_whole[t], y[t][:].indirect(order_t[:]), 0.5, 0.0, ALU.mult, ALU.add)
-            for j0, n in ((0, V), last_piece):
+            for j0, n in ((0, V // 2), (V // 2, V // 2), last_piece) if t == PACK - 1 else ((0, V), last_piece):
                 if t not in WHOLE_PLANES:
                     line_up(t, j0, n)
                 if (t, j0) in TURNED:
@@ -235,12 +236,14 @@ def tile_picked_lshmean_silu_po_kernel(
                 queue = nc.sync if r % 2 == 0 else nc.scalar
                 queue.dma_start(out_2[0, r:16:4, cols].bitcast(I32), o_scales[r:P:32, cols].bitcast(I32))
 
-        for c in range(last):
+        differences(0)
+        differences(1)
+        second_product(0)
+        differences(2)
+        for c in (last - 1, last):
+            second_product(c - 2, (0,))
             differences(c)
-            if c >= 1:
-                second_product(c - 1, (0,) if c == last - 1 else (0, 2))
-        differences(last)
-        second_product(last - 2, (2,))
+            second_product(c - 2, (2,))
         second_product(last - 1)
         second_product(last)
         round_out(0)

@@ -37,7 +37,7 @@ def tile_picked_lshmean_silu_po_kernel(
     with ExitStack() as ctx:
         lists = ctx.enter_context(tc.tile_pool(name="lists", bufs=1))
         keep = ctx.enter_context(tc.tile_pool(name="keep", bufs=1))
-        ring = ctx.enter_context(tc.tile_pool(name="ring", bufs=2))
+        ring = ctx.enter_context(tc.tile_pool(name="ring", bufs=1))
         reuse = ctx.enter_context(tc.tile_pool(name="reuse", bufs=1))
         psum = ctx.enter_context(tc.psum_pool(name="psum", bufs=8))
 
@@ -121,17 +121,21 @@ def tile_picked_lshmean_silu_po_kernel(
         s_first = keep.tile([P, S], F32, name="s_first", align_bytes=64)
         s_whole = [s_first[:], s_mid[:], s_wide[:]]
         s = [[s_whole[t][:, h * V : (h + 1) * V] for h in range(2)] for t in range(PACK - 1)]
-        s_last = [ring.tile([P, V], F32, name=f"s_last{h}", tag="ring", align_bytes=64) for h in range(2)]
-        s.append([s_last[h][:] for h in range(2)])
         p = [keep.tile([P, V], F32, name=f"p{t}", align_bytes=64) for t in range(PACK)]
+        s_quarter = ring.tile([P, V // 2], F32, name="s_quarter", align_bytes=64, offset=0)
+        s_half = ring.tile([P, V], F32, name="s_half", align_bytes=64, offset=4096)
+        last_plane = {0: s_quarter[:], V // 2: p[PACK - 1][:, V // 2 : V], V: s_half[:]}
+
+        def lined_up(t, j0, n):
+            return last_plane[j0] if t == PACK - 1 else s[t][j0 // V][:, j0 % V : j0 % V + n]
 
         def line_up(t, j0, n):
             nc.vector.tensor_scalar(
-                s[t][j0 // V][:, j0 % V : j0 % V + n], y[t][:].indirect(order_t[:, j0 // 16 : (j0 + n) // 16]), 0.5, 0.0, ALU.mult, ALU.add
+                lined_up(t, j0, n), y[t][:].indirect(order_t[:, j0 // 16 : (j0 + n) // 16]), 0.5, 0.0, ALU.mult, ALU.add
             )
 
         def pair_sums(engine, t, j0, n):
-            pairs = s[t][j0 // V][:, j0 % V : j0 % V + n].rearrange("p (v e) -> p v e", e=2)
+            pairs = lined_up(t, j0, n).rearrange("p (v e) -> p v e", e=2)
             engine.tensor_tensor(p[t][:, j0 // 2 : (j0 + n) // 2], pairs[:, :, 0], pairs[:, :, 1], ALU.add)
 
         def pair_sums_turned(t, j0):
@@ -166,7 +170,7 @@ def tile_picked_lshmean_silu_po_kernel(
         o_scales = keep.tile([P, S], U8, name="o_scales", align_bytes=64)
         last = len(CHUNKS) - 1
         starts = [sum(CHUNKS[:c]) for c in range(len(CHUNKS))]
-        u = [ring.tile([P, PACK, n], F32, name=f"u{c}", tag="ring", align_bytes=64) for c, n in enumerate(CHUNKS)]
+        u = [ring.tile([P, PACK, n], F32, name=f"u{c}", align_bytes=64, offset=(0, 4096)[c % 2]) for c, n in enumerate(CHUNKS)]
         z_bf = [keep.tile([P, PACK * n], BF16, name=f"z_bf{c}", tag=f"z_bf{c}", align_bytes=64) for c, n in enumerate(CHUNKS)]
         z_codes = [keep.tile([P, n], U32, name=f"z_codes{c}", align_bytes=64) for c, n in enumerate(CHUNKS)]
         z_scales = [keep.tile([P, n], U8, name=f"z_scales{c}", align_bytes=64) for c, n in enumerate(CHUNKS)]
@@ -174,7 +178,7 @@ def tile_picked_lshmean_silu_po_kernel(
         o_short = keep.tile([P, PACK, 2 * STRIP], F32, name="o_short", align_bytes=64)
         o_f32 = o_f32 + [o_short[:, :, 0:STRIP], o_short[:, :, STRIP : 2 * STRIP]]
         o_bf = [
-            ring.tile([P, PACK * STRIP * len(g)], BF16, name=f"o_bf{g[0]}", tag="ring", align_bytes=64) if i in (0,)
+            ring.tile([P, PACK * STRIP * len(g)], BF16, name=f"o_bf{g[0]}", align_bytes=64, offset=4096) if i in (0,)
             else keep.tile([P, PACK * STRIP * len(g)], BF16, name=f"o_bf{g[0]}", tag=f"z_bf{last}" if i == 1 else f"o_bf{i}", align_bytes=64)
             for i, g in enumerate(WORD_GROUPS)
         ]

@@ -62,7 +62,7 @@ def tile_picked_lshmean_silu_po_kernel(
 
         w1_rows = w1.rearrange("(p j) c -> p j c", j=PACK)
         nc.sync.dma_start(offs_t[:], offs)
-        nc.scalar.dma_start(xs_all[16:32, :].bitcast(I32), x_scales[0].bitcast(I32))
+        nc.sync.dma_start(xs_all[16:32, :].bitcast(I32), x_scales[0].bitcast(I32))
         nc.sync.dma_start(xw_all[:], x_words[0].rearrange("p c r -> p (c r)").bitcast(I32))
         for h in range(2):
             nc.sync.dma_start(w1_raw[:, 2 * h : 2 * h + 2, :], w1_rows[:, 2 * h : 2 * h + 2, :])
@@ -83,14 +83,19 @@ def tile_picked_lshmean_silu_po_kernel(
         w1_src = w1_raw[:].rearrange("p j (m t) -> p m j t", t=PACK)
         w1_bf = [keep.tile([P, 2 * H], BF16, name=f"w1_bf{i}", tag=f"w1_bf{i}", align_bytes=64) for i in range(2)]
         w1_dealt = [w1_bf[i][:].rearrange("p (t m j) -> p m j t", t=2, j=PACK) for i in range(2)]
-        w1_codes = [keep.tile([P, P], U32, name=f"w1_codes{t}", tag=f"w1_codes{t}", align_bytes=64) for t in range(PACK)]
-        w1_scales = [keep.tile([P, P], U8, name=f"w1_scales{t}", align_bytes=64) for t in range(PACK)]
+        late_codes = keep.tile([P, 2 * P], U32, name="late_codes", tag="late_codes", align_bytes=64)
+        late_scales = keep.tile([P, 2 * P], U8, name="late_scales", align_bytes=64)
+        early_codes = [keep.tile([P, P], U32, name=f"w1_codes{t}", align_bytes=64) for t in range(2)]
+        early_scales = [keep.tile([P, P], U8, name=f"w1_scales{t}", align_bytes=64) for t in range(2)]
+        w1_codes = [early_codes[0][:], early_codes[1][:], late_codes[:, 0:P], late_codes[:, P : 2 * P]]
+        w1_scales = [early_scales[0][:], early_scales[1][:], late_scales[:, 0:P], late_scales[:, P : 2 * P]]
         nc.scalar.copy(w1_dealt[0][:, :, 0:2, :], w1_src[:, :, 0:2, 0:2])
         nc.scalar.copy(w1_dealt[0][:, 0:FIRST_ON_SCALAR, 2:4, :], w1_src[:, 0:FIRST_ON_SCALAR, 2:4, 0:2])
         nc.vector.tensor_copy(w1_dealt[0][:, FIRST_ON_SCALAR:P, 2:4, :], w1_src[:, FIRST_ON_SCALAR:P, 2:4, 0:2])
         nc.scalar.copy(w1_dealt[1], w1_src[:, :, :, 2:4])
-        for t in range(PACK):
-            nc.vector.quantize_mx(w1_codes[t][:].bitcast(FP8X4), w1_scales[t][:], w1_bf[t // 2][:, t % 2 * H : (t % 2 + 1) * H])
+        for t in range(2):
+            nc.vector.quantize_mx(w1_codes[t].bitcast(FP8X4), w1_scales[t], w1_bf[0][:, t * H : (t + 1) * H])
+        nc.vector.quantize_mx(late_codes[:].bitcast(FP8X4), late_scales[:], w1_bf[1][:])
 
         y = [keep.tile([P, 2 * S if t in WHOLE_PLANES else S], F32, name=f"y{t}", align_bytes=64) for t in range(PACK)]
         nc.gpsimd.memset(y[1][:, S : 2 * S], 0.0)
@@ -101,7 +106,7 @@ def tile_picked_lshmean_silu_po_kernel(
                 cols = slice(j0, j0 + n)
                 acc = psum.tile([P, n], F32, name="acc", tag="bank")
                 nc.tensor.matmul_mx(
-                    acc[:], lhsT=w1_codes[t][:].bitcast(FP8X4), lhsT_scale=w1_scales[t][:],
+                    acc[:], lhsT=w1_codes[t].bitcast(FP8X4), lhsT_scale=w1_scales[t],
                     rhs=xw[:, cols].bitcast(FP8X4), rhs_scale=xs[:, cols], start=True, stop=True,
                 )
                 if t == 0 and k % 2 == 1:
@@ -110,7 +115,7 @@ def tile_picked_lshmean_silu_po_kernel(
                     nc.scalar.copy(y[t][:, cols], acc[:])
 
         w2w = keep.tile([P, 2 * N], U8, name="w2w", tag="w1_bf1", align_bytes=64)
-        w2s = keep.tile([P, N], U8, name="w2s", tag="w1_codes3", align_bytes=64)
+        w2s = keep.tile([P, N], U8, name="w2s", tag="late_codes", align_bytes=64)
         nc.gpsimd.tensor_copy(
             w2w[:].rearrange("p (t m b) -> p t m b", t=PACK, b=2), w2w_raw[:].rearrange("p (m t b) -> p t m b", t=PACK, b=2)
         )
@@ -232,13 +237,11 @@ def tile_picked_lshmean_silu_po_kernel(
             if cols.stop in WORD_STORE_ENDS:
                 k = WORD_STORE_ENDS.index(cols.stop)
                 stored = slice(WORD_STORE_ENDS[k - 1] if k else 0, cols.stop)
-                queue = nc.scalar if cols.stop == S else nc.sync
-                queue.dma_start(out_words[:, stored], o_codes[:, stored])
+                nc.sync.dma_start(out_words[:, stored], o_codes[:, stored])
 
         def store_scales(cols):
             for r in range(4):
-                queue = nc.sync if r % 2 == 0 else nc.scalar
-                queue.dma_start(out_2[0, r:16:4, cols].bitcast(I32), o_scales[r:P:32, cols].bitcast(I32))
+                nc.sync.dma_start(out_2[0, r:16:4, cols].bitcast(I32), o_scales[r:P:32, cols].bitcast(I32))
 
         differences(0)
         differences(1)

@@ -23,7 +23,7 @@ STRIP = 128
 FIRST_ON_SCALAR = 64
 CHUNKS = (256, 256, 256, 128, 128)
 WORD_GROUPS = ((0, 1), (2, 3), (4, 5), (6,), (7,))
-WORD_STORE_ENDS = (256, 768, 1024)
+WORD_STORE_ENDS = (512, 1024)
 FIRST_PIECES = (256, 256, 256, 128, 128)
 TURNED = ((PACK - 2, V),)
 WHOLE_PLANES = (1,)
@@ -184,10 +184,10 @@ def tile_picked_lshmean_silu_po_kernel(
         o_f32 = o_f32 + [o_short[:, :, 0:STRIP], o_short[:, :, STRIP : 2 * STRIP]]
         o_bf = [
             ring.tile([P, PACK * STRIP * len(g)], BF16, name=f"o_bf{g[0]}", align_bytes=64, offset=4096) if i in (0,)
-            else keep.tile([P, PACK * STRIP * len(g)], BF16, name=f"o_bf{g[0]}", tag=f"z_bf{last}" if i == 1 else f"o_bf{i}", align_bytes=64)
+            else keep.tile([P, PACK * STRIP * len(g)], BF16, name=f"o_bf{g[0]}", tag=f"z_bf{last - 1}" if i == 1 else f"o_bf{i}", align_bytes=64)
             for i, g in enumerate(WORD_GROUPS)
         ]
-        o_codes = keep.tile([P, S], I32, name="o_codes", align_bytes=64)
+        o_codes = keep.tile([P, S], I32, name="o_codes", tag=f"z_bf{last}", align_bytes=64)
 
         def woven(ap):
             return ap.rearrange("p (g i t) -> p g t i", i=RUN, t=PACK)
@@ -254,9 +254,11 @@ def tile_picked_lshmean_silu_po_kernel(
         second_product(last - 1)
         second_product(last)
         round_out(0)
-        hand_on(0)
         round_out(1)
-        for i in range(1, len(WORD_GROUPS)):
+        hand_on(0)
+        hand_on(1)
+        round_out(2)
+        for i in range(2, len(WORD_GROUPS)):
             if i + 1 < len(WORD_GROUPS):
                 round_out(i + 1)
             hand_on(i)

@@ -1,7 +1,6 @@
 from contextlib import ExitStack
 
 import concourse.mybir as mybir
-from concourse.masks import make_identity
 
 F32 = mybir.dt.float32
 BF16 = mybir.dt.bfloat16
@@ -18,15 +17,10 @@ K, T, S, V, N, H = 512, 2048, 1024, 512, 512, 512
 FLOPS = 2 * K * H * S + 2 * H * N * S
 P = 128
 PACK = 4
-BANK = 512
-STRIP = 128
-FIRST_ON_SCALAR = 64
+HALF = S // 2
+W1_ON_SCALAR = 56
+WORD_PIECES = (256, 256, 256, 128, 128)
 CHUNKS = (256, 256, 256, 128, 128)
-WORD_GROUPS = ((0, 1), (2, 3), (4, 5), (6,), (7,))
-WORD_STORE_ENDS = (512, 1024)
-FIRST_PIECES = (256, 256, 256, 128, 128)
-TURNED = ((PACK - 2, V),)
-WHOLE_PLANES = (1,)
 RUN = 2
 
 
@@ -37,13 +31,15 @@ def tile_picked_lshmean_silu_po_kernel(
     with ExitStack() as ctx:
         lists = ctx.enter_context(tc.tile_pool(name="lists", bufs=1))
         keep = ctx.enter_context(tc.tile_pool(name="keep", bufs=1))
-        ring = ctx.enter_context(tc.tile_pool(name="ring", bufs=1))
         reuse = ctx.enter_context(tc.tile_pool(name="reuse", bufs=1))
         psum = ctx.enter_context(tc.psum_pool(name="psum", bufs=8))
 
         offs_t = lists.tile([P, S // 16], U16, name="offs_t")
         order_t = lists.tile([P, S // 16], U16, name="order_t")
         bucket_t = lists.tile([P, S // 16], U16, name="bucket_t")
+
+        def entries(list_t, j0, n):
+            return list_t[:, j0 // 16 : (j0 + n) // 16]
 
         xs_all = reuse.tile([P, T], U8, name="xs_all", align_bytes=64, offset=0)
         xw_all = keep.tile([P, T], I32, name="xw_all", align_bytes=64)
@@ -57,20 +53,14 @@ def tile_picked_lshmean_silu_po_kernel(
         nc.gpsimd.memset(xs_all[64:P, :].bitcast(I32), 0)
         nc.vector.memset(xs[:].bitcast(I32), 0)
 
-        ident = keep.tile([P, P], F32, name="ident", align_bytes=64)
-        make_identity(nc, ident[:])
-
-        w1_rows = w1.rearrange("(p j) c -> p j c", j=PACK)
         nc.sync.dma_start(offs_t[:], offs)
         nc.sync.dma_start(xs_all[16:32, :].bitcast(I32), x_scales[0].bitcast(I32))
+        nc.sync.dma_start(w1_raw[:], w1.rearrange("(p j) c -> p j c", j=PACK))
         nc.sync.dma_start(xw_all[:], x_words[0].rearrange("p c r -> p (c r)").bitcast(I32))
-        for h in range(2):
-            nc.sync.dma_start(w1_raw[:, 2 * h : 2 * h + 2, :], w1_rows[:, 2 * h : 2 * h + 2, :])
         nc.sync.dma_start(order_t[:], order)
         nc.sync.dma_start(bucket_t[:], bucket)
 
         xs_picked = keep.tile([P, S], U8, name="xs_picked", align_bytes=64)
-        xw = keep.tile([P, S], U32, name="xw", align_bytes=64)
         nc.vector.tensor_copy(xs_picked[:], xs_all[:].indirect(offs_t[:]))
         for r in range(4):
             nc.sync.dma_start(xs[r:P:32, :].bitcast(I32), xs_picked[16 + r : 32 : 4, :].bitcast(I32))
@@ -78,116 +68,115 @@ def tile_picked_lshmean_silu_po_kernel(
         nc.gpsimd.memset(w2s_raw[:].bitcast(I32), 0)
         for r in range(4):
             nc.sync.dma_start(w2s_raw[r:P:32, :].bitcast(I32), w2_scales[0, r:16:4, :].bitcast(I32))
-        nc.vector.tensor_copy(xw[:], xw_all[:].bitcast(U32).indirect(offs_t[:]))
 
         w1_src = w1_raw[:].rearrange("p j (m t) -> p m j t", t=PACK)
-        w1_bf = [keep.tile([P, 2 * H], BF16, name=f"w1_bf{i}", tag=f"w1_bf{i}", align_bytes=64) for i in range(2)]
-        w1_dealt = [w1_bf[i][:].rearrange("p (t m j) -> p m j t", t=2, j=PACK) for i in range(2)]
-        late_codes = keep.tile([P, 2 * P], U32, name="late_codes", tag="late_codes", align_bytes=64)
-        late_scales = keep.tile([P, 2 * P], U8, name="late_scales", align_bytes=64)
-        early_codes = [keep.tile([P, P], U32, name=f"w1_codes{t}", align_bytes=64) for t in range(2)]
-        early_scales = [keep.tile([P, P], U8, name=f"w1_scales{t}", align_bytes=64) for t in range(2)]
-        w1_codes = [early_codes[0][:], early_codes[1][:], late_codes[:, 0:P], late_codes[:, P : 2 * P]]
-        w1_scales = [early_scales[0][:], early_scales[1][:], late_scales[:, 0:P], late_scales[:, P : 2 * P]]
-        nc.scalar.copy(w1_dealt[0][:, :, 0:2, :], w1_src[:, :, 0:2, 0:2])
-        nc.scalar.copy(w1_dealt[0][:, 0:FIRST_ON_SCALAR, 2:4, :], w1_src[:, 0:FIRST_ON_SCALAR, 2:4, 0:2])
-        nc.vector.tensor_copy(w1_dealt[0][:, FIRST_ON_SCALAR:P, 2:4, :], w1_src[:, FIRST_ON_SCALAR:P, 2:4, 0:2])
-        nc.scalar.copy(w1_dealt[1], w1_src[:, :, :, 2:4])
-        for t in range(2):
-            nc.vector.quantize_mx(w1_codes[t].bitcast(FP8X4), w1_scales[t], w1_bf[0][:, t * H : (t + 1) * H])
-        nc.vector.quantize_mx(late_codes[:].bitcast(FP8X4), late_scales[:], w1_bf[1][:])
+        w1_bf = keep.tile([P, PACK * H], BF16, name="w1_bf", tag="w1_bf", align_bytes=64)
+        w1_dealt = w1_bf[:].rearrange("p (t m j) -> p m j t", t=PACK, j=PACK)
+        w1_codes = keep.tile([P, H], U32, name="w1_codes", align_bytes=64)
+        w1_scales = keep.tile([P, H], U8, name="w1_scales", align_bytes=64)
+        nc.scalar.copy(w1_dealt[:, 0:W1_ON_SCALAR], w1_src[:, 0:W1_ON_SCALAR])
+        nc.vector.tensor_copy(w1_dealt[:, W1_ON_SCALAR:P], w1_src[:, W1_ON_SCALAR:P])
+        nc.vector.quantize_mx(w1_codes[:].bitcast(FP8X4), w1_scales[:], w1_bf[:])
 
-        y = [keep.tile([P, 2 * S if t in WHOLE_PLANES else S], F32, name=f"y{t}", align_bytes=64) for t in range(PACK)]
-        nc.gpsimd.memset(y[1][:, S : 2 * S], 0.0)
-        for t in range(PACK):
-            widths = FIRST_PIECES if t == 0 else (BANK, BANK)
-            for k, n in enumerate(widths):
-                j0 = sum(widths[:k])
-                cols = slice(j0, j0 + n)
-                acc = psum.tile([P, n], F32, name="acc", tag="bank")
-                nc.tensor.matmul_mx(
-                    acc[:], lhsT=w1_codes[t].bitcast(FP8X4), lhsT_scale=w1_scales[t],
-                    rhs=xw[:, cols].bitcast(FP8X4), rhs_scale=xs[:, cols], start=True, stop=True,
-                )
-                if t == 0 and k % 2 == 1:
-                    nc.vector.tensor_copy(y[t][:, cols], acc[:])
-                else:
-                    nc.scalar.copy(y[t][:, cols], acc[:])
+        xw = keep.tile([P, S], U32, name="xw", tag="w1_bf", align_bytes=64)
+        word_starts = [sum(WORD_PIECES[:k]) for k in range(len(WORD_PIECES))]
+        for j0, n in zip(word_starts, WORD_PIECES):
+            nc.vector.tensor_copy(xw[:, j0 : j0 + n], xw_all[:].bitcast(U32).indirect(entries(offs_t, j0, n)))
 
-        w2w = keep.tile([P, 2 * N], U8, name="w2w", tag="w1_bf1", align_bytes=64)
-        w2s = keep.tile([P, N], U8, name="w2s", tag="late_codes", align_bytes=64)
+        w2w = keep.tile([P, 2 * N], U8, name="w2w", align_bytes=64)
+        w2s = keep.tile([P, N], U8, name="w2s", align_bytes=64)
         nc.gpsimd.tensor_copy(
             w2w[:].rearrange("p (t m b) -> p t m b", t=PACK, b=2), w2w_raw[:].rearrange("p (m t b) -> p t m b", t=PACK, b=2)
         )
         nc.gpsimd.tensor_copy(w2s[:].rearrange("p (t m) -> p t m", t=PACK), w2s_raw[:].rearrange("p (m t) -> p t m", t=PACK))
 
-        s_wide = keep.tile([P, S], F32, name="s_wide", align_bytes=64)
-        s_mid = keep.tile([P, S], F32, name="s_mid", align_bytes=64)
-        s_first = keep.tile([P, S], F32, name="s_first", align_bytes=64)
-        s_whole = [s_first[:], s_mid[:], s_wide[:]]
-        s = [[s_whole[t][:, h * V : (h + 1) * V] for h in range(2)] for t in range(PACK - 1)]
-        p = [keep.tile([P, V], F32, name=f"p{t}", align_bytes=64) for t in range(PACK)]
-        s_quarter = ring.tile([P, V // 2], F32, name="s_quarter", align_bytes=64, offset=0)
-        s_half = ring.tile([P, V], F32, name="s_half", align_bytes=64, offset=4096)
-        last_plane = {0: s_quarter[:], V // 2: p[PACK - 1][:, V // 2 : V], V: s_half[:]}
+        y = [keep.tile([P, S], F32, name=f"y{t}", align_bytes=64) for t in range(PACK)]
 
-        def lined_up(t, j0, n):
-            return last_plane[j0] if t == PACK - 1 else s[t][j0 // V][:, j0 % V : j0 % V + n]
-
-        def line_up(t, j0, n):
-            nc.vector.tensor_scalar(
-                lined_up(t, j0, n), y[t][:].indirect(order_t[:, j0 // 16 : (j0 + n) // 16]), 0.5, 0.0, ALU.mult, ALU.add
+        def first_product(acc, t, j0, n):
+            nc.tensor.matmul_mx(
+                acc, lhsT=w1_codes[:, P * t : P * (t + 1)].bitcast(FP8X4), lhsT_scale=w1_scales[:, P * t : P * (t + 1)],
+                rhs=xw[:, j0 : j0 + n].bitcast(FP8X4), rhs_scale=xs[:, j0 : j0 + n], start=True, stop=True,
             )
 
-        def pair_sums(engine, t, j0, n):
-            pairs = lined_up(t, j0, n).rearrange("p (v e) -> p v e", e=2)
-            engine.tensor_tensor(p[t][:, j0 // 2 : (j0 + n) // 2], pairs[:, :, 0], pairs[:, :, 1], ALU.add)
+        def product_into_y(copy, t, j0, n):
+            acc = psum.tile([P, n], F32, name="acc", tag="bank")
+            first_product(acc[:], t, j0, n)
+            copy(y[t][:, j0 : j0 + n], acc[:])
 
-        def pair_sums_turned(t, j0):
-            pairs = s[t][j0 // V].rearrange("p (v e) -> p v e", e=2)
-            turned = psum.tile([P, 2, P], F32, name="turned", tag="bank")
-            for b in range(2):
-                for e in range(2):
-                    nc.tensor.matmul(
-                        turned[:, b, :], lhsT=pairs[:, b * P : (b + 1) * P, e], rhs=ident[:], is_transpose=True, start=(e == 0), stop=(e == 1)
-                    )
-            turned_sb = keep.tile([P, 2, P], F32, name=f"turned_sb{t}_{j0}", align_bytes=64)
-            nc.scalar.copy(turned_sb[:], turned[:])
-            back = psum.tile([P, 2, P], F32, name="back", tag="bank")
-            for b in range(2):
-                nc.tensor.transpose(back[:, b, :], turned_sb[:, b, :], ident[:])
-            nc.scalar.copy(p[t][:, j0 // 2 : (j0 + V) // 2], back[:].rearrange("p b v -> p (b v)"))
+        on_scalar, on_vector = nc.scalar.copy, nc.vector.tensor_copy
+        early = psum.tile([P, HALF], F32, name="early", tag="bank")
+        for k in range(2):
+            product_into_y(on_scalar, 0, word_starts[k], WORD_PIECES[k])
+            first_product(early[:, word_starts[k] : word_starts[k + 1]], 1, word_starts[k], WORD_PIECES[k])
+        on_scalar(y[1][:, 0:HALF], early[:])
+        product_into_y(on_scalar, 0, word_starts[2], WORD_PIECES[2])
+        product_into_y(on_scalar, 2, 0, HALF)
+        for k in (3, 4):
+            product_into_y(on_vector, 0, word_starts[k], WORD_PIECES[k])
 
-        last_piece = (V, V)
-        for t in range(PACK):
-            if t in WHOLE_PLANES:
-                nc.vector.tensor_scalar(s_whole[t], y[t][:].indirect(order_t[:]), 0.5, 0.0, ALU.mult, ALU.add)
-            for j0, n in ((0, V // 2), (V // 2, V // 2), last_piece) if t == PACK - 1 else ((0, V), last_piece):
-                if t not in WHOLE_PLANES:
-                    line_up(t, j0, n)
-                if (t, j0) in TURNED:
-                    pair_sums_turned(t, j0)
-                elif (t, j0) != (PACK - 1, last_piece[0]):
-                    pair_sums(nc.gpsimd, t, j0, n)
+        means = [keep.tile([P, V + S if t < 2 else V], F32, name=f"means{t}", align_bytes=64) for t in range(PACK)]
+        lined = [means[0][:, V : V + S], means[1][:, V : V + S]]
+        lined = lined + [keep.tile([P, S], F32, name=f"lined{t}", align_bytes=64)[:] for t in (2, 3)]
+        u = keep.tile([P, 7, HALF], F32, name="u", align_bytes=64)
+
+        def u_rows(h):
+            return u[:, 3:7, :] if h == 0 else u[:, 0:4, :]
+
+        def line_up_on_vector(t, h):
+            nc.vector.tensor_scalar(
+                lined[t][:, h * HALF : (h + 1) * HALF], y[t][:].indirect(entries(order_t, h * HALF, HALF)), 0.5, 0.0, ALU.mult, ALU.add
+            )
+
+        def line_up_on_scalar(t, h):
+            nc.scalar.activation(lined[t][:, h * HALF : (h + 1) * HALF], y[t][:].indirect(entries(order_t, h * HALF, HALF)), ACT.Copy, scale=0.5)
+
+        def pair_sums(t, j0, n):
+            pairs = lined[t][:, j0 : j0 + n].rearrange("p (v e) -> p v e", e=2)
+            nc.vector.tensor_tensor(means[t][:, j0 // 2 : (j0 + n) // 2], pairs[:, :, 0], pairs[:, :, 1], ALU.add)
+
+        def difference(t, j0, n):
+            nc.vector.tensor_tensor(
+                u_rows(j0 // HALF)[:, t, j0 % HALF : j0 % HALF + n], means[t][:].indirect(entries(bucket_t, j0, n)),
+                y[t][:, j0 : j0 + n], ALU.subtract,
+            )
+
+        line_up_on_vector(0, 0)
+        line_up_on_scalar(0, 1)
+        product_into_y(on_vector, 1, HALF, HALF)
+        product_into_y(on_scalar, 2, HALF, HALF)
+        line_up_on_scalar(1, 0)
+        line_up_on_scalar(1, 1)
+        product_into_y(on_scalar, 3, 0, HALF)
+        line_up_on_scalar(2, 0)
+        product_into_y(on_scalar, 3, HALF, HALF)
+        line_up_on_scalar(2, 1)
+        line_up_on_scalar(3, 0)
+        line_up_on_scalar(3, 1)
+        for t in range(2):
+            pair_sums(t, 0, S)
+            for h in range(2):
+                difference(t, h * HALF, HALF)
+        pair_sums(2, 0, S)
+        for c in range(2):
+            difference(2, c * CHUNKS[0], CHUNKS[0])
+        pair_sums(3, 0, HALF)
+        difference(2, HALF, CHUNKS[2])
+        pair_sums(3, HALF, HALF)
 
         out_rows = out_0.rearrange("(p t) j -> p t j", t=PACK)
         out_words = out_1[0].rearrange("p c r -> p (c r)").bitcast(I32)
         o_scales = keep.tile([P, S], U8, name="o_scales", align_bytes=64)
+        o_codes = keep.tile([P, S], I32, name="o_codes", align_bytes=64)
         last = len(CHUNKS) - 1
         starts = [sum(CHUNKS[:c]) for c in range(len(CHUNKS))]
-        u = [ring.tile([P, PACK, n], F32, name=f"u{c}", align_bytes=64, offset=(0, 4096)[c % 2]) for c, n in enumerate(CHUNKS)]
-        z_bf = [keep.tile([P, PACK * n], BF16, name=f"z_bf{c}", tag=f"z_bf{c}", align_bytes=64) for c, n in enumerate(CHUNKS)]
+        z_bf = [keep.tile([P, PACK * n], BF16, name=f"z_bf{c}", align_bytes=64) for c, n in enumerate(CHUNKS)]
         z_codes = [keep.tile([P, n], U32, name=f"z_codes{c}", align_bytes=64) for c, n in enumerate(CHUNKS)]
         z_scales = [keep.tile([P, n], U8, name=f"z_scales{c}", align_bytes=64) for c, n in enumerate(CHUNKS)]
         o_f32 = [keep.tile([P, PACK, n], F32, name=f"o_f32{c}", align_bytes=64)[:] for c, n in enumerate(CHUNKS[: last - 1])]
-        o_short = keep.tile([P, PACK, 2 * STRIP], F32, name="o_short", align_bytes=64)
-        o_f32 = o_f32 + [o_short[:, :, 0:STRIP], o_short[:, :, STRIP : 2 * STRIP]]
-        o_bf = [
-            ring.tile([P, PACK * STRIP * len(g)], BF16, name=f"o_bf{g[0]}", align_bytes=64, offset=4096) if i in (0,)
-            else keep.tile([P, PACK * STRIP * len(g)], BF16, name=f"o_bf{g[0]}", tag=f"z_bf{last - 1}" if i == 1 else f"o_bf{i}", align_bytes=64)
-            for i, g in enumerate(WORD_GROUPS)
-        ]
-        o_codes = keep.tile([P, S], I32, name="o_codes", tag=f"z_bf{last}", align_bytes=64)
+        short = CHUNKS[last]
+        o_short = keep.tile([P, PACK, 2 * short], F32, name="o_short", align_bytes=64)
+        o_f32 = o_f32 + [o_short[:, :, 0:short], o_short[:, :, short : 2 * short]]
+        o_bf = [keep.tile([P, PACK * n], BF16, name=f"o_bf{c}", align_bytes=64) for c, n in enumerate(CHUNKS)]
 
         def woven(ap):
             return ap.rearrange("p (g i t) -> p g t i", i=RUN, t=PACK)
@@ -195,71 +184,75 @@ def tile_picked_lshmean_silu_po_kernel(
         def planes(ap):
             return ap.rearrange("p t (g i) -> p g t i", i=RUN)
 
-        def differences(c):
+        def silu(c):
             j0, n = starts[c], CHUNKS[c]
-            for t in range(PACK):
-                nc.vector.tensor_tensor(
-                    u[c][:, t, :], p[t][:].indirect(bucket_t[:, j0 // 16 : (j0 + n) // 16]), y[t][:, j0 : j0 + n], ALU.subtract
+            nc.scalar.activation(woven(z_bf[c][:]), planes(u_rows(j0 // HALF)[:, :, j0 % HALF : j0 % HALF + n]), ACT.Silu, scale=-1.0)
+
+        def quantise_z(c):
+            nc.vector.quantize_mx(z_codes[c][:].bitcast(FP8X4), z_scales[c][:], z_bf[c][:])
+
+        def second_product(c, t0, copy):
+            j0, n = starts[c], CHUNKS[c]
+            res = psum.tile([P, 2, n], F32, name="res", tag="bank")
+            for t in (t0, t0 + 1):
+                nc.tensor.matmul_mx(
+                    res[:, t - t0, :], lhsT=w2w[:, 2 * P * t : 2 * P * (t + 1)].bitcast(FP4X4), lhsT_scale=w2s[:, P * t : P * (t + 1)],
+                    rhs=z_codes[c][:].bitcast(FP8X4), rhs_scale=z_scales[c][:], start=True, stop=True,
                 )
-                if c == 0 and t == 0:
-                    pair_sums(nc.vector, PACK - 1, *last_piece)
-            nc.scalar.activation(woven(z_bf[c][:]), planes(u[c][:]), ACT.Silu, scale=-1.0)
+            copy(o_f32[c][:, t0 : t0 + 2, :], res[:])
+            if c < last - 1:
+                nc.sync.dma_start(out_rows[:, t0 : t0 + 2, j0 : j0 + n], o_f32[c][:, t0 : t0 + 2, :])
+            elif c == last:
+                nc.sync.dma_start(out_rows[:, t0 : t0 + 2, starts[last - 1] : S], o_short[:, t0 : t0 + 2, :])
 
-        def second_product(c, halves=(0, 2)):
-            j0, n = starts[c], CHUNKS[c]
-            if 0 in halves:
-                nc.vector.quantize_mx(z_codes[c][:].bitcast(FP8X4), z_scales[c][:], z_bf[c][:])
-            for t0 in halves:
-                res = psum.tile([P, 2, n], F32, name="res", tag="bank")
-                for t in (t0, t0 + 1):
-                    nc.tensor.matmul_mx(
-                        res[:, t - t0, :], lhsT=w2w[:, 2 * P * t : 2 * P * (t + 1)].bitcast(FP4X4), lhsT_scale=w2s[:, P * t : P * (t + 1)],
-                        rhs=z_codes[c][:].bitcast(FP8X4), rhs_scale=z_scales[c][:], start=True, stop=True,
-                    )
-                nc.scalar.copy(o_f32[c][:, t0 : t0 + 2, :], res[:])
-                if c < last - 1:
-                    nc.sync.dma_start(out_rows[:, t0 : t0 + 2, j0 : j0 + n], o_f32[c][:, t0 : t0 + 2, :])
-                elif c == last:
-                    nc.sync.dma_start(out_rows[:, t0 : t0 + 2, starts[last - 1] : S], o_short[:, t0 : t0 + 2, :])
+        def round_out(c):
+            nc.vector.tensor_copy(woven(o_bf[c][:]), planes(o_f32[c]))
 
-        def round_out(i):
-            g = WORD_GROUPS[i]
-            c = max(k for k in range(last + 1) if starts[k] <= g[0] * STRIP)
-            if c == last:
-                nc.scalar.copy(woven(o_bf[i][:]), planes(o_f32[c]))
-            else:
-                nc.vector.tensor_copy(woven(o_bf[i][:]), planes(o_f32[c]))
-
-        def hand_on(i):
-            g = WORD_GROUPS[i]
-            cols = slice(g[0] * STRIP, (g[-1] + 1) * STRIP)
-            nc.vector.quantize_mx(o_codes[:, cols].bitcast(FP8X4), o_scales[:, cols], o_bf[i][:])
-            if cols.stop in WORD_STORE_ENDS:
-                k = WORD_STORE_ENDS.index(cols.stop)
-                stored = slice(WORD_STORE_ENDS[k - 1] if k else 0, cols.stop)
+        def hand_on(c):
+            cols = slice(starts[c], starts[c] + CHUNKS[c])
+            nc.vector.quantize_mx(o_codes[:, cols].bitcast(FP8X4), o_scales[:, cols], o_bf[c][:])
+            if cols.stop % HALF == 0:
+                stored = slice(cols.stop - HALF, cols.stop)
                 nc.sync.dma_start(out_words[:, stored], o_codes[:, stored])
 
-        def store_scales(cols):
-            for r in range(4):
-                nc.sync.dma_start(out_2[0, r:16:4, cols].bitcast(I32), o_scales[r:P:32, cols].bitcast(I32))
+        def last_difference(c):
+            difference(PACK - 1, starts[c], CHUNKS[c])
 
-        differences(0)
-        differences(1)
-        second_product(0)
-        differences(2)
-        for c in (last - 1, last):
-            second_product(c - 2, (0,))
-            differences(c)
-            second_product(c - 2, (2,))
-        second_product(last - 1)
-        second_product(last)
+        for c in range(2):
+            last_difference(c)
+            silu(c)
+        for c in (3, 4):
+            difference(2, starts[c], CHUNKS[c])
+        quantise_z(0)
+        last_difference(2)
+        second_product(0, 0, on_scalar)
+        second_product(0, 2, on_scalar)
+        silu(2)
+        quantise_z(1)
+        last_difference(3)
+        last_difference(4)
         round_out(0)
-        round_out(1)
+        second_product(1, 0, on_scalar)
+        second_product(1, 2, on_vector)
+        silu(3)
+        quantise_z(2)
         hand_on(0)
+        silu(4)
+        quantise_z(3)
+        round_out(1)
+        quantise_z(4)
         hand_on(1)
+        second_product(2, 0, on_scalar)
+        second_product(2, 2, on_scalar)
+        second_product(3, 0, on_scalar)
+        second_product(3, 2, on_scalar)
+        second_product(4, 0, on_scalar)
+        second_product(4, 2, on_scalar)
         round_out(2)
-        for i in range(2, len(WORD_GROUPS)):
-            if i + 1 < len(WORD_GROUPS):
-                round_out(i + 1)
-            hand_on(i)
-        store_scales(slice(0, S))
+        round_out(3)
+        hand_on(2)
+        round_out(4)
+        hand_on(3)
+        hand_on(4)
+        for r in range(4):
+            nc.sync.dma_start(out_2[0, r:16:4, :].bitcast(I32), o_scales[r:P:32, :].bitcast(I32))

@@ -18,10 +18,11 @@ FLOPS = 2 * K * H * S + 2 * H * N * S
 P = 128
 PACK = 4
 HALF = S // 2
-W1_ON_SCALAR = 56
+W1_ON_SCALAR = 44
 WORD_PIECES = (256, 256, 256, 128, 128)
 CHUNKS = (256, 256, 256, 128, 128)
 RUN = 2
+BANK_BYTES = 2048
 
 
 def tile_picked_lshmean_silu_po_kernel(
@@ -32,7 +33,10 @@ def tile_picked_lshmean_silu_po_kernel(
         lists = ctx.enter_context(tc.tile_pool(name="lists", bufs=1))
         keep = ctx.enter_context(tc.tile_pool(name="keep", bufs=1))
         reuse = ctx.enter_context(tc.tile_pool(name="reuse", bufs=1))
-        psum = ctx.enter_context(tc.psum_pool(name="psum", bufs=8))
+        turns = ctx.enter_context(tc.tile_pool(name="turns", bufs=1))
+        ring = ctx.enter_context(tc.tile_pool(name="ring", bufs=1))
+        late = ctx.enter_context(tc.tile_pool(name="late", bufs=1))
+        psum = ctx.enter_context(tc.psum_pool(name="psum", bufs=1))
 
         offs_t = lists.tile([P, S // 16], U16, name="offs_t")
         order_t = lists.tile([P, S // 16], U16, name="order_t")
@@ -43,20 +47,31 @@ def tile_picked_lshmean_silu_po_kernel(
 
         xs_all = reuse.tile([P, T], U8, name="xs_all", align_bytes=64, offset=0)
         xw_all = keep.tile([P, T], I32, name="xw_all", align_bytes=64)
-        w2s_raw = reuse.tile([P, N], U8, name="w2s_raw", align_bytes=64, offset=2 * N)
-        w2w_raw = reuse.tile([P, 2 * N], U8, name="w2w_raw", align_bytes=64, offset=0)
-        w1_raw = keep.tile([P, PACK, H], F32, name="w1_raw", align_bytes=64)
+        w2s_raw = keep.tile([P, N], U8, name="w2s_raw", align_bytes=64)
+        w2s_dealt = keep.tile([P, N], U8, name="w2s_dealt", align_bytes=64)
+        w2s = reuse.tile([P, N], U8, name="w2s", align_bytes=64, offset=0)
+        w2w_raw = keep.tile([P, 2 * N], U8, name="w2w_raw", align_bytes=64)
+        w1_raw = turns.tile([P, PACK, H], F32, name="w1_raw", align_bytes=64, offset=0)
 
         xs = keep.tile([P, S], U8, name="xs", align_bytes=64)
         nc.vector.memset(xs_all[0:16, :].bitcast(I32), 0)
-        nc.gpsimd.memset(xs_all[32:64, :].bitcast(I32), 0)
-        nc.gpsimd.memset(xs_all[64:P, :].bitcast(I32), 0)
+        nc.vector.memset(xs_all[32:64, :].bitcast(I32), 0)
+        nc.vector.memset(xs_all[64:P, :].bitcast(I32), 0)
         nc.vector.memset(xs[:].bitcast(I32), 0)
+        nc.vector.memset(w2s_raw[0:16, :].bitcast(I32), 0)
+        nc.vector.memset(w2s_raw[32:64, :].bitcast(I32), 0)
+        nc.vector.memset(w2s_raw[64:P, :].bitcast(I32), 0)
+
+        warm = keep.tile([P, 16], F32, name="warm", align_bytes=64)
+        nc.gpsimd.memset(warm[:, 0:1], 0.0)
+        nc.scalar.activation(warm[:, 8:9], warm[:, 0:1], ACT.Silu)
 
         nc.sync.dma_start(offs_t[:], offs)
         nc.sync.dma_start(xs_all[16:32, :].bitcast(I32), x_scales[0].bitcast(I32))
+        nc.sync.dma_start(w2s_raw[16:32, :].bitcast(I32), w2_scales[0].bitcast(I32))
         nc.sync.dma_start(w1_raw[:], w1.rearrange("(p j) c -> p j c", j=PACK))
         nc.sync.dma_start(xw_all[:], x_words[0].rearrange("p c r -> p (c r)").bitcast(I32))
+        nc.sync.dma_start(w2w_raw[:].bitcast(I32), w2_words[0].bitcast(I32))
         nc.sync.dma_start(order_t[:], order)
         nc.sync.dma_start(bucket_t[:], bucket)
 
@@ -64,10 +79,7 @@ def tile_picked_lshmean_silu_po_kernel(
         nc.vector.tensor_copy(xs_picked[:], xs_all[:].indirect(offs_t[:]))
         for r in range(4):
             nc.sync.dma_start(xs[r:P:32, :].bitcast(I32), xs_picked[16 + r : 32 : 4, :].bitcast(I32))
-        nc.sync.dma_start(w2w_raw[:].bitcast(I32), w2_words[0].bitcast(I32))
-        nc.gpsimd.memset(w2s_raw[:].bitcast(I32), 0)
-        for r in range(4):
-            nc.sync.dma_start(w2s_raw[r:P:32, :].bitcast(I32), w2_scales[0, r:16:4, :].bitcast(I32))
+        nc.gpsimd.tensor_copy(w2s_dealt[:].rearrange("p (t m) -> p t m", t=PACK), w2s_raw[:].rearrange("p (m t) -> p t m", t=PACK))
 
         w1_src = w1_raw[:].rearrange("p j (m t) -> p m j t", t=PACK)
         w1_bf = keep.tile([P, PACK * H], BF16, name="w1_bf", tag="w1_bf", align_bytes=64)
@@ -84,13 +96,14 @@ def tile_picked_lshmean_silu_po_kernel(
             nc.vector.tensor_copy(xw[:, j0 : j0 + n], xw_all[:].bitcast(U32).indirect(entries(offs_t, j0, n)))
 
         w2w = keep.tile([P, 2 * N], U8, name="w2w", align_bytes=64)
-        w2s = keep.tile([P, N], U8, name="w2s", align_bytes=64)
-        nc.gpsimd.tensor_copy(
-            w2w[:].rearrange("p (t m b) -> p t m b", t=PACK, b=2), w2w_raw[:].rearrange("p (m t b) -> p t m b", t=PACK, b=2)
-        )
-        nc.gpsimd.tensor_copy(w2s[:].rearrange("p (t m) -> p t m", t=PACK), w2s_raw[:].rearrange("p (m t) -> p t m", t=PACK))
+        nc.scalar.copy(w2w[:].bitcast(U16).rearrange("p (t m) -> p t m", t=PACK), w2w_raw[:].bitcast(U16).rearrange("p (m t) -> p t m", t=PACK))
+
+        nc.gpsimd.memset(w2s[:].bitcast(I32), 0)
+        for r in range(4):
+            nc.sync.dma_start(w2s[r:P:32, :].bitcast(I32), w2s_dealt[16 + r : 32 : 4, :].bitcast(I32))
 
         y = [keep.tile([P, S], F32, name=f"y{t}", align_bytes=64) for t in range(PACK)]
+        first, second, third, fourth = 1, 2, 0, 3
 
         def first_product(acc, t, j0, n):
             nc.tensor.matmul_mx(
@@ -98,70 +111,85 @@ def tile_picked_lshmean_silu_po_kernel(
                 rhs=xw[:, j0 : j0 + n].bitcast(FP8X4), rhs_scale=xs[:, j0 : j0 + n], start=True, stop=True,
             )
 
-        def product_into_y(copy, t, j0, n):
-            acc = psum.tile([P, n], F32, name="acc", tag="bank")
+        def product_into_y(copy, t, j0, n, bank):
+            acc = psum.tile([P, n], F32, name=f"acc{t}_{j0}", offset=bank * BANK_BYTES)
             first_product(acc[:], t, j0, n)
             copy(y[t][:, j0 : j0 + n], acc[:])
 
         on_scalar, on_vector = nc.scalar.copy, nc.vector.tensor_copy
-        early = psum.tile([P, HALF], F32, name="early", tag="bank")
+        quarter = S // 4
         for k in range(2):
-            product_into_y(on_scalar, 0, word_starts[k], WORD_PIECES[k])
-            first_product(early[:, word_starts[k] : word_starts[k + 1]], 1, word_starts[k], WORD_PIECES[k])
-        on_scalar(y[1][:, 0:HALF], early[:])
-        product_into_y(on_scalar, 0, word_starts[2], WORD_PIECES[2])
-        product_into_y(on_scalar, 2, 0, HALF)
+            product_into_y(on_scalar, first, word_starts[k], WORD_PIECES[k], k)
+        both = psum.tile([P, 2, HALF], F32, name="both", offset=2 * BANK_BYTES)
+        first_product(both[:, 0, 0:quarter], second, 0, quarter)
+        first_product(both[:, 1, 0:quarter], first, HALF, quarter)
+        on_scalar(y[first][:, HALF : HALF + quarter], both[:, 1, 0:quarter])
         for k in (3, 4):
-            product_into_y(on_vector, 0, word_starts[k], WORD_PIECES[k])
+            product_into_y(on_vector, first, word_starts[k], WORD_PIECES[k], k + 1)
+        on_scalar(y[second][:, 0:quarter], both[:, 0, 0:quarter])
+        product_into_y(on_scalar, second, S - quarter, quarter, 6)
 
-        means = [keep.tile([P, V + S if t < 2 else V], F32, name=f"means{t}", align_bytes=64) for t in range(PACK)]
-        lined = [means[0][:, V : V + S], means[1][:, V : V + S]]
-        lined = lined + [keep.tile([P, S], F32, name=f"lined{t}", align_bytes=64)[:] for t in (2, 3)]
-        u = keep.tile([P, 7, HALF], F32, name="u", align_bytes=64)
+        means = {
+            first: turns.tile([P, S], F32, name="means_first", align_bytes=64, offset=0),
+            second: turns.tile([P, S], F32, name="means_second", align_bytes=64, offset=4 * S),
+            third: keep.tile([P, V], F32, name="means_third", align_bytes=64),
+            fourth: turns.tile([P, V], F32, name="means_fourth", align_bytes=64, offset=8 * S),
+        }
+        whole = {
+            first: keep.tile([P, S], F32, name="lined_first", align_bytes=64),
+            second: turns.tile([P, S], F32, name="lined_second", align_bytes=64, offset=8 * S),
+            fourth: ring.tile([P, S], F32, name="lined_fourth", align_bytes=64, offset=4 * S),
+        }
+        third_late = keep.tile([P, HALF], F32, name="third_late", align_bytes=64)
+        lined = {t: [whole[t][:, 0:HALF], whole[t][:, HALF:S]] for t in whole}
+        lined[third] = [means[first][:, V:S], third_late[:]]
+        u = [ring.tile([P, PACK, quarter], F32, name=f"u{q}", align_bytes=64, offset=q % 2 * 4 * S) for q in range(4)]
 
-        def u_rows(h):
-            return u[:, 3:7, :] if h == 0 else u[:, 0:4, :]
+        def u_block(j0, n):
+            return u[j0 // quarter][:, :, j0 % quarter : j0 % quarter + n]
 
         def line_up_on_vector(t, h):
             nc.vector.tensor_scalar(
-                lined[t][:, h * HALF : (h + 1) * HALF], y[t][:].indirect(entries(order_t, h * HALF, HALF)), 0.5, 0.0, ALU.mult, ALU.add
+                lined[t][h], y[t][:].indirect(entries(order_t, h * HALF, HALF)), 0.5, 0.0, ALU.mult, ALU.add
             )
 
         def line_up_on_scalar(t, h):
-            nc.scalar.activation(lined[t][:, h * HALF : (h + 1) * HALF], y[t][:].indirect(entries(order_t, h * HALF, HALF)), ACT.Copy, scale=0.5)
+            nc.scalar.activation(lined[t][h], y[t][:].indirect(entries(order_t, h * HALF, HALF)), ACT.Copy, scale=0.5)
 
-        def pair_sums(t, j0, n):
-            pairs = lined[t][:, j0 : j0 + n].rearrange("p (v e) -> p v e", e=2)
-            nc.vector.tensor_tensor(means[t][:, j0 // 2 : (j0 + n) // 2], pairs[:, :, 0], pairs[:, :, 1], ALU.add)
+        def pair_sums(engine, t, values, v0):
+            pairs = values.rearrange("p (v e) -> p v e", e=2)
+            engine.tensor_tensor(means[t][:, v0 : v0 + pairs.shape[1]], pairs[:, :, 0], pairs[:, :, 1], ALU.add)
 
         def difference(t, j0, n):
             nc.vector.tensor_tensor(
-                u_rows(j0 // HALF)[:, t, j0 % HALF : j0 % HALF + n], means[t][:].indirect(entries(bucket_t, j0, n)),
+                u_block(j0, n)[:, t, :], means[t][:].indirect(entries(bucket_t, j0, n)),
                 y[t][:, j0 : j0 + n], ALU.subtract,
             )
 
-        line_up_on_vector(0, 0)
-        line_up_on_scalar(0, 1)
-        product_into_y(on_vector, 1, HALF, HALF)
-        product_into_y(on_scalar, 2, HALF, HALF)
-        line_up_on_scalar(1, 0)
-        line_up_on_scalar(1, 1)
-        product_into_y(on_scalar, 3, 0, HALF)
-        line_up_on_scalar(2, 0)
-        product_into_y(on_scalar, 3, HALF, HALF)
-        line_up_on_scalar(2, 1)
-        line_up_on_scalar(3, 0)
-        line_up_on_scalar(3, 1)
-        for t in range(2):
-            pair_sums(t, 0, S)
-            for h in range(2):
-                difference(t, h * HALF, HALF)
-        pair_sums(2, 0, S)
-        for c in range(2):
-            difference(2, c * CHUNKS[0], CHUNKS[0])
-        pair_sums(3, 0, HALF)
-        difference(2, HALF, CHUNKS[2])
-        pair_sums(3, HALF, HALF)
+        line_up_on_vector(first, 0)
+        line_up_on_scalar(first, 1)
+        pair_sums(nc.gpsimd, first, whole[first][:], 0)
+        product_into_y(on_vector, second, quarter, HALF, 2)
+        product_into_y(on_vector, third, 0, HALF, 3)
+        product_into_y(on_scalar, fourth, 0, HALF, 7)
+        product_into_y(on_vector, third, HALF, HALF, 6)
+        for h in range(2):
+            line_up_on_scalar(second, h)
+        pair_sums(nc.gpsimd, second, whole[second][:], 0)
+        difference(first, 0, quarter)
+        line_up_on_vector(third, 0)
+        product_into_y(on_vector, fourth, HALF, HALF, 3)
+        line_up_on_scalar(third, 1)
+        for h in range(2):
+            line_up_on_scalar(fourth, h)
+        for h in range(2):
+            pair_sums(nc.vector, third, lined[third][h], h * V // 2)
+        difference(second, 0, quarter)
+        difference(third, 0, quarter)
+        pair_sums(nc.vector, fourth, whole[fourth][:], 0)
+        fetched = keep.tile([P, HALF], F32, name="fetched", align_bytes=64)
+        for j0 in (0, quarter):
+            nc.scalar.activation(fetched[:, j0 : j0 + quarter], means[third][:].indirect(entries(bucket_t, HALF + j0, quarter)), ACT.Copy)
 
         out_rows = out_0.rearrange("(p t) j -> p t j", t=PACK)
         out_words = out_1[0].rearrange("p c r -> p (c r)").bitcast(I32)
@@ -169,14 +197,18 @@ def tile_picked_lshmean_silu_po_kernel(
         o_codes = keep.tile([P, S], I32, name="o_codes", align_bytes=64)
         last = len(CHUNKS) - 1
         starts = [sum(CHUNKS[:c]) for c in range(len(CHUNKS))]
-        z_bf = [keep.tile([P, PACK * n], BF16, name=f"z_bf{c}", align_bytes=64) for c, n in enumerate(CHUNKS)]
-        z_codes = [keep.tile([P, n], U32, name=f"z_codes{c}", align_bytes=64) for c, n in enumerate(CHUNKS)]
+        z_bf = [keep.tile([P, PACK * n], BF16, name=f"z_bf{c}", align_bytes=64) for c, n in enumerate(CHUNKS[:2])]
+        z_bf = z_bf + [late.tile([P, PACK * CHUNKS[c]], BF16, name=f"z_bf{c}", align_bytes=64, offset=2048 * (c - 2)) for c in (2, 3, 4)]
+        z_codes = [late.tile([P, n], U32, name=f"z_codes{c}", align_bytes=64, offset=2048 * c) for c, n in enumerate(CHUNKS[:2])]
+        z_codes = z_codes + [keep.tile([P, CHUNKS[c]], U32, name=f"z_codes{c}", align_bytes=64) for c in (2, 3, 4)]
         z_scales = [keep.tile([P, n], U8, name=f"z_scales{c}", align_bytes=64) for c, n in enumerate(CHUNKS)]
+        z_scales[1] = late.tile([P, CHUNKS[1]], U8, name="z_scales_second", align_bytes=64, offset=4096)
         o_f32 = [keep.tile([P, PACK, n], F32, name=f"o_f32{c}", align_bytes=64)[:] for c, n in enumerate(CHUNKS[: last - 1])]
         short = CHUNKS[last]
         o_short = keep.tile([P, PACK, 2 * short], F32, name="o_short", align_bytes=64)
         o_f32 = o_f32 + [o_short[:, :, 0:short], o_short[:, :, short : 2 * short]]
-        o_bf = [keep.tile([P, PACK * n], BF16, name=f"o_bf{c}", align_bytes=64) for c, n in enumerate(CHUNKS)]
+        o_bf = [ring.tile([P, PACK * CHUNKS[0]], BF16, name="o_bf0", align_bytes=64, offset=0)]
+        o_bf = o_bf + [keep.tile([P, PACK * CHUNKS[c]], BF16, name=f"o_bf{c}", align_bytes=64) for c in range(1, len(CHUNKS))]
 
         def woven(ap):
             return ap.rearrange("p (g i t) -> p g t i", i=RUN, t=PACK)
@@ -186,14 +218,14 @@ def tile_picked_lshmean_silu_po_kernel(
 
         def silu(c):
             j0, n = starts[c], CHUNKS[c]
-            nc.scalar.activation(woven(z_bf[c][:]), planes(u_rows(j0 // HALF)[:, :, j0 % HALF : j0 % HALF + n]), ACT.Silu, scale=-1.0)
+            nc.scalar.activation(woven(z_bf[c][:]), planes(u_block(j0, n)), ACT.Silu, scale=-1.0)
 
         def quantise_z(c):
             nc.vector.quantize_mx(z_codes[c][:].bitcast(FP8X4), z_scales[c][:], z_bf[c][:])
 
         def second_product(c, t0, copy):
             j0, n = starts[c], CHUNKS[c]
-            res = psum.tile([P, 2, n], F32, name="res", tag="bank")
+            res = psum.tile([P, 2, n], F32, name=f"res{c}_{t0}", offset=(2 * c + t0 // 2) % 8 * BANK_BYTES)
             for t in (t0, t0 + 1):
                 nc.tensor.matmul_mx(
                     res[:, t - t0, :], lhsT=w2w[:, 2 * P * t : 2 * P * (t + 1)].bitcast(FP4X4), lhsT_scale=w2s[:, P * t : P * (t + 1)],
@@ -216,31 +248,40 @@ def tile_picked_lshmean_silu_po_kernel(
                 nc.sync.dma_start(out_words[:, stored], o_codes[:, stored])
 
         def last_difference(c):
-            difference(PACK - 1, starts[c], CHUNKS[c])
+            difference(fourth, starts[c], CHUNKS[c])
 
-        for c in range(2):
-            last_difference(c)
-            silu(c)
-        for c in (3, 4):
-            difference(2, starts[c], CHUNKS[c])
+        def fetched_difference(j0):
+            nc.vector.tensor_tensor(u_block(j0, quarter)[:, third, :], fetched[:, j0 - HALF : j0 - HALF + quarter], y[third][:, j0 : j0 + quarter], ALU.subtract)
+
+        last_difference(0)
+        silu(0)
+        for t in (first, third, second, fourth):
+            difference(t, quarter, quarter)
+        silu(1)
         quantise_z(0)
+        fetched_difference(HALF)
+        for t in (first, second):
+            difference(t, HALF, quarter)
+        quantise_z(1)
         last_difference(2)
         second_product(0, 0, on_scalar)
         second_product(0, 2, on_scalar)
         silu(2)
-        quantise_z(1)
+        fetched_difference(S - quarter)
+        for t in (first, second):
+            difference(t, S - quarter, quarter)
+        quantise_z(2)
         last_difference(3)
         last_difference(4)
-        round_out(0)
         second_product(1, 0, on_scalar)
-        second_product(1, 2, on_vector)
+        second_product(1, 2, on_scalar)
         silu(3)
-        quantise_z(2)
-        hand_on(0)
         silu(4)
+        round_out(0)
         quantise_z(3)
         round_out(1)
         quantise_z(4)
+        hand_on(0)
         hand_on(1)
         second_product(2, 0, on_scalar)
         second_product(2, 2, on_scalar)

@@ -130,19 +130,18 @@ def tile_picked_lshmean_silu_po_kernel(
         product_into_y(on_scalar, second, S - quarter, quarter, 6)
 
         means = {
-            first: turns.tile([P, S], F32, name="means_first", align_bytes=64, offset=0),
-            second: turns.tile([P, S], F32, name="means_second", align_bytes=64, offset=4 * S),
+            first: keep.tile([P, V], F32, name="means_first", align_bytes=64),
+            second: keep.tile([P, V], F32, name="means_second", align_bytes=64),
             third: keep.tile([P, V], F32, name="means_third", align_bytes=64),
             fourth: turns.tile([P, V], F32, name="means_fourth", align_bytes=64, offset=8 * S),
         }
         whole = {
             first: keep.tile([P, S], F32, name="lined_first", align_bytes=64),
             second: turns.tile([P, S], F32, name="lined_second", align_bytes=64, offset=8 * S),
+            third: keep.tile([P, S], F32, name="lined_third", align_bytes=64),
             fourth: ring.tile([P, S], F32, name="lined_fourth", align_bytes=64, offset=4 * S),
         }
-        third_late = keep.tile([P, HALF], F32, name="third_late", align_bytes=64)
         lined = {t: [whole[t][:, 0:HALF], whole[t][:, HALF:S]] for t in whole}
-        lined[third] = [means[first][:, V:S], third_late[:]]
         u = [ring.tile([P, PACK, quarter], F32, name=f"u{q}", align_bytes=64, offset=q % 2 * 4 * S) for q in range(4)]
 
         def u_block(j0, n):
@@ -168,28 +167,31 @@ def tile_picked_lshmean_silu_po_kernel(
 
         line_up_on_vector(first, 0)
         line_up_on_scalar(first, 1)
-        pair_sums(nc.gpsimd, first, whole[first][:], 0)
         product_into_y(on_vector, second, quarter, HALF, 2)
+        pair_sums(nc.vector, first, whole[first][:], 0)
         product_into_y(on_vector, third, 0, HALF, 3)
         product_into_y(on_scalar, fourth, 0, HALF, 7)
+        difference(first, 0, quarter)
         product_into_y(on_vector, third, HALF, HALF, 6)
         for h in range(2):
             line_up_on_scalar(second, h)
-        pair_sums(nc.gpsimd, second, whole[second][:], 0)
-        difference(first, 0, quarter)
+        product_into_y(on_scalar, fourth, HALF, HALF, 3)
+        pair_sums(nc.vector, second, whole[second][:], 0)
         line_up_on_vector(third, 0)
-        product_into_y(on_vector, fourth, HALF, HALF, 3)
         line_up_on_scalar(third, 1)
         for h in range(2):
             line_up_on_scalar(fourth, h)
-        for h in range(2):
-            pair_sums(nc.vector, third, lined[third][h], h * V // 2)
         difference(second, 0, quarter)
+        pair_sums(nc.vector, third, whole[third][:], 0)
         difference(third, 0, quarter)
         pair_sums(nc.vector, fourth, whole[fourth][:], 0)
-        fetched = keep.tile([P, HALF], F32, name="fetched", align_bytes=64)
-        for j0 in (0, quarter):
-            nc.scalar.activation(fetched[:, j0 : j0 + quarter], means[third][:].indirect(entries(bucket_t, HALF + j0, quarter)), ACT.Copy)
+        def fetch(into, t, j0):
+            nc.scalar.activation(into, means[t][:].indirect(entries(bucket_t, j0, quarter)), ACT.Copy)
+
+        ahead = [(third, j0) for j0 in (quarter, HALF, S - quarter)]
+        fetched = {key: keep.tile([P, quarter], F32, name=f"fetched{i}", align_bytes=64)[:] for i, key in enumerate(ahead)}
+        for t, j0 in ahead:
+            fetch(fetched[t, j0], t, j0)
 
         out_rows = out_0.rearrange("(p t) j -> p t j", t=PACK)
         out_words = out_1[0].rearrange("p c r -> p (c r)").bitcast(I32)
@@ -250,29 +252,33 @@ def tile_picked_lshmean_silu_po_kernel(
         def last_difference(c):
             difference(fourth, starts[c], CHUNKS[c])
 
-        def fetched_difference(j0):
-            nc.vector.tensor_tensor(u_block(j0, quarter)[:, third, :], fetched[:, j0 - HALF : j0 - HALF + quarter], y[third][:, j0 : j0 + quarter], ALU.subtract)
+        def fetched_difference(t, j0):
+            nc.vector.tensor_tensor(u_block(j0, quarter)[:, t, :], fetched[t, j0], y[t][:, j0 : j0 + quarter], ALU.subtract)
 
         last_difference(0)
         silu(0)
-        for t in (first, third, second, fourth):
-            difference(t, quarter, quarter)
+        difference(first, quarter, quarter)
+        fetched_difference(third, quarter)
+        difference(second, quarter, quarter)
+        last_difference(1)
+        fetched[second, HALF] = u_block(HALF, quarter)[:, second, :]
+        fetch(fetched[second, HALF], second, HALF)
         silu(1)
         quantise_z(0)
-        fetched_difference(HALF)
-        for t in (first, second):
-            difference(t, HALF, quarter)
-        quantise_z(1)
+        fetched_difference(third, HALF)
+        difference(first, HALF, quarter)
+        fetched_difference(second, HALF)
         last_difference(2)
+        quantise_z(1)
         second_product(0, 0, on_scalar)
         second_product(0, 2, on_scalar)
         silu(2)
-        fetched_difference(S - quarter)
+        fetched_difference(third, S - quarter)
         for t in (first, second):
             difference(t, S - quarter, quarter)
-        quantise_z(2)
         last_difference(3)
         last_difference(4)
+        quantise_z(2)
         second_product(1, 0, on_scalar)
         second_product(1, 2, on_scalar)
         silu(3)

@@ -102,8 +102,9 @@ def tile_picked_lshmean_silu_po_kernel(
         for r in range(4):
             nc.sync.dma_start(w2s[r:P:32, :].bitcast(I32), w2s_dealt[16 + r : 32 : 4, :].bitcast(I32))
 
-        y = [keep.tile([P, S], F32, name=f"y{t}", align_bytes=64) for t in range(PACK)]
         first, second, third, fourth = 1, 2, 0, 3
+        y = {t: keep.tile([P, S], F32, name=f"y{t}", align_bytes=64) for t in (first, third, fourth)}
+        y[second] = turns.tile([P, S + HALF], F32, name="y_second", align_bytes=64, offset=0)
 
         def first_product(acc, t, j0, n):
             nc.tensor.matmul_mx(
@@ -138,11 +139,12 @@ def tile_picked_lshmean_silu_po_kernel(
         whole = {
             first: keep.tile([P, S], F32, name="lined_first", align_bytes=64),
             second: turns.tile([P, S], F32, name="lined_second", align_bytes=64, offset=8 * S),
-            third: keep.tile([P, S], F32, name="lined_third", align_bytes=64),
-            fourth: ring.tile([P, S], F32, name="lined_fourth", align_bytes=64, offset=4 * S),
+            fourth: ring.tile([P, S], F32, name="lined_fourth", align_bytes=64, offset=8 * S),
         }
+        third_late = keep.tile([P, HALF], F32, name="third_late", align_bytes=64)
         lined = {t: [whole[t][:, 0:HALF], whole[t][:, HALF:S]] for t in whole}
-        u = [ring.tile([P, PACK, quarter], F32, name=f"u{q}", align_bytes=64, offset=q % 2 * 4 * S) for q in range(4)]
+        lined[third] = [y[second][:, S : S + HALF], third_late[:]]
+        u = [ring.tile([P, PACK, quarter], F32, name=f"u{q}", align_bytes=64, offset=q % 3 * 4 * S) for q in range(4)]
 
         def u_block(j0, n):
             return u[j0 // quarter][:, :, j0 % quarter : j0 % quarter + n]
@@ -167,23 +169,26 @@ def tile_picked_lshmean_silu_po_kernel(
 
         line_up_on_vector(first, 0)
         line_up_on_scalar(first, 1)
+        pair_sums(nc.gpsimd, first, whole[first][:], 0)
         product_into_y(on_vector, second, quarter, HALF, 2)
-        pair_sums(nc.vector, first, whole[first][:], 0)
         product_into_y(on_vector, third, 0, HALF, 3)
         product_into_y(on_scalar, fourth, 0, HALF, 7)
-        difference(first, 0, quarter)
         product_into_y(on_vector, third, HALF, HALF, 6)
         for h in range(2):
             line_up_on_scalar(second, h)
-        product_into_y(on_scalar, fourth, HALF, HALF, 3)
-        pair_sums(nc.vector, second, whole[second][:], 0)
+        pair_sums(nc.gpsimd, second, whole[second][:], 0)
+        for j0 in (0, quarter):
+            difference(first, j0, quarter)
+        product_into_y(on_vector, fourth, HALF, HALF, 3)
         line_up_on_vector(third, 0)
         line_up_on_scalar(third, 1)
         for h in range(2):
             line_up_on_scalar(fourth, h)
+        for h in (1, 0):
+            pair_sums(nc.vector, third, lined[third][h], h * V // 2)
         difference(second, 0, quarter)
-        pair_sums(nc.vector, third, whole[third][:], 0)
         difference(third, 0, quarter)
+        difference(second, quarter, quarter)
         pair_sums(nc.vector, fourth, whole[fourth][:], 0)
         def fetch(into, t, j0):
             nc.scalar.activation(into, means[t][:].indirect(entries(bucket_t, j0, quarter)), ACT.Copy)
@@ -199,8 +204,8 @@ def tile_picked_lshmean_silu_po_kernel(
         o_codes = keep.tile([P, S], I32, name="o_codes", align_bytes=64)
         last = len(CHUNKS) - 1
         starts = [sum(CHUNKS[:c]) for c in range(len(CHUNKS))]
-        z_bf = [keep.tile([P, PACK * n], BF16, name=f"z_bf{c}", align_bytes=64) for c, n in enumerate(CHUNKS[:2])]
-        z_bf = z_bf + [late.tile([P, PACK * CHUNKS[c]], BF16, name=f"z_bf{c}", align_bytes=64, offset=2048 * (c - 2)) for c in (2, 3, 4)]
+        z_bf = [keep.tile([P, PACK * n], BF16, name=f"z_bf{c}", align_bytes=64) for c, n in enumerate(CHUNKS[:3])]
+        z_bf = z_bf + [late.tile([P, PACK * CHUNKS[c]], BF16, name=f"z_bf{c}", align_bytes=64, offset=2048 * (c - 2)) for c in (3, 4)]
         z_codes = [late.tile([P, n], U32, name=f"z_codes{c}", align_bytes=64, offset=2048 * c) for c, n in enumerate(CHUNKS[:2])]
         z_codes = z_codes + [keep.tile([P, CHUNKS[c]], U32, name=f"z_codes{c}", align_bytes=64) for c in (2, 3, 4)]
         z_scales = [keep.tile([P, n], U8, name=f"z_scales{c}", align_bytes=64) for c, n in enumerate(CHUNKS)]
@@ -209,7 +214,7 @@ def tile_picked_lshmean_silu_po_kernel(
         short = CHUNKS[last]
         o_short = keep.tile([P, PACK, 2 * short], F32, name="o_short", align_bytes=64)
         o_f32 = o_f32 + [o_short[:, :, 0:short], o_short[:, :, short : 2 * short]]
-        o_bf = [ring.tile([P, PACK * CHUNKS[0]], BF16, name="o_bf0", align_bytes=64, offset=0)]
+        o_bf = [ring.tile([P, PACK * CHUNKS[0]], BF16, name="o_bf0", align_bytes=64, offset=8 * S)]
         o_bf = o_bf + [keep.tile([P, PACK * CHUNKS[c]], BF16, name=f"o_bf{c}", align_bytes=64) for c in range(1, len(CHUNKS))]
 
         def woven(ap):
@@ -257,22 +262,18 @@ def tile_picked_lshmean_silu_po_kernel(
 
         last_difference(0)
         silu(0)
-        difference(first, quarter, quarter)
         fetched_difference(third, quarter)
-        difference(second, quarter, quarter)
         last_difference(1)
-        fetched[second, HALF] = u_block(HALF, quarter)[:, second, :]
-        fetch(fetched[second, HALF], second, HALF)
         silu(1)
+        for t in (first, second):
+            difference(t, HALF, quarter)
         quantise_z(0)
         fetched_difference(third, HALF)
-        difference(first, HALF, quarter)
-        fetched_difference(second, HALF)
         last_difference(2)
         quantise_z(1)
+        silu(2)
         second_product(0, 0, on_scalar)
         second_product(0, 2, on_scalar)
-        silu(2)
         fetched_difference(third, S - quarter)
         for t in (first, second):
             difference(t, S - quarter, quarter)
@@ -290,7 +291,7 @@ def tile_picked_lshmean_silu_po_kernel(
         hand_on(0)
         hand_on(1)
         second_product(2, 0, on_scalar)
-        second_product(2, 2, on_scalar)
+        second_product(2, 2, on_vector)
         second_product(3, 0, on_scalar)
         second_product(3, 2, on_scalar)
         second_product(4, 0, on_scalar)

@@ -22,6 +22,7 @@ W1_ON_SCALAR = 44
 WORD_PIECES = (256, 256, 256, 128, 128)
 CHUNKS = (256, 256, 256, 128, 128)
 RUN = 2
+WORD_STORES = {1: 0, 2: 512, 4: 768}
 BANK_BYTES = 2048
 
 
@@ -36,6 +37,7 @@ def tile_picked_lshmean_silu_po_kernel(
         turns = ctx.enter_context(tc.tile_pool(name="turns", bufs=1))
         ring = ctx.enter_context(tc.tile_pool(name="ring", bufs=1))
         late = ctx.enter_context(tc.tile_pool(name="late", bufs=1))
+        spent = ctx.enter_context(tc.tile_pool(name="spent", bufs=1))
         psum = ctx.enter_context(tc.psum_pool(name="psum", bufs=1))
 
         offs_t = lists.tile([P, S // 16], U16, name="offs_t")
@@ -46,7 +48,7 @@ def tile_picked_lshmean_silu_po_kernel(
             return list_t[:, j0 // 16 : (j0 + n) // 16]
 
         xs_all = reuse.tile([P, T], U8, name="xs_all", align_bytes=64, offset=0)
-        xw_all = keep.tile([P, T], I32, name="xw_all", align_bytes=64)
+        xw_all = spent.tile([P, T], I32, name="xw_all", align_bytes=64, offset=0)
         w2s_raw = keep.tile([P, N], U8, name="w2s_raw", align_bytes=64)
         w2s_dealt = keep.tile([P, N], U8, name="w2s_dealt", align_bytes=64)
         w2s = reuse.tile([P, N], U8, name="w2s", align_bytes=64, offset=0)
@@ -103,8 +105,9 @@ def tile_picked_lshmean_silu_po_kernel(
             nc.sync.dma_start(w2s[r:P:32, :].bitcast(I32), w2s_dealt[16 + r : 32 : 4, :].bitcast(I32))
 
         first, second, third, fourth = 1, 2, 0, 3
-        y = {t: keep.tile([P, S], F32, name=f"y{t}", align_bytes=64) for t in (first, third, fourth)}
-        y[second] = turns.tile([P, S + HALF], F32, name="y_second", align_bytes=64, offset=0)
+        y = {t: keep.tile([P, S], F32, name=f"y{t}", align_bytes=64) for t in (first, third)}
+        y[second] = turns.tile([P, 2 * S], F32, name="y_second", align_bytes=64, offset=0)
+        y[fourth] = spent.tile([P, 2 * S], F32, name="y_fourth", align_bytes=64, offset=0)
 
         def first_product(acc, t, j0, n):
             nc.tensor.matmul_mx(
@@ -119,31 +122,32 @@ def tile_picked_lshmean_silu_po_kernel(
 
         on_scalar, on_vector = nc.scalar.copy, nc.vector.tensor_copy
         quarter = S // 4
-        for k in range(2):
-            product_into_y(on_scalar, first, word_starts[k], WORD_PIECES[k], k)
         both = psum.tile([P, 2, HALF], F32, name="both", offset=2 * BANK_BYTES)
+        product_into_y(on_scalar, first, 0, quarter, 0)
         first_product(both[:, 0, 0:quarter], second, 0, quarter)
+        product_into_y(on_scalar, first, quarter, quarter, 1)
+        first_product(both[:, 0, quarter:HALF], second, quarter, quarter)
         first_product(both[:, 1, 0:quarter], first, HALF, quarter)
+        on_scalar(y[second][:, 0:HALF], both[:, 0, :])
         on_scalar(y[first][:, HALF : HALF + quarter], both[:, 1, 0:quarter])
         for k in (3, 4):
             product_into_y(on_vector, first, word_starts[k], WORD_PIECES[k], k + 1)
-        on_scalar(y[second][:, 0:quarter], both[:, 0, 0:quarter])
         product_into_y(on_scalar, second, S - quarter, quarter, 6)
 
         means = {
             first: keep.tile([P, V], F32, name="means_first", align_bytes=64),
             second: keep.tile([P, V], F32, name="means_second", align_bytes=64),
-            third: keep.tile([P, V], F32, name="means_third", align_bytes=64),
+            third: spent.tile([P, S], F32, name="means_third", align_bytes=64, offset=8 * S),
             fourth: turns.tile([P, V], F32, name="means_fourth", align_bytes=64, offset=8 * S),
         }
         whole = {
-            first: keep.tile([P, S], F32, name="lined_first", align_bytes=64),
+            first: spent.tile([P, S], F32, name="lined_first", align_bytes=64, offset=8 * S),
             second: turns.tile([P, S], F32, name="lined_second", align_bytes=64, offset=8 * S),
             fourth: ring.tile([P, S], F32, name="lined_fourth", align_bytes=64, offset=8 * S),
         }
-        third_late = keep.tile([P, HALF], F32, name="third_late", align_bytes=64)
+        whole = {t: whole[t][:] for t in whole}
+        whole[third] = y[second][:, S : 2 * S]
         lined = {t: [whole[t][:, 0:HALF], whole[t][:, HALF:S]] for t in whole}
-        lined[third] = [y[second][:, S : S + HALF], third_late[:]]
         u = [ring.tile([P, PACK, quarter], F32, name=f"u{q}", align_bytes=64, offset=q % 3 * 4 * S) for q in range(4)]
 
         def u_block(j0, n):
@@ -157,6 +161,9 @@ def tile_picked_lshmean_silu_po_kernel(
         def line_up_on_scalar(t, h):
             nc.scalar.activation(lined[t][h], y[t][:].indirect(entries(order_t, h * HALF, HALF)), ACT.Copy, scale=0.5)
 
+        def line_up_whole(t):
+            nc.scalar.activation(whole[t], y[t][:].indirect(order_t[:]), ACT.Copy, scale=0.5)
+
         def pair_sums(engine, t, values, v0):
             pairs = values.rearrange("p (v e) -> p v e", e=2)
             engine.tensor_tensor(means[t][:, v0 : v0 + pairs.shape[1]], pairs[:, :, 0], pairs[:, :, 1], ALU.add)
@@ -169,39 +176,33 @@ def tile_picked_lshmean_silu_po_kernel(
 
         line_up_on_vector(first, 0)
         line_up_on_scalar(first, 1)
-        pair_sums(nc.gpsimd, first, whole[first][:], 0)
-        product_into_y(on_vector, second, quarter, HALF, 2)
+        pair_sums(nc.gpsimd, first, whole[first], 0)
+        product_into_y(on_vector, second, HALF, quarter, 2)
         product_into_y(on_vector, third, 0, HALF, 3)
         product_into_y(on_scalar, fourth, 0, HALF, 7)
         product_into_y(on_vector, third, HALF, HALF, 6)
-        for h in range(2):
-            line_up_on_scalar(second, h)
-        pair_sums(nc.gpsimd, second, whole[second][:], 0)
+        line_up_whole(second)
+        pair_sums(nc.gpsimd, second, whole[second], 0)
         for j0 in (0, quarter):
             difference(first, j0, quarter)
         product_into_y(on_vector, fourth, HALF, HALF, 3)
         line_up_on_vector(third, 0)
         line_up_on_scalar(third, 1)
-        for h in range(2):
-            line_up_on_scalar(fourth, h)
-        for h in (1, 0):
-            pair_sums(nc.vector, third, lined[third][h], h * V // 2)
+        line_up_whole(fourth)
         difference(second, 0, quarter)
-        difference(third, 0, quarter)
+        pair_sums(nc.vector, third, whole[third], 0)
         difference(second, quarter, quarter)
-        pair_sums(nc.vector, fourth, whole[fourth][:], 0)
-        def fetch(into, t, j0):
-            nc.scalar.activation(into, means[t][:].indirect(entries(bucket_t, j0, quarter)), ACT.Copy)
+        difference(third, 0, quarter)
+        pair_sums(nc.vector, fourth, whole[fourth], 0)
 
-        ahead = [(third, j0) for j0 in (quarter, HALF, S - quarter)]
-        fetched = {key: keep.tile([P, quarter], F32, name=f"fetched{i}", align_bytes=64)[:] for i, key in enumerate(ahead)}
-        for t, j0 in ahead:
-            fetch(fetched[t, j0], t, j0)
+        fetched = keep.tile([P, S - quarter], F32, name="fetched", align_bytes=64)
+        for j0, n in ((quarter, quarter), (HALF, HALF)):
+            nc.scalar.activation(fetched[:, j0 - quarter : j0 - quarter + n], means[third][:].indirect(entries(bucket_t, j0, n)), ACT.Copy)
 
         out_rows = out_0.rearrange("(p t) j -> p t j", t=PACK)
         out_words = out_1[0].rearrange("p c r -> p (c r)").bitcast(I32)
         o_scales = keep.tile([P, S], U8, name="o_scales", align_bytes=64)
-        o_codes = keep.tile([P, S], I32, name="o_codes", align_bytes=64)
+        o_codes = late.tile([P, S], I32, name="o_codes", align_bytes=64, offset=4096)
         last = len(CHUNKS) - 1
         starts = [sum(CHUNKS[:c]) for c in range(len(CHUNKS))]
         z_bf = [keep.tile([P, PACK * n], BF16, name=f"z_bf{c}", align_bytes=64) for c, n in enumerate(CHUNKS[:3])]
@@ -210,12 +211,10 @@ def tile_picked_lshmean_silu_po_kernel(
         z_codes = z_codes + [keep.tile([P, CHUNKS[c]], U32, name=f"z_codes{c}", align_bytes=64) for c in (2, 3, 4)]
         z_scales = [keep.tile([P, n], U8, name=f"z_scales{c}", align_bytes=64) for c, n in enumerate(CHUNKS)]
         z_scales[1] = late.tile([P, CHUNKS[1]], U8, name="z_scales_second", align_bytes=64, offset=4096)
-        o_f32 = [keep.tile([P, PACK, n], F32, name=f"o_f32{c}", align_bytes=64)[:] for c, n in enumerate(CHUNKS[: last - 1])]
-        short = CHUNKS[last]
-        o_short = keep.tile([P, PACK, 2 * short], F32, name="o_short", align_bytes=64)
-        o_f32 = o_f32 + [o_short[:, :, 0:short], o_short[:, :, short : 2 * short]]
+        o_f32 = [keep.tile([P, PACK, n], F32, name=f"o_f32{c}", align_bytes=64)[:] for c, n in enumerate(CHUNKS)]
         o_bf = [ring.tile([P, PACK * CHUNKS[0]], BF16, name="o_bf0", align_bytes=64, offset=8 * S)]
-        o_bf = o_bf + [keep.tile([P, PACK * CHUNKS[c]], BF16, name=f"o_bf{c}", align_bytes=64) for c in range(1, len(CHUNKS))]
+        o_bf = o_bf + [late.tile([P, PACK * CHUNKS[1]], BF16, name="o_bf1", align_bytes=64, offset=2048)]
+        o_bf = o_bf + [keep.tile([P, PACK * CHUNKS[c]], BF16, name=f"o_bf{c}", align_bytes=64) for c in range(2, len(CHUNKS))]
 
         def woven(ap):
             return ap.rearrange("p (g i t) -> p g t i", i=RUN, t=PACK)
@@ -232,33 +231,31 @@ def tile_picked_lshmean_silu_po_kernel(
 
         def second_product(c, t0, copy):
             j0, n = starts[c], CHUNKS[c]
-            res = psum.tile([P, 2, n], F32, name=f"res{c}_{t0}", offset=(2 * c + t0 // 2) % 8 * BANK_BYTES)
-            for t in (t0, t0 + 1):
+            count = BANK_BYTES // (4 * n)
+            res = psum.tile([P, count, n], F32, name=f"res{c}_{t0}", offset=(2 * c + t0 // 2) % 8 * BANK_BYTES)
+            for t in range(t0, t0 + count):
                 nc.tensor.matmul_mx(
                     res[:, t - t0, :], lhsT=w2w[:, 2 * P * t : 2 * P * (t + 1)].bitcast(FP4X4), lhsT_scale=w2s[:, P * t : P * (t + 1)],
                     rhs=z_codes[c][:].bitcast(FP8X4), rhs_scale=z_scales[c][:], start=True, stop=True,
                 )
-            copy(o_f32[c][:, t0 : t0 + 2, :], res[:])
-            if c < last - 1:
-                nc.sync.dma_start(out_rows[:, t0 : t0 + 2, j0 : j0 + n], o_f32[c][:, t0 : t0 + 2, :])
-            elif c == last:
-                nc.sync.dma_start(out_rows[:, t0 : t0 + 2, starts[last - 1] : S], o_short[:, t0 : t0 + 2, :])
+            copy(o_f32[c][:, t0 : t0 + count, :], res[:])
+            nc.sync.dma_start(out_rows[:, t0 : t0 + count, j0 : j0 + n], o_f32[c][:, t0 : t0 + count, :])
 
         def round_out(c):
-            nc.vector.tensor_copy(woven(o_bf[c][:]), planes(o_f32[c]))
+            on_vector(woven(o_bf[c][:]), planes(o_f32[c]))
 
         def hand_on(c):
             cols = slice(starts[c], starts[c] + CHUNKS[c])
             nc.vector.quantize_mx(o_codes[:, cols].bitcast(FP8X4), o_scales[:, cols], o_bf[c][:])
-            if cols.stop % HALF == 0:
-                stored = slice(cols.stop - HALF, cols.stop)
+            if c in WORD_STORES:
+                stored = slice(WORD_STORES[c], cols.stop)
                 nc.sync.dma_start(out_words[:, stored], o_codes[:, stored])
 
         def last_difference(c):
             difference(fourth, starts[c], CHUNKS[c])
 
         def fetched_difference(t, j0):
-            nc.vector.tensor_tensor(u_block(j0, quarter)[:, t, :], fetched[t, j0], y[t][:, j0 : j0 + quarter], ALU.subtract)
+            nc.vector.tensor_tensor(u_block(j0, quarter)[:, t, :], fetched[:, j0 - quarter : j0], y[t][:, j0 : j0 + quarter], ALU.subtract)
 
         last_difference(0)
         silu(0)
@@ -277,25 +274,22 @@ def tile_picked_lshmean_silu_po_kernel(
         fetched_difference(third, S - quarter)
         for t in (first, second):
             difference(t, S - quarter, quarter)
-        last_difference(3)
-        last_difference(4)
+        difference(fourth, S - quarter, quarter)
         quantise_z(2)
         second_product(1, 0, on_scalar)
         second_product(1, 2, on_scalar)
         silu(3)
         silu(4)
         round_out(0)
+        second_product(2, 0, on_scalar)
+        second_product(2, 2, on_vector)
         quantise_z(3)
         round_out(1)
         quantise_z(4)
         hand_on(0)
         hand_on(1)
-        second_product(2, 0, on_scalar)
-        second_product(2, 2, on_vector)
         second_product(3, 0, on_scalar)
-        second_product(3, 2, on_scalar)
         second_product(4, 0, on_scalar)
-        second_product(4, 2, on_scalar)
         round_out(2)
         round_out(3)
         hand_on(2)

@@ -104,7 +104,7 @@ def tile_picked_lshmean_silu_po_kernel(
         for r in range(4):
             nc.sync.dma_start(w2s[r:P:32, :].bitcast(I32), w2s_dealt[16 + r : 32 : 4, :].bitcast(I32))
 
-        first, second, third, fourth = 1, 2, 0, 3
+        first, second, third, fourth = range(PACK)
         y = {t: keep.tile([P, S], F32, name=f"y{t}", align_bytes=64) for t in (first, third)}
         y[second] = turns.tile([P, 2 * S], F32, name="y_second", align_bytes=64, offset=0)
         y[fourth] = spent.tile([P, 2 * S], F32, name="y_fourth", align_bytes=64, offset=0)
@@ -143,12 +143,14 @@ def tile_picked_lshmean_silu_po_kernel(
         whole = {
             first: spent.tile([P, S], F32, name="lined_first", align_bytes=64, offset=8 * S),
             second: turns.tile([P, S], F32, name="lined_second", align_bytes=64, offset=8 * S),
-            fourth: ring.tile([P, S], F32, name="lined_fourth", align_bytes=64, offset=8 * S),
         }
         whole = {t: whole[t][:] for t in whole}
         whole[third] = y[second][:, S : 2 * S]
+        even = ring.tile([P, 2 * S], F32, name="even", align_bytes=64, offset=0)
+        whole[fourth] = even[:, 0:S]
         lined = {t: [whole[t][:, 0:HALF], whole[t][:, HALF:S]] for t in whole}
-        u = [ring.tile([P, PACK, quarter], F32, name=f"u{q}", align_bytes=64, offset=q % 3 * 4 * S) for q in range(4)]
+        odd = [ring.tile([P, PACK, quarter], F32, name=f"u{q}", align_bytes=64, offset=8 * S) for q in (1, 3)]
+        u = [even[:, S : 2 * S].rearrange("p (t j) -> p t j", t=PACK), odd[0][:], even[:, HALF : S + HALF].rearrange("p (t j) -> p t j", t=PACK), odd[1][:]]
 
         def u_block(j0, n):
             return u[j0 // quarter][:, :, j0 % quarter : j0 % quarter + n]
@@ -205,14 +207,17 @@ def tile_picked_lshmean_silu_po_kernel(
         o_codes = late.tile([P, S], I32, name="o_codes", align_bytes=64, offset=4096)
         last = len(CHUNKS) - 1
         starts = [sum(CHUNKS[:c]) for c in range(len(CHUNKS))]
-        z_bf = [keep.tile([P, PACK * n], BF16, name=f"z_bf{c}", align_bytes=64) for c, n in enumerate(CHUNKS[:3])]
-        z_bf = z_bf + [late.tile([P, PACK * CHUNKS[c]], BF16, name=f"z_bf{c}", align_bytes=64, offset=2048 * (c - 2)) for c in (3, 4)]
+        z_bf = [keep.tile([P, PACK * n], BF16, name=f"z_bf{c}", align_bytes=64) for c, n in enumerate(CHUNKS[:2])]
+        z_bf = z_bf + [late.tile([P, PACK * CHUNKS[c]], BF16, name=f"z_bf{c}", align_bytes=64, offset=2048 * (c - 2)) for c in (2, 3, 4)]
         z_codes = [late.tile([P, n], U32, name=f"z_codes{c}", align_bytes=64, offset=2048 * c) for c, n in enumerate(CHUNKS[:2])]
         z_codes = z_codes + [keep.tile([P, CHUNKS[c]], U32, name=f"z_codes{c}", align_bytes=64) for c in (2, 3, 4)]
         z_scales = [keep.tile([P, n], U8, name=f"z_scales{c}", align_bytes=64) for c, n in enumerate(CHUNKS)]
         z_scales[1] = late.tile([P, CHUNKS[1]], U8, name="z_scales_second", align_bytes=64, offset=4096)
-        o_f32 = [keep.tile([P, PACK, n], F32, name=f"o_f32{c}", align_bytes=64)[:] for c, n in enumerate(CHUNKS)]
-        o_bf = [ring.tile([P, PACK * CHUNKS[0]], BF16, name="o_bf0", align_bytes=64, offset=8 * S)]
+        o_f32 = [keep.tile([P, PACK, n], F32, name=f"o_f32{c}", align_bytes=64)[:] for c, n in enumerate(CHUNKS[: last - 1])]
+        short = CHUNKS[last]
+        o_short = keep.tile([P, PACK, 2 * short], F32, name="o_short", align_bytes=64)
+        o_f32 = o_f32 + [o_short[:, :, 0:short], o_short[:, :, short : 2 * short]]
+        o_bf = [ring.tile([P, PACK * CHUNKS[0]], BF16, name="o_bf0", align_bytes=64, offset=0)]
         o_bf = o_bf + [late.tile([P, PACK * CHUNKS[1]], BF16, name="o_bf1", align_bytes=64, offset=2048)]
         o_bf = o_bf + [keep.tile([P, PACK * CHUNKS[c]], BF16, name=f"o_bf{c}", align_bytes=64) for c in range(2, len(CHUNKS))]
 
@@ -231,7 +236,7 @@ def tile_picked_lshmean_silu_po_kernel(
 
         def second_product(c, t0, copy):
             j0, n = starts[c], CHUNKS[c]
-            count = BANK_BYTES // (4 * n)
+            count = 2
             res = psum.tile([P, count, n], F32, name=f"res{c}_{t0}", offset=(2 * c + t0 // 2) % 8 * BANK_BYTES)
             for t in range(t0, t0 + count):
                 nc.tensor.matmul_mx(
@@ -239,7 +244,10 @@ def tile_picked_lshmean_silu_po_kernel(
                     rhs=z_codes[c][:].bitcast(FP8X4), rhs_scale=z_scales[c][:], start=True, stop=True,
                 )
             copy(o_f32[c][:, t0 : t0 + count, :], res[:])
-            nc.sync.dma_start(out_rows[:, t0 : t0 + count, j0 : j0 + n], o_f32[c][:, t0 : t0 + count, :])
+            if c < last - 1:
+                nc.sync.dma_start(out_rows[:, t0 : t0 + count, j0 : j0 + n], o_f32[c][:, t0 : t0 + count, :])
+            elif c == last:
+                nc.sync.dma_start(out_rows[:, t0 : t0 + 2, starts[last - 1] : S], o_short[:, t0 : t0 + 2, :])
 
         def round_out(c):
             on_vector(woven(o_bf[c][:]), planes(o_f32[c]))
@@ -268,28 +276,27 @@ def tile_picked_lshmean_silu_po_kernel(
         fetched_difference(third, HALF)
         last_difference(2)
         quantise_z(1)
-        silu(2)
         second_product(0, 0, on_scalar)
         second_product(0, 2, on_scalar)
+        silu(2)
         fetched_difference(third, S - quarter)
         for t in (first, second):
             difference(t, S - quarter, quarter)
         difference(fourth, S - quarter, quarter)
-        quantise_z(2)
         second_product(1, 0, on_scalar)
-        second_product(1, 2, on_scalar)
+        second_product(1, 2, on_vector)
+        quantise_z(2)
         silu(3)
         silu(4)
         round_out(0)
-        second_product(2, 0, on_scalar)
-        second_product(2, 2, on_vector)
         quantise_z(3)
         round_out(1)
         quantise_z(4)
         hand_on(0)
         hand_on(1)
-        second_product(3, 0, on_scalar)
-        second_product(4, 0, on_scalar)
+        for c in (2, 3, 4):
+            second_product(c, 0, on_scalar)
+            second_product(c, 2, on_scalar)
         round_out(2)
         round_out(3)
         hand_on(2)

@@ -22,7 +22,7 @@ W1_ON_SCALAR = 44
 WORD_PIECES = (256, 256, 256, 128, 128)
 CHUNKS = (256, 256, 256, 128, 128)
 RUN = 2
-WORD_STORES = {1: 0, 2: 512, 4: 768}
+WORD_STORES = {0: 0, 1: 256, 2: 512, 4: 768}
 BANK_BYTES = 2048
 
 
@@ -204,21 +204,21 @@ def tile_picked_lshmean_silu_po_kernel(
         out_rows = out_0.rearrange("(p t) j -> p t j", t=PACK)
         out_words = out_1[0].rearrange("p c r -> p (c r)").bitcast(I32)
         o_scales = keep.tile([P, S], U8, name="o_scales", align_bytes=64)
-        o_codes = late.tile([P, S], I32, name="o_codes", align_bytes=64, offset=4096)
+        o_codes = late.tile([P, S], I32, name="o_codes", align_bytes=64, offset=2560)
         last = len(CHUNKS) - 1
         starts = [sum(CHUNKS[:c]) for c in range(len(CHUNKS))]
         z_bf = [keep.tile([P, PACK * n], BF16, name=f"z_bf{c}", align_bytes=64) for c, n in enumerate(CHUNKS[:2])]
-        z_bf = z_bf + [late.tile([P, PACK * CHUNKS[c]], BF16, name=f"z_bf{c}", align_bytes=64, offset=2048 * (c - 2)) for c in (2, 3, 4)]
+        z_bf = z_bf + [late.tile([P, PACK * CHUNKS[c]], BF16, name=f"z_bf{c}", align_bytes=64, offset=(0, 2048, 8192)[c - 2]) for c in (2, 3, 4)]
         z_codes = [late.tile([P, n], U32, name=f"z_codes{c}", align_bytes=64, offset=2048 * c) for c, n in enumerate(CHUNKS[:2])]
         z_codes = z_codes + [keep.tile([P, CHUNKS[c]], U32, name=f"z_codes{c}", align_bytes=64) for c in (2, 3, 4)]
         z_scales = [keep.tile([P, n], U8, name=f"z_scales{c}", align_bytes=64) for c, n in enumerate(CHUNKS)]
-        z_scales[1] = late.tile([P, CHUNKS[1]], U8, name="z_scales_second", align_bytes=64, offset=4096)
+        z_scales[1] = late.tile([P, CHUNKS[1]], U8, name="z_scales_second", align_bytes=64, offset=8192)
         o_f32 = [keep.tile([P, PACK, n], F32, name=f"o_f32{c}", align_bytes=64)[:] for c, n in enumerate(CHUNKS[: last - 1])]
         short = CHUNKS[last]
         o_short = keep.tile([P, PACK, 2 * short], F32, name="o_short", align_bytes=64)
         o_f32 = o_f32 + [o_short[:, :, 0:short], o_short[:, :, short : 2 * short]]
         o_bf = [ring.tile([P, PACK * CHUNKS[0]], BF16, name="o_bf0", align_bytes=64, offset=0)]
-        o_bf = o_bf + [late.tile([P, PACK * CHUNKS[1]], BF16, name="o_bf1", align_bytes=64, offset=2048)]
+        o_bf = o_bf + [late.tile([P, PACK * CHUNKS[1]], BF16, name="o_bf1", align_bytes=64, offset=512)]
         o_bf = o_bf + [keep.tile([P, PACK * CHUNKS[c]], BF16, name=f"o_bf{c}", align_bytes=64) for c in range(2, len(CHUNKS))]
 
         def woven(ap):
@@ -290,9 +290,9 @@ def tile_picked_lshmean_silu_po_kernel(
         silu(4)
         round_out(0)
         quantise_z(3)
+        hand_on(0)
         round_out(1)
         quantise_z(4)
-        hand_on(0)
         hand_on(1)
         for c in (2, 3, 4):
             second_product(c, 0, on_scalar)

from contextlib import ExitStack

import concourse.mybir as mybir

F32 = mybir.dt.float32
BF16 = mybir.dt.bfloat16
I32 = mybir.dt.int32
U32 = mybir.dt.uint32
U16 = mybir.dt.uint16
U8 = mybir.dt.uint8
FP8X4 = mybir.dt.float8_e4m3fn_x4
FP4X4 = mybir.dt.float4_e2m1fn_x4
ALU = mybir.AluOpType
ACT = mybir.ActivationFunctionType

K, T, S, V, N, H = 512, 2048, 1024, 512, 512, 512
FLOPS = 2 * K * H * S + 2 * H * N * S
P = 128
PACK = 4
HALF = S // 2
W1_ON_SCALAR = 44
WORD_PIECES = (256, 256, 256, 128, 128)
CHUNKS = (256, 256, 256, 128, 128)
RUN = 2
WORD_STORES = {0: 0, 1: 256, 2: 512, 4: 768}
BANK_BYTES = 2048


def tile_picked_lshmean_silu_po_kernel(
    tc, x_words, x_scales, w1, w2_words, w2_scales, offs, order, bucket, out_0, out_1, out_2
):
    nc = tc.nc
    with ExitStack() as ctx:
        lists = ctx.enter_context(tc.tile_pool(name="lists", bufs=1))
        keep = ctx.enter_context(tc.tile_pool(name="keep", bufs=1))
        reuse = ctx.enter_context(tc.tile_pool(name="reuse", bufs=1))
        turns = ctx.enter_context(tc.tile_pool(name="turns", bufs=1))
        ring = ctx.enter_context(tc.tile_pool(name="ring", bufs=1))
        late = ctx.enter_context(tc.tile_pool(name="late", bufs=1))
        spent = ctx.enter_context(tc.tile_pool(name="spent", bufs=1))
        psum = ctx.enter_context(tc.psum_pool(name="psum", bufs=1))

        offs_t = lists.tile([P, S // 16], U16, name="offs_t")
        order_t = lists.tile([P, S // 16], U16, name="order_t")
        bucket_t = lists.tile([P, S // 16], U16, name="bucket_t")

        def entries(list_t, j0, n):
            return list_t[:, j0 // 16 : (j0 + n) // 16]

        xs_all = reuse.tile([P, T], U8, name="xs_all", align_bytes=64, offset=0)
        xw_all = spent.tile([P, T], I32, name="xw_all", align_bytes=64, offset=0)
        w2s_raw = keep.tile([P, N], U8, name="w2s_raw", align_bytes=64)
        w2s_dealt = keep.tile([P, N], U8, name="w2s_dealt", align_bytes=64)
        w2s = reuse.tile([P, N], U8, name="w2s", align_bytes=64, offset=0)
        w2w_raw = keep.tile([P, 2 * N], U8, name="w2w_raw", align_bytes=64)
        w1_raw = turns.tile([P, PACK, H], F32, name="w1_raw", align_bytes=64, offset=0)

        xs = keep.tile([P, S], U8, name="xs", align_bytes=64)
        nc.vector.memset(xs_all[0:16, :].bitcast(I32), 0)
        nc.vector.memset(xs_all[32:64, :].bitcast(I32), 0)
        nc.vector.memset(xs_all[64:P, :].bitcast(I32), 0)
        nc.vector.memset(xs[:].bitcast(I32), 0)
        nc.vector.memset(w2s_raw[0:16, :].bitcast(I32), 0)
        nc.vector.memset(w2s_raw[32:64, :].bitcast(I32), 0)
        nc.vector.memset(w2s_raw[64:P, :].bitcast(I32), 0)

        warm = keep.tile([P, 16], F32, name="warm", align_bytes=64)
        nc.gpsimd.memset(warm[:, 0:1], 0.0)
        nc.scalar.activation(warm[:, 8:9], warm[:, 0:1], ACT.Silu)

        nc.sync.dma_start(offs_t[:], offs)
        nc.sync.dma_start(xs_all[16:32, :].bitcast(I32), x_scales[0].bitcast(I32))
        nc.sync.dma_start(w2s_raw[16:32, :].bitcast(I32), w2_scales[0].bitcast(I32))
        nc.sync.dma_start(w1_raw[:], w1.rearrange("(p j) c -> p j c", j=PACK))
        nc.sync.dma_start(xw_all[:], x_words[0].rearrange("p c r -> p (c r)").bitcast(I32))
        nc.sync.dma_start(w2w_raw[:].bitcast(I32), w2_words[0].bitcast(I32))
        nc.sync.dma_start(order_t[:], order)
        nc.sync.dma_start(bucket_t[:], bucket)

        xs_picked = keep.tile([P, S], U8, name="xs_picked", align_bytes=64)
        nc.vector.tensor_copy(xs_picked[:], xs_all[:].indirect(offs_t[:]))
        for r in range(4):
            nc.sync.dma_start(xs[r:P:32, :].bitcast(I32), xs_picked[16 + r : 32 : 4, :].bitcast(I32))
        nc.gpsimd.tensor_copy(w2s_dealt[:].rearrange("p (t m) -> p t m", t=PACK), w2s_raw[:].rearrange("p (m t) -> p t m", t=PACK))

        w1_src = w1_raw[:].rearrange("p j (m t) -> p m j t", t=PACK)
        w1_bf = keep.tile([P, PACK * H], BF16, name="w1_bf", tag="w1_bf", align_bytes=64)
        w1_dealt = w1_bf[:].rearrange("p (t m j) -> p m j t", t=PACK, j=PACK)
        w1_codes = keep.tile([P, H], U32, name="w1_codes", align_bytes=64)
        w1_scales = keep.tile([P, H], U8, name="w1_scales", align_bytes=64)
        nc.scalar.copy(w1_dealt[:, 0:W1_ON_SCALAR], w1_src[:, 0:W1_ON_SCALAR])
        nc.vector.tensor_copy(w1_dealt[:, W1_ON_SCALAR:P], w1_src[:, W1_ON_SCALAR:P])
        nc.vector.quantize_mx(w1_codes[:].bitcast(FP8X4), w1_scales[:], w1_bf[:])

        xw = keep.tile([P, S], U32, name="xw", tag="w1_bf", align_bytes=64)
        word_starts = [sum(WORD_PIECES[:k]) for k in range(len(WORD_PIECES))]
        for j0, n in zip(word_starts, WORD_PIECES):
            nc.vector.tensor_copy(xw[:, j0 : j0 + n], xw_all[:].bitcast(U32).indirect(entries(offs_t, j0, n)))

        w2w = keep.tile([P, 2 * N], U8, name="w2w", align_bytes=64)
        nc.scalar.copy(w2w[:].bitcast(U16).rearrange("p (t m) -> p t m", t=PACK), w2w_raw[:].bitcast(U16).rearrange("p (m t) -> p t m", t=PACK))

        nc.gpsimd.memset(w2s[:].bitcast(I32), 0)
        for r in range(4):
            nc.sync.dma_start(w2s[r:P:32, :].bitcast(I32), w2s_dealt[16 + r : 32 : 4, :].bitcast(I32))

        first, second, third, fourth = range(PACK)
        y = {t: keep.tile([P, S], F32, name=f"y{t}", align_bytes=64) for t in (first, third)}
        y[second] = turns.tile([P, 2 * S], F32, name="y_second", align_bytes=64, offset=0)
        y[fourth] = spent.tile([P, 2 * S], F32, name="y_fourth", align_bytes=64, offset=0)

        def first_product(acc, t, j0, n):
            nc.tensor.matmul_mx(
                acc, lhsT=w1_codes[:, P * t : P * (t + 1)].bitcast(FP8X4), lhsT_scale=w1_scales[:, P * t : P * (t + 1)],
                rhs=xw[:, j0 : j0 + n].bitcast(FP8X4), rhs_scale=xs[:, j0 : j0 + n], start=True, stop=True,
            )

        def product_into_y(copy, t, j0, n, bank):
            acc = psum.tile([P, n], F32, name=f"acc{t}_{j0}", offset=bank * BANK_BYTES)
            first_product(acc[:], t, j0, n)
            copy(y[t][:, j0 : j0 + n], acc[:])

        on_scalar, on_vector = nc.scalar.copy, nc.vector.tensor_copy
        quarter = S // 4
        both = psum.tile([P, 2, HALF], F32, name="both", offset=2 * BANK_BYTES)
        product_into_y(on_scalar, first, 0, quarter, 0)
        first_product(both[:, 0, 0:quarter], second, 0, quarter)
        product_into_y(on_scalar, first, quarter, quarter, 1)
        first_product(both[:, 0, quarter:HALF], second, quarter, quarter)
        first_product(both[:, 1, 0:quarter], first, HALF, quarter)
        on_scalar(y[second][:, 0:HALF], both[:, 0, :])
        on_scalar(y[first][:, HALF : HALF + quarter], both[:, 1, 0:quarter])
        for k in (3, 4):
            product_into_y(on_vector, first, word_starts[k], WORD_PIECES[k], k + 1)
        product_into_y(on_scalar, second, S - quarter, quarter, 6)

        means = {
            first: keep.tile([P, V], F32, name="means_first", align_bytes=64),
            second: keep.tile([P, V], F32, name="means_second", align_bytes=64),
            third: spent.tile([P, S], F32, name="means_third", align_bytes=64, offset=8 * S),
            fourth: turns.tile([P, V], F32, name="means_fourth", align_bytes=64, offset=8 * S),
        }
        whole = {
            first: spent.tile([P, S], F32, name="lined_first", align_bytes=64, offset=8 * S),
            second: turns.tile([P, S], F32, name="lined_second", align_bytes=64, offset=8 * S),
        }
        whole = {t: whole[t][:] for t in whole}
        whole[third] = y[second][:, S : 2 * S]
        even = ring.tile([P, 2 * S], F32, name="even", align_bytes=64, offset=0)
        whole[fourth] = even[:, 0:S]
        lined = {t: [whole[t][:, 0:HALF], whole[t][:, HALF:S]] for t in whole}
        odd = [ring.tile([P, PACK, quarter], F32, name=f"u{q}", align_bytes=64, offset=8 * S) for q in (1, 3)]
        u = [even[:, S : 2 * S].rearrange("p (t j) -> p t j", t=PACK), odd[0][:], even[:, HALF : S + HALF].rearrange("p (t j) -> p t j", t=PACK), odd[1][:]]

        def u_block(j0, n):
            return u[j0 // quarter][:, :, j0 % quarter : j0 % quarter + n]

        def line_up_on_vector(t, h):
            nc.vector.tensor_scalar(
                lined[t][h], y[t][:].indirect(entries(order_t, h * HALF, HALF)), 0.5, 0.0, ALU.mult, ALU.add
            )

        def line_up_on_scalar(t, h):
            nc.scalar.activation(lined[t][h], y[t][:].indirect(entries(order_t, h * HALF, HALF)), ACT.Copy, scale=0.5)

        def line_up_whole(t):
            nc.scalar.activation(whole[t], y[t][:].indirect(order_t[:]), ACT.Copy, scale=0.5)

        def pair_sums(engine, t, values, v0):
            pairs = values.rearrange("p (v e) -> p v e", e=2)
            engine.tensor_tensor(means[t][:, v0 : v0 + pairs.shape[1]], pairs[:, :, 0], pairs[:, :, 1], ALU.add)

        def difference(t, j0, n):
            nc.vector.tensor_tensor(
                u_block(j0, n)[:, t, :], means[t][:].indirect(entries(bucket_t, j0, n)),
                y[t][:, j0 : j0 + n], ALU.subtract,
            )

        line_up_on_vector(first, 0)
        line_up_on_scalar(first, 1)
        pair_sums(nc.gpsimd, first, whole[first], 0)
        product_into_y(on_vector, second, HALF, quarter, 2)
        product_into_y(on_vector, third, 0, HALF, 3)
        product_into_y(on_scalar, fourth, 0, HALF, 7)
        product_into_y(on_vector, third, HALF, HALF, 6)
        line_up_whole(second)
        pair_sums(nc.gpsimd, second, whole[second], 0)
        for j0 in (0, quarter):
            difference(first, j0, quarter)
        product_into_y(on_vector, fourth, HALF, HALF, 3)
        line_up_on_vector(third, 0)
        line_up_on_scalar(third, 1)
        line_up_whole(fourth)
        difference(second, 0, quarter)
        pair_sums(nc.vector, third, whole[third], 0)
        difference(second, quarter, quarter)
        difference(third, 0, quarter)
        pair_sums(nc.vector, fourth, whole[fourth], 0)

        fetched = keep.tile([P, S - quarter], F32, name="fetched", align_bytes=64)
        for j0, n in ((quarter, quarter), (HALF, HALF)):
            nc.scalar.activation(fetched[:, j0 - quarter : j0 - quarter + n], means[third][:].indirect(entries(bucket_t, j0, n)), ACT.Copy)

        out_rows = out_0.rearrange("(p t) j -> p t j", t=PACK)
        out_words = out_1[0].rearrange("p c r -> p (c r)").bitcast(I32)
        o_scales = keep.tile([P, S], U8, name="o_scales", align_bytes=64)
        o_codes = late.tile([P, S], I32, name="o_codes", align_bytes=64, offset=2560)
        last = len(CHUNKS) - 1
        starts = [sum(CHUNKS[:c]) for c in range(len(CHUNKS))]
        z_bf = [keep.tile([P, PACK * n], BF16, name=f"z_bf{c}", align_bytes=64) for c, n in enumerate(CHUNKS[:2])]
        z_bf = z_bf + [late.tile([P, PACK * CHUNKS[c]], BF16, name=f"z_bf{c}", align_bytes=64, offset=(0, 2048, 8192)[c - 2]) for c in (2, 3, 4)]
        z_codes = [late.tile([P, n], U32, name=f"z_codes{c}", align_bytes=64, offset=2048 * c) for c, n in enumerate(CHUNKS[:2])]
        z_codes = z_codes + [keep.tile([P, CHUNKS[c]], U32, name=f"z_codes{c}", align_bytes=64) for c in (2, 3, 4)]
        z_scales = [keep.tile([P, n], U8, name=f"z_scales{c}", align_bytes=64) for c, n in enumerate(CHUNKS)]
        z_scales[1] = late.tile([P, CHUNKS[1]], U8, name="z_scales_second", align_bytes=64, offset=8192)
        o_f32 = [keep.tile([P, PACK, n], F32, name=f"o_f32{c}", align_bytes=64)[:] for c, n in enumerate(CHUNKS[: last - 1])]
        short = CHUNKS[last]
        o_short = keep.tile([P, PACK, 2 * short], F32, name="o_short", align_bytes=64)
        o_f32 = o_f32 + [o_short[:, :, 0:short], o_short[:, :, short : 2 * short]]
        o_bf = [ring.tile([P, PACK * CHUNKS[0]], BF16, name="o_bf0", align_bytes=64, offset=0)]
        o_bf = o_bf + [late.tile([P, PACK * CHUNKS[1]], BF16, name="o_bf1", align_bytes=64, offset=512)]
        o_bf = o_bf + [keep.tile([P, PACK * CHUNKS[c]], BF16, name=f"o_bf{c}", align_bytes=64) for c in range(2, len(CHUNKS))]

        def woven(ap):
            return ap.rearrange("p (g i t) -> p g t i", i=RUN, t=PACK)

        def planes(ap):
            return ap.rearrange("p t (g i) -> p g t i", i=RUN)

        def silu(c):
            j0, n = starts[c], CHUNKS[c]
            nc.scalar.activation(woven(z_bf[c][:]), planes(u_block(j0, n)), ACT.Silu, scale=-1.0)

        def quantise_z(c):
            nc.vector.quantize_mx(z_codes[c][:].bitcast(FP8X4), z_scales[c][:], z_bf[c][:])

        def second_product(c, t0, copy):
            j0, n = starts[c], CHUNKS[c]
            count = 2
            res = psum.tile([P, count, n], F32, name=f"res{c}_{t0}", offset=(2 * c + t0 // 2) % 8 * BANK_BYTES)
            for t in range(t0, t0 + count):
                nc.tensor.matmul_mx(
                    res[:, t - t0, :], lhsT=w2w[:, 2 * P * t : 2 * P * (t + 1)].bitcast(FP4X4), lhsT_scale=w2s[:, P * t : P * (t + 1)],
                    rhs=z_codes[c][:].bitcast(FP8X4), rhs_scale=z_scales[c][:], start=True, stop=True,
                )
            copy(o_f32[c][:, t0 : t0 + count, :], res[:])
            if c < last - 1:
                nc.sync.dma_start(out_rows[:, t0 : t0 + count, j0 : j0 + n], o_f32[c][:, t0 : t0 + count, :])
            elif c == last:
                nc.sync.dma_start(out_rows[:, t0 : t0 + 2, starts[last - 1] : S], o_short[:, t0 : t0 + 2, :])

        def round_out(c):
            on_vector(woven(o_bf[c][:]), planes(o_f32[c]))

        def hand_on(c):
            cols = slice(starts[c], starts[c] + CHUNKS[c])
            nc.vector.quantize_mx(o_codes[:, cols].bitcast(FP8X4), o_scales[:, cols], o_bf[c][:])
            if c in WORD_STORES:
                stored = slice(WORD_STORES[c], cols.stop)
                nc.sync.dma_start(out_words[:, stored], o_codes[:, stored])

        def last_difference(c):
            difference(fourth, starts[c], CHUNKS[c])

        def fetched_difference(t, j0):
            nc.vector.tensor_tensor(u_block(j0, quarter)[:, t, :], fetched[:, j0 - quarter : j0], y[t][:, j0 : j0 + quarter], ALU.subtract)

        last_difference(0)
        silu(0)
        fetched_difference(third, quarter)
        last_difference(1)
        silu(1)
        for t in (first, second):
            difference(t, HALF, quarter)
        quantise_z(0)
        fetched_difference(third, HALF)
        last_difference(2)
        quantise_z(1)
        second_product(0, 0, on_scalar)
        second_product(0, 2, on_scalar)
        silu(2)
        fetched_difference(third, S - quarter)
        for t in (first, second):
            difference(t, S - quarter, quarter)
        difference(fourth, S - quarter, quarter)
        second_product(1, 0, on_scalar)
        second_product(1, 2, on_vector)
        quantise_z(2)
        silu(3)
        silu(4)
        round_out(0)
        quantise_z(3)
        hand_on(0)
        round_out(1)
        quantise_z(4)
        hand_on(1)
        for c in (2, 3, 4):
            second_product(c, 0, on_scalar)
            second_product(c, 2, on_scalar)
        round_out(2)
        round_out(3)
        hand_on(2)
        round_out(4)
        hand_on(3)
        hand_on(4)
        for r in range(4):
            nc.sync.dma_start(out_2[0, r:16:4, :].bitcast(I32), o_scales[r:P:32, :].bitcast(I32))
